import numpy as np, ml_dtypes
CORES = [36,164,52,180,100,228,116,244]
N = 8
BF = ml_dtypes.bfloat16
def gentries(a):
    return np.ascontiguousarray(a.reshape(8, 16, -1).transpose(0, 2, 1)).reshape(8, -1)
def gtable(e):
    e = np.asarray(e); return np.ascontiguousarray(e.reshape(8, -1, 16).transpose(0, 2, 1)).reshape(128, -1).astype(np.int32)
def f(rng, *shape):
    return (rng.standard_normal(shape, dtype=np.float32) * np.exp2(rng.integers(-2, 3, shape[:-1] + (1,)))).astype(BF)
def wide(rng, *shape):
    v = f(rng, *shape).astype(np.float32); k = shape[:-2] + (1, shape[-1])
    return (v * np.exp2(rng.integers(-6, 7, k)) * (rng.random(k) > 0.0625)).astype(BF)
W, K, S, RO, FI, CAP = 3072, 768, 2, 3, 4, 96
def parts(rng):
    b = rng.random((N, 8, S, W)) < rng.choice(np.array([0.5, 0.6, 0.75]), (N, 8, S, 1)); b[..., 0] = True; b[..., W - 1] = True
    nx = np.zeros((N, 8, S, W), np.int64); cur = np.zeros((N, 8, S, K), np.int64)
    for a in range(N):
        for g in range(8):
            for i in range(S):
                v = np.nonzero(b[a, g, i])[0]
                nx[a, g, i] = rng.choice(v, W); nx[a, g, i, v] = rng.permutation(v); cur[a, g, i] = rng.choice(v, K)
    return b, nx, cur, rng.integers(0, S, (N, 8, K)), rng.integers(0, W, (N, 8, W))
def pack(x, b, nx, cur, typ, fro, w):
    mem = np.add.reduce(b.astype(np.int64) << np.arange(S)[:, None], axis=2)
    return {"x": x.astype(BF).reshape(N, 128, W), "nxt": nx.reshape(N, 8, S * W).astype(np.int32), "mem": mem.astype(np.int32), "fro": fro.astype(np.int32),
            "cur": np.stack([gtable(a.reshape(8, S * K)) for a in cur]), "typ": np.stack([gtable(a) for a in typ]), "w0": w.astype(BF).reshape(N, 128, K)}
def setup_inputs(rng):
    b, nx, cur, typ, fro = parts(rng)
    return pack(f(rng, N, 128, W), b, nx, cur, typ, fro, f(rng, N, 128, K))
def setup_inputs_room(rng):
    b, nx, cur, typ, fro = parts(rng)
    x = np.minimum(f(rng, N, 128, W).astype(np.float32), 24); w = f(rng, N, 128, K).astype(np.float32).reshape(N, 8, 16, K)
    w[:, ::2] = np.abs(w[:, ::2]) + 32; w[:, 1] = np.abs(w[:, 1]) + 32
    at = np.take_along_axis(cur, typ[:, :, None, :], 2)[:, :, 0]
    for q in range(FI): at = np.take_along_axis(nx.reshape(N, 8, S * W), typ * W + at, 2)
    z = np.where(typ == S - 1, 0, typ + 1)
    for a in range(N):
        m, zz, cc, i = at[a, 1], z[a, 1], cur[a, 1], a % S
        o = rng.permutation(np.arange(1, K - 1)); o = o[b[a, 1, zz[o], m[o]] & (m[o] > 0) & (m[o] < W - 2)]
        o = rng.permutation(o[np.unique(m[o], return_index=True)[1]])
        by = [o[zz[o] == j] for j in range(S)]
        cc[zz, np.arange(K)] = m
        for j in range(S): cc[j, by[j][:3]] = (0, W - 2, W - 1)
        u, v, p, q, e1, e2 = by[i][3:9]
        ends = [K - 1, 0] if a % 2 == 0 else [0, K - 1]
        typ[a, 1, ends] = typ[a, 1, [u, v]]; cc[:, ends] = cc[:, [u, v]]
        cc[i, ends[0]] = m[q]; cc[i, p] = m[v]
        r = rng.choice(np.nonzero(~b[a, 1, i, :W - 2])[0]); nx[a, 1, i, r] = nx[a, 1, i, m[e1]]; cc[i, e1] = r; cc[i, e2] = r
        b[a, 1, typ[a, 1, [u, p]], m[[u, p]]] = False
    for a in range(N):
        for g in range(0, 8, 2):
            m = at[a, g]; zz = z[a, g]; e = rng.permutation(np.nonzero(b[a, g, zz, m])[0])
            k = int(rng.choice(np.array([0, 1, CAP - 1, CAP, CAP + 1, len(e)])))
            if a < 2: k = ((CAP, CAP + 1, CAP - 1, 0), (1, CAP, len(e), CAP + 1))[a][g // 2]
            cur[a, g, zz[e], e] = m[e]
            one = e[(zz[e] == 0) & (m[e] != 0)][:1] if k == 1 else e[:0]
            e = np.concatenate([one, e])[:k]; k = len(e)
            c = rng.choice(np.concatenate([rng.permutation(W)[:int(rng.choice(np.array([24, 150, 600, W])))], m[e[:k // 4]]]), k)
            cur[a, g, zz[e], e] = np.where(c == m[e], (c + 1) % W, c)
            cur[a, g, 0, one] = 0
    return pack(x, b, nx, cur, typ, fro, w)
def setup_inputs_ties(rng):
    b, nx, cur, typ, fro = parts(rng)
    x = 4.0 * rng.integers(-3, 4, (N, 8, 16, W)); w = 4.0 * rng.integers(-3, 4, (N, 8, 16, K))
    x[::2, 5] = rng.choice(np.array([7.96875, 8, 8, 8, 8.0625]), (N // 2, 16, W)); x[1::2, 5] = 64
    w[:, 5] = rng.choice(np.array([-1.0, 1.0]), (N, 16, K)) * np.exp2(-1.0 * rng.integers(14, 21, (N, 16, K)))
    return pack(x, b, nx, cur, typ, fro, w)
def setup_inputs_alike(rng):
    b, nx, cur, typ, fro = parts(rng)
    cur[:, 0] = rng.choice(np.array([0, W - 1]), (N, S, K)); nx[:, 1] = rng.choice(np.array([0, 3, W // 2, W - 1]), (N, S, W)); nx[:, 2] = np.arange(W)
    fro[:, 3] = rng.choice(np.array([0, W - 1]), (N, W)); b[:, 4] = True; b[:, 5] = False; typ[:, 6] = 0; cur[:, 7] = np.repeat(cur[:, 7, :1], S, axis=1)
    return pack(f(rng, N, 128, W), b, nx, cur, typ, fro, f(rng, N, 128, K))
def setup_inputs_hot(rng):
    b, nx, cur, typ, fro = parts(rng)
    sh = rng.choice(np.array([-64, 0, 64]), (N, 8, 1, 1)); sh[0, :4, 0, 0] = (-64, 64, -64, 0); sh[1, 4:, 0, 0] = (0, -64, 64, -64)
    b[rng.random((N, 8)) < 0.3] = True; b[0, 0] = True; b[1, 5] = True
    x = f(rng, N, 128, W).reshape(N, 8, 16, W); w = f(rng, N, 128, K).astype(np.float32).reshape(N, 8, 16, K) + sh
    for g in (3, 6):
        b[:, g] = True; w[:, g] = 4
        x[::2, g] = (rng.integers(0, 25, x[::2, g].shape) * 0.125).astype(BF); x[1::2, g] = (rng.integers(-32, -7, x[1::2, g].shape) * 0.125).astype(BF)
    for a in range(0, N, 2):
        o = np.concatenate([CAP // 2 + rng.permutation(CAP // 2)[:CAP // 4], CAP + rng.permutation(K - CAP)[:CAP // 8]])
        w[a, 6][:, o] = 1000
    return pack(x, b, nx, cur, typ, fro, w)
def setup_inputs_spread(rng):
    b, nx, cur, typ, fro = parts(rng)
    return pack(wide(rng, N, 128, W), b, nx, cur, typ, fro, wide(rng, N, 128, K))
def check_inputs(d):
    bad = []
    for k, hi in (("nxt", W - 1), ("mem", 2 ** S - 1), ("fro", W - 1), ("cur", W - 1), ("typ", S - 1)):
        if np.min(d[k]) < 0 or np.max(d[k]) > hi: bad.append("range of " + k)
    for k in ("x", "w0"):
        if not np.all(np.abs(d[k].astype(np.float32)) < 2.0 ** 60): bad.append("size of " + k)
    return bad
def reference(x, nxt, mem, fro, cur, typ, w0):
    pick = np.take_along_axis
    X = x.astype(np.float32).reshape(N, 8, 16, W); w = w0.astype(np.float32).reshape(N, 8, 16, K)
    nx = nxt.astype(np.int64); mb = mem.astype(np.int64); fo = fro.astype(np.int64)
    c = np.stack([gentries(a) for a in cur]).astype(np.int64).reshape(N, 8, S, K); s = np.stack([gentries(a) for a in typ]).astype(np.int64)
    for t in range(RO):
        for q in range(FI):
            at = pick(c, s[:, :, None, :], 2)[:, :, 0]
            m = pick(nx, s * W + at, 2)
            hit = np.add.reduce((pick(X, m[:, :, None, :], 3) >= w).astype(np.int64), axis=2) >= 9
            bits = pick(mb, m, 2)
            for i in range(S): c[:, :, i] = np.where((s == i) | (hit & (((bits >> i) & 1) == 1)), m, c[:, :, i])
            s = np.where(hit, np.where(s == S - 1, 0, s + 1), s)
        z = np.where(s == S - 1, 0, s + 1)
        m = pick(c, s[:, :, None, :], 2)[:, :, 0]; e = pick(c, z[:, :, None, :], 2)[:, :, 0]
        want = (((pick(mb, m, 2) >> z) & 1) == 1) & (m != e)
        slot = want & (np.add.accumulate(want.astype(np.int64), axis=2) <= CAP)
        for a in range(N):
            for g in range(8):
                j = np.nonzero(slot[a, g])[0]
                p1 = z[a, g, j] * W + m[a, g, j]; p2 = z[a, g, j] * W + e[a, g, j]
                named = np.bincount(np.concatenate([p1, p2]), minlength=S * W)
                ok = (named[p1] == 1) & (named[p2] == 1); p1 = p1[ok]; p2 = p2[ok]
                v1 = nx[a, g, p1]; v2 = nx[a, g, p2]
                nx[a, g, p1] = v2; nx[a, g, p2] = v1
        k = pick(fo, m, 2)
        y = np.stack([pick(X[(a + 1 + t) % N], k[a][:, None, :], 2) for a in range(N)])
        w = w + np.minimum(np.maximum(y - w, np.float32(-8)), np.float32(8))
    return {"yc": np.stack([gtable(a.reshape(8, S * K)) for a in c]).astype(np.float32), "yw": w.reshape(N, 128, K).astype(np.float32), "yn": nx.astype(np.float32)}

@@ -1,0 +1,465 @@
+from concourse.mybir import AluOpType as A, ActivationFunctionType as F, AxisListType
+
+W, K, PL, DUM = 3072, 768, 6144, 6336
+F4, B2, I4, U2 = "float32", "bfloat16", "int32", "uint16"
+SCRATCH = {}
+for names, shape, dtype in (
+        ("XS XF0 XF1 XF2", [W], B2), ("XN NX", [DUM], B2), ("INFO Z", [PL], B2), ("N32", [DUM], F4), ("WW DD", [K], F4),
+        ("nb_", [24, 16], I4), ("nbf", [24, 16], F4), ("ld2 lt2", [24, 2, 16], F4), ("fr", [384], F4), ("LX", [384], U2),
+        ("memc froc", [192], I4), ("curc", [96], I4), ("typc", [48], I4), ("cl yco", [96], F4), ("cd cx cp cq", [48], F4), ("ti", [4, 192], I4),
+        ("T0 T1 TL M0 M1 M01 MT1 MT0 ML1 ML0 NM0 NM1 FH FL", [192], B2), ("ZR", [384], B2),
+        ("pc", [8], I4), ("pf", [8], F4), ("kr kg BL", [128], F4), ("tb", [192], F4), ("mk nbj nb1", [64], F4), ("dm0 dumL", [12], F4),
+        ("pi co", [16], F4), ("hm", [2], F4), ("CN", [24], B2), ("CK", [8], B2), ("CP G8", [16], B2), ("CB1 CB2", [128], B2), ("Mk", [4], F4),
+        ("DL", [24], F4), ("S96 I96 O96 DUMC", [96], B2), ("I6", [6], F4),
+        ("PO", [2, 2, 8, 4], F4), ("PI", [2, 2, 8, 4], I4), ("LP LO LD LK", [48], U2), ("ge nr RA RB", [K], B2),
+        ("t1", [2, 8, 4], F4), ("dd hd", [2, 16, 4], F4), ("TP TO TK", [2, 8, 4, 4], F4),
+        ("fl df d2 ne de", [2, 8, 4], F4), ("wt cs", [64], B2), ("rk wd", [64], F4), ("CC", [1536], B2),
+        ("RU", [192], U2), ("L6", [256], F4), ("Lf tk Lq", [12], F4), ("tot nk", [6], F4), ("eq", [2304], B2), ("jk", [1536], B2),
+        ("gx gn", [192], B2), ("g32", [192], F4), ("LE", [18], U2)):
+    for nm in names.split():
+        SCRATCH[nm] = ("sbuf", [128] + shape, dtype)
+PSUMS = ("N0", "N1", "C0", "C1", "XB", "L0", "L1", "XA")
+for nm in PSUMS:
+    SCRATCH[nm] = ("psum", [128, 512] if nm in ("L0", "L1", "XA") else [128, 128, 4], F4)
+SEMAPHORES = ["qv", "qp", "qs", "qg", "xl", "xa0", "xa1", "xa2"] + ["e%d" % k for k in range(12)] + ["d%d" % k for k in range(60)]
+AZ = "abcdefghijklmnopqrstuvwxyz"
+SEQ, NV = "st C PO' pd' ls' t1 dO dP hh LP' hd".split(), 2
+
+
+def rank_program(g, core, T, topo):
+    rank = T.rank_of(core)
+    if rank is None:
+        return
+    eng = {"v": g.vector, "p": g.tensor, "s": g.scalar, "g": g, "y": g.sync}
+    total, snap, last, reads, nd = {}, {}, {}, {}, {"d": 0, "e": 0}
+    know = {q: {} for q in eng}
+
+    def a(name, *idx, k=""):
+        t = T[name]
+        return (t[idx] if idx else t[:], [name + c for c in k] if k else [name])
+
+    def ind(win, off):
+        return (win[0].indirect(off[0]), win[1] + off[1])
+
+    def need(q, sem, val):
+        kn = know[q]
+        if kn.get(sem, 0) >= val:
+            return
+        eng[q].wait_ge(T.sem[sem], val)
+        for s2, v2 in snap.get((sem, val), {}).items():
+            kn[s2] = max(kn.get(s2, 0), v2)
+        kn[sem] = max(kn.get(sem, 0), val)
+
+    def deps(q, rd, wr, acc=False):
+        for key in rd + wr:
+            w = last.get(key)
+            if w is not None and not (acc and w[2] == q and key in wr):
+                need(q, w[0], w[1])
+            if key in PSUMS or key in wr:
+                for s2, (v2, q2) in list(reads.get(key, {}).items()):
+                    if q2 != q or s2[0] in "de":
+                        need(q, s2, v2)
+
+    def done(q, sem, val, rd, wr):
+        m = dict(know[q])
+        m[sem] = val
+        snap[(sem, val)] = m
+        for key in wr:
+            last[key] = (sem, val, q)
+            reads[key] = {}
+        for key in rd:
+            if key not in wr:
+                reads.setdefault(key, {})[sem] = (val, q)
+
+    def run(q, fn, outs, ins, acc=False):
+        rd = [x for i in ins for x in i[1]]
+        wr = [x for o in outs for x in o[1]]
+        deps(q, rd, wr, acc)
+        sem = "q" + q
+        total[sem] = total.get(sem, 0) + 1
+        fn().then_inc(T.sem[sem], 1)
+        done(q, sem, total[sem], rd, wr)
+
+    def dma(q, out, in_, **kw):
+        deps(q, in_[1], out[1])
+        c = "e" if q == "g" else "d"
+        sem = "%s%d" % (c, nd[c])
+        nd[c] += 1
+        total[sem] = 16
+        eng[q].dma_start(out[0], in_[0], **kw).then_inc(T.sem[sem], 16)
+        done(q, sem, 16, in_[1], out[1])
+
+    def tt(out, i0, i1, op):
+        run("v", lambda: g.vector.tensor_tensor(out[0], i0[0], i1[0], op), [out], [i0, i1])
+
+    def ts(out, i0, s1, op0, s2=None, op1=None):
+        ins = [i0] + [s for s in (s1, s2) if isinstance(s, tuple)]
+        x1 = s1[0] if isinstance(s1, tuple) else s1
+        x2 = s2[0] if isinstance(s2, tuple) else s2
+        more = [x2, op0] if op1 is None else [x2, op0, op1]
+        run("v", lambda: g.vector.tensor_scalar(out[0], i0[0], x1, *more), [out], ins)
+
+    def cp(out, i0):
+        run("v", lambda: g.vector.tensor_copy(out[0], i0[0]), [out], [i0])
+
+    def fill(out, v):
+        run("v", lambda: g.vector.memset(out[0], v), [out], [])
+
+    def act(out, i0, scale=None, bias=None, acc=None):
+        kw, ins, outs = {}, [i0], [out]
+        for nm, x in (("scale", scale), ("bias", bias)):
+            if isinstance(x, tuple):
+                ins.append(x)
+                kw[nm] = x[0]
+            elif x is not None:
+                kw[nm] = x
+        if acc is not None:
+            outs.append(acc)
+            kw["accum_out"] = acc[0]
+        fn = F.Identity if isinstance(bias, tuple) else F.Copy
+        run("s", lambda: g.scalar.activation(out[0], i0[0], fn, **kw), outs, ins)
+
+    def mm(out, lhsT, rhs, start=True, stop=True):
+        run("p", lambda: g.tensor.matmul(out[0], lhsT[0], rhs[0], start, stop), [out], [lhsT, rhs], acc=True)
+
+    def iota(out, pattern, base, cm, **kw):
+        run("g", lambda: g.iota(out[0], pattern, base, cm, **kw), [out], [])
+
+    ext = lambda ap: (ap, [])
+    al, R = slice(None), slice(0, 96)
+    cols = lambda nm, lo, hi, k="": a(nm, al, slice(lo, hi), k=k)
+    col = lambda nm, j: a(nm, al, slice(j, j + 1), k=AZ[j])
+    half = lambda nm, b: cols(nm, 384 * b, 384 * b + 384, k=str(b))
+    l24 = lambda nm, b: cols(nm, 24 * b, 24 * b + 24, k=str(b))
+
+    dma("s", a("nb_"), ext(T.nxt[:]))
+    dma("y", a("memc"), ext(T.mem[:]))
+    dma("s", a("curc"), ext(T.cur[:]))
+    dma("y", a("froc"), ext(T.fro[:]))
+    dma("s", a("typc"), ext(T.typ[:]))
+    dma("y", a("XS"), ext(T.x[:]))
+
+    fl_ = {"allow_small_or_imprecise_dtypes": True}
+    iota(col("pc", 0), [[0, 1]], 0, 1)
+    iota(a("tb"), [[64, 3], [0, 64]], 0, 0, **fl_)
+    iota(a("TL"), [[0, 3], [1, 64]], 0, 0, **fl_)
+    iota(a("kr"), [[1, 128]], 0, 0, **fl_)
+    dma("g", a("WW", k="01"), ext(T.w0[:]))
+    iota(a("kg"), [[1, 8], [0, 16]], 0, 0, **fl_)
+    iota(a("mk"), [[0, 16], [1, 4]], 0, 0, **fl_)
+    iota(a("nbj"), [[384, 2], [0, 8], [1, 4]], 768, 4, **fl_)
+    iota(a("nb1"), [[384, 2], [0, 8], [1, 4]], 769, 4, **fl_)
+    iota(a("dm0"), [[96, 2], [16, 6]], 6144, 0, **fl_)
+    for j, op in ((1, (15, A.bitwise_and)),
+                  (2, (4, A.arith_shift_right)),
+                  (3, (3, A.bitwise_and)), (4, (2, A.arith_shift_right)),
+                  (5, (4, A.arith_shift_right, 1, A.bitwise_and))):
+        ts(col("pc", j), col("pc", 0), *op)
+    cp(cols("pf", 0, 6, k=AZ[:6]), cols("pc", 0, 6, k=AZ[:6]))
+    p0, pm, gi = col("pf", 0), col("pf", 1), col("pf", 2)
+    ts(col("pf", 6), pm, 192.0, A.mult)
+    ts(col("hm", 0), col("pf", 5), -1.0, A.mult, 1.0, A.add)
+    ts(a("T0"), a("tb"), col("pf", 6), A.add)
+    ts(a("T1"), a("T0"), 3072.0, A.add)
+    act(cols("L0", 0, 192), a("T0"))
+    act(cols("L0", 192, 384), a("T1"))
+    act(cols("L1", 0, 192), a("TL"))
+    fill(a("ZR"), 0.0)
+    ts(a("pi", k=AZ[:16]), cols("kr", 0, 16), pm, A.is_equal)
+    ts(cols("G8", 0, 8, k="0"), cols("kr", 0, 8), gi, A.is_equal)
+    co, pi = (lambda j: col("co", j)), (lambda j: col("pi", j))
+    g8 = cols("G8", 0, 8, k="0")
+    act(co(7), pi(4), scale=0.25)
+    act(co(1), pi(0), bias=pi(1))
+    act(co(0), co(1), bias=co(7))
+    act(co(10), pi(2), bias=pi(3))
+    act(co(11), co(10), bias=pi(5))
+    act(co(12), co(0), scale=-1.0)
+    act(co(2), co(11), bias=co(12))
+    act(cols("CN", 0, 8, k="0"), g8, scale=co(0))
+    act(cols("CN", 8, 16, k="1"), g8, scale=pi(6))
+    act(cols("CN", 16, 24, k="2"), g8, scale=co(2))
+    act(cols("G8", 8, 16, k="1"), g8)
+    ts(a("Mk"), cols("kr", 0, 4), col("pf", 3), A.is_equal)
+    ts(a("DL"), cols("kr", 0, 24), col("pf", 4), A.is_equal)
+
+    ti = lambda j: a("ti", al, j, al, k=str(j))
+    ts(ti(0), a("memc"), 1, A.bitwise_and)
+    ts(ti(1), a("memc"), 1, A.arith_shift_right)
+    cp(a("M0"), ti(0))
+    cp(a("M1"), ti(1))
+    cp(a("nbf"), a("nb_"))
+    tt(a("MT1"), a("M1"), cols("L0", 192, 384), A.mult)
+    tt(a("MT0"), a("M0"), cols("L0", 0, 192), A.mult)
+    tt(a("ML1"), a("M1"), cols("L1", 0, 192), A.mult)
+    tt(a("ML0"), a("M0"), cols("L1", 0, 192), A.mult)
+    act(a("ld2", al, al, 0, al, k="0"), a("nbf"), scale=col("hm", 0))
+    act(a("ld2", al, al, 1, al, k="1"), a("nbf"), scale=col("pf", 5))
+    act(a("NM0"), a("M0"), scale=-1.0, bias=1.0)
+    act(a("NM1"), a("M1"), scale=-1.0, bias=1.0)
+    act(cols("L1", 192, 384), a("M1"), scale=0.25)
+    lo_, hi_ = cols("cl", 0, 48, k="0"), cols("cl", 48, 96, k="1")
+    cp(lo_, cols("curc", 0, 48))
+    ts(hi_, cols("curc", 48, 96), 3072.0, A.add)
+    ts(ti(2), a("froc"), 6, A.arith_shift_right)
+    tt(a("cd"), hi_, lo_, A.subtract)
+    ts(ti(3), a("froc"), 63, A.bitwise_and)
+    tt(a("cx"), a("cd"), a("typc"), A.mult)
+    ts(a("FH"), ti(2), 64.0, A.mult)
+    tt(a("cp"), lo_, a("cx"), A.add)
+    tt(a("cq"), hi_, a("cx"), A.subtract)
+    cp(a("FL"), ti(3))
+    cp(a("LP", k="01"), a("cp"))
+    cp(a("LO", k="01"), a("cq"))
+    tt(a("M01"), a("M0"), cols("L1", 192, 384), A.mult)
+    for n in range(6):
+        dma("y", (T.INFO[10 + n:128:16, :], ["INFO" + AZ[20 + n]]), a("ZR"))
+    for r, lo, hi in ((0, "T0", "T1"), (1, "TL", "TL"), (7, "T1", "T0"), (4, "M1", "M0"), (2, "MT1", "MT0"), (3, "ML1", "ML0"), (6, "NM1", "NM0"),
+                      (8, "FH", "FH"), (9, "FL", "FL"), (5, "M01", "M01")):
+        for h, nm in enumerate((lo, hi)):
+            dma("sy"[h], (T.INFO[r:128:16, W * h:W * h + W], ["INFO" + AZ[2 * r + h]]), a(nm))
+    info = lambda lo, hi: cols("INFO", lo, hi, k=AZ)
+
+    run("v", lambda: g.vector.transpose(T.lt2[:], T.ld2[:]), [a("lt2")], [a("ld2", k="01")])
+    lx = lambda h: cols("LX", 192 * h, 192 * h + 192, k=str(h))
+    for h in range(2):
+        for ch in range(8 * h, 8 * h + 8):
+            tt(cols("fr", 24 * ch, 24 * ch + 24, k=AZ[ch]), a("lt2", al, al, 0, ch), a("lt2", al, al, 1, ch), A.add)
+        cp(lx(h), cols("fr", 192 * h, 192 * h + 192, k=AZ[8 * h:8 * h + 8]))
+    fill(cols("NX", PL, DUM, k="2"), 0.0)
+    fill(cols("XN", PL, DUM, k="2"), 0.0)
+    for h in range(2):
+        cp(cols("XN", W * h, W * h + W, k=str(h)), ind(a("XS"), lx(h)))
+        act(cols("NX", W * h, W * h + W, k=str(h)), ind(info(W * h, W * h + W), lx(h)))
+        if h == 0:
+            cp(half("RB", 0), ind(info(0, PL), l24("LO", 0)))
+            act(half("RB", 1), ind(info(0, PL), l24("LO", 1)))
+    XN, NX = a("XN", k="012"), a("NX", k="012")
+
+    def sendx(t):
+        deps("g", ["XS"], [])
+        if t:
+            need("g", "xl", total["xl"])
+        dst = T.cores[(rank - 1 - t) % 8]
+        rid, pid = topo.addr(dst, core)
+        n = len(topo.engines(core, dst))
+        sem = "xa%d" % t
+        total["xl"] = total.get("xl", 0) + n
+        total[sem] = n
+        g.remote_dma(T["XF%d" % t][:], T.XS[:], T.sem[sem], T.sem.xl, pid, rid, topo.mask(core, dst))
+        last["XF%d" % t] = (sem, n, "-")
+    sendx(0)
+    iota(a("Z"), [[0, PL]], 0, 0, **fl_)
+    iota(a("N32"), [[0, DUM]], 0, 0, **fl_)
+    for k, (r, h, nm) in enumerate(((10, 0, "T0"), (10, 1, "T1"), (11, 0, "TL"), (11, 1, "TL"))):
+        deps("y", [], ["Z"])
+        dma("y", (T.Z[r:128:16, W * h:W * h + W], ["Z" + AZ[k]]), a(nm))
+    zz = (T.Z[:], ["Z", "Za", "Zb", "Zc", "Zd"])
+
+    def tform(bank, c0, n, rowbuf, b, rhs):
+        for i1 in range(4):
+            mm(a(bank, R, slice(c0, c0 + n), i1), a(rowbuf, al, slice(384 * b + i1, 384 * b + 384, 4), k=str(b)), rhs)
+
+    def pads(tp, b, src, nv, between=()):
+        for i0 in range(4):
+            if i0 in (1, 3) and between:
+                between[i0 // 2]()
+            out, m = a(tp, R, b, al, i0, al, k=str(4 * b + i0)), a("Mk", R, slice(i0, i0 + 1))
+            if i0 < nv:
+                ts(out, src, m, A.mult)
+            else:
+                act(out, src, scale=m)
+
+    def tolist(bank, c0, tp, b):
+        mm(cols(bank, c0, c0 + 24), (T[tp][0:96, b], [tp + str(4 * b + i) for i in range(4)]), a("DL", R))
+
+    ot = lambda b: (T.PO[0:96, b, 0], ["PO%d" % b])
+    pt = lambda b: (T.PO[0:96, b, 1], ["PO%d" % b])
+    for b in range(2):
+        tform("XB", 8 * b, 8, "RB", b, cols("CN", 0, 8, k="0"))
+        cp(ot(b), a("XB", R, slice(8 * b, 8 * b + 8), al))
+
+    def start(b):
+        off, gew, ww = l24("LP", b), half("ge", b), half("WW", b)
+        tt(gew, ind(XN, off), ww, A.is_ge)
+        act(a("N%d" % b, R, slice(0, 8), al), ot(b))
+        c, k2 = 384 * b, (str(b), "xy"[b])
+        act(cols("nr", c, c + 256, k=k2[0]), ind(NX, cols("LP", 24 * b, 24 * b + 16, k=str(b))))
+        act(cols("nr", c + 256, c + 384, k=k2[1]), ind(NX, cols("LP", 24 * b + 16, 24 * b + 24, k=str(b))))
+        for lo, hi, kk in ((0, 64, k2[0]), (64, 96, k2[1])):
+            for i1 in range(4):
+                mm(a("N%d" % b, slice(lo, hi), slice(8, 32), i1), a("nr", al, slice(c + 4 * lo + i1, c + 4 * hi, 4), k=kk), a("CN", k="012"))
+
+    def find_ops(b, nv):
+        C, N, k = "C%d" % b, "N%d" % b, str(b)
+        t1, hh, hd = a("t1", R, b, k=k), a(C, R, slice(32, 48), al), a("hd", R, b, k=k)
+        dO, dP, dd = (T.dd[0:96, b, 0:8, :], ["ddO" + k]), (T.dd[0:96, b, 8:16, :], ["ddP" + k]), (T.dd[0:96, b], ["ddO" + k, "ddP" + k])
+        po = (T.PO[0:96, b], ["PO" + k])
+        return {"st": lambda: start(b), "C": lambda: tform(C, 0, 16, "ge", b, a("G8", k="01")),
+                "t1": lambda: tt(t1, a(N, R, slice(16, 24), al), ot(b), A.mult),
+                "dO": lambda: tt(dO, a(N, R, slice(8, 16), al), ot(b), A.subtract),
+                "dP": lambda: tt(dP, a(N, R, slice(24, 32), al), t1, A.add),
+                "hh": lambda: ts(hh, a(C, R, slice(0, 16), al), 8.5, A.is_ge),
+                "hd": lambda: tt(hd, hh, dd, A.mult),
+                "PO": lambda: tt(po, a(N, R, slice(0, 16), al), hd, A.add),
+                "pd": lambda: pads("TP", b, pt(b), nv),
+                "ls": lambda: tolist("L%d" % b, 0, "TP", b),
+                "LP": lambda: cp(l24("LP", b), cols("L%d" % b, 0, 24))}
+
+    def wants(b):
+        k = str(b)
+        PO, PI = (lambda j: (T.PO[0:96, b, j], ["PO" + k])), (lambda j: (T.PI[0:96, b, j], ["PI" + k]))
+        f = lambda nm: a(nm, R, b, k=k)
+        return [lambda: cp((T.PI[0:96, b], ["PI" + k]), (T.PO[0:96, b], ["PO" + k])),
+                lambda: tt(f("fl"), PO(1), PI(1), A.subtract),
+                lambda: tt(f("df"), PI(0), PI(1), A.subtract),
+                lambda: tt(f("d2"), f("df"), f("df"), A.mult),
+                lambda: ts(f("ne"), f("d2"), 9437184.0, A.not_equal, 4.0, A.mult),
+                lambda: tt(a("wt", R, slice(32 * b, 32 * b + 32), k=k), f("fl"), f("ne"), A.mult)]
+
+    def late_constants():
+        for j, i, k in ((3, 8, 9), (4, 7, 1), (5, 10, 11), (6, 1, 11)):
+            act(co(j), pi(i), bias=pi(k))
+        act(co(8), pi(7), scale=6144.0)
+        act(co(9), pi(10), scale=6240.0)
+        act(co(13), co(8), bias=co(9))
+        act(a("CK"), g8, scale=co(3))
+        act(cols("CP", 0, 8, k="0"), g8, scale=co(4))
+        act(cols("CP", 8, 16, k="1"), g8, scale=co(5))
+        ts(a("BL"), a("kg"), gi, A.is_equal)
+        act(a("CB1"), a("BL"), scale=co(4))
+        act(a("CB2"), a("BL"), scale=co(5))
+        ts(a("mk"), a("mk"), 0.5, A.is_ge)
+        ts(a("I96"), cols("kr", 0, 96), p0, A.is_equal)
+        ts(a("S96"), cols("kr", 0, 96), p0, A.is_gt)
+        fill(a("O96"), 1.0)
+        ts(a("I6"), cols("kr", 0, 6), p0, A.is_equal)
+        ts(a("DUMC"), cols("kr", 0, 96), co(6), A.mult, co(13), A.add)
+        ts(a("dumL"), a("dm0"), pm, A.add)
+
+    for t in range(3):
+        for q in range(4):
+            for b in range(2):
+                cur_, prv_ = find_ops(b, NV), find_ops(1 - b, NV)
+                for x in SEQ:
+                    if x[-1] != "'":
+                        cur_[x]()
+                    elif q + b > 0:
+                        prv_[x[:-1]]()
+            if t == 0 and q == 0:
+                late_constants()
+        fin = find_ops(1, NV)
+        for x in SEQ:
+            if x in ("hh'", "hd'", "PO'"):
+                fin[x[:-1]]()
+        pads("TO", 0, ot(0), 0)
+        tolist("L0", 64, "TO", 0)
+        w0, w1 = wants(0), wants(1)
+        w0[0]()
+        w1[0]()
+        w0[1]()
+        pads("TP", 1, pt(1), 4, w1[1:3])
+        tolist("L1", 0, "TP", 1)
+        act(half("RA", 0), ind(info(0, PL), l24("LP", 0)))
+        pads("TO", 1, ot(1), 0)
+        tolist("L0", 88, "TO", 1)
+        w0[2]()
+        w1[3]()
+        w0[3]()
+        cp(l24("LO", 0), cols("L0", 64, 88))
+        w0[4]()
+        w1[4]()
+        cp(cols("CC", 0, 96), a("DUMC"))
+        w1[5]()
+        w0[5]()
+        fin["LP"]()
+        act(half("RA", 1), ind(info(0, PL), l24("LP", 1)))
+        run("v", lambda: g.vector.tensor_tensor_scan(T.cs[0:96, :], T.mk[0:96, :], T.wt[0:96, :], 0.0, A.mult, A.add), [a("cs")], [a("mk"), a("wt", k="01")])
+        cp(l24("LO", 1), cols("L0", 88, 112))
+        for b in range(2):
+            act(half("RB", b), ind(zz, l24("LO", b)))
+        mm(a("XA", R, slice(0, 64)), a("I96", R), a("cs", R), True, False)
+        for i1 in range(4):
+            mm(a("XA", R, slice(i1, 64, 4)), a("S96", R), a("cs", R, slice(3, 64, 4)), False, False)
+            mm(a("XA", R, slice(32 + i1, 64, 4)), a("O96", R), a("cs", R, slice(3, 32, 4)), False, i1 == 3)
+        h32 = lambda nm, b, k: (T[nm][0:96, 32 * b:32 * b + 32], [nm + k])
+        for b in range(2):
+            tt(h32("rk", b, str(b)), h32("XA", b, ""), h32("nb1", b, ""), A.subtract)
+        for b in range(2):
+            tt(h32("wd", b, str(b)), h32("wt", b, str(b)), h32("rk", b, str(b)), A.mult)
+        for b in range(2):
+            tt(a("de", R, b, k=str(b)), h32("wd", b, str(b)), h32("nbj", b, ""), A.add)
+        for b in range(2):
+            pads("TP", b, a("de", R, b, k=str(b)), 4)
+            tolist("L1", 24 * b, "TP", b)
+        cp(a("LD"), cols("L1", 0, 48))
+        tt((T.CC[:].indirect(T.LD[:]), ["CC"]), a("RA", k="01"), (T.RB[:], ["RB0", "RB1", "LD"]), A.add)
+        for b in range(2):
+            tform("XB", 8 * b, 8, "RA", b, a("CK"))
+        for b in range(2):
+            pads("TK", b, a("XB", R, slice(8 * b, 8 * b + 8), al), 0)
+            tolist("L0", 24 * b, "TK", b)
+        for i in range(16):
+            mm(a("L1", slice(0, 6), slice(i, 256, 16)), a("CC", al, slice(i, 96, 16)), a("CP", k="01"))
+        mm(cols("XA", 128, 224), a("CB1"), cols("CC", 0, 96))
+        mm(cols("XA", 224, 320), a("CB2"), cols("CC", 0, 96))
+        act(a("L6", slice(0, 6)), a("L1", slice(0, 6), slice(0, 256)))
+        for k in range(2):
+            mm(cols("L1", 256 + 6 * k, 262 + 6 * k), a("L6", slice(0, 6), slice(128 * k, 128 * k + 128)), a("I6", slice(0, 6)))
+        cp(a("LK"), cols("L0", 0, 48))
+
+        def pull(b):
+            tt(half("DD", b), ind(a("XF%d" % t), cols("LK", 24 * b, 24 * b + 24)), half("WW", b), A.subtract)
+
+        def addw(b):
+            ts(half("DD", b), half("DD", b), 8.0, A.min, -8.0, A.max)
+            dma("g", half("WW", b), half("DD", b), accum_op=A.add)
+        if t < 2:
+            sendx(t + 1)
+        pull(0)
+        addw(0)
+        cp(a("RU"), cols("XA", 128, 320))
+        pull(1)
+        cp(a("Lf"), cols("L1", 256, 268))
+        for k in range(6):
+            for w in range(2):
+                ts(cols("eq", 384 * k + 192 * w, 384 * k + 192 * w + 192, k=AZ[2 * k + w]), a("RU"), (T.Lf[:, 6 * w + k:6 * w + k + 1], ["Lf"]), A.is_equal)
+            if k < 4:
+                act(cols("jk", 384 * k, 384 * k + 384, k=AZ[k]), cols("eq", 384 * k, 384 * k + 384, k=AZ[2 * k:2 * k + 2]), acc=col("tot", k))
+        addw(1)
+        for k in range(4, 6):
+            run("v", lambda k=k: g.vector.tensor_reduce(T.tot[:, k:k + 1], T.eq[:, 384 * k:384 * k + 384], AxisListType.X, A.add),
+                [col("tot", k)], [cols("eq", 0, 1, k=AZ[2 * k:2 * k + 2])])
+        ts(a("nk"), cols("tot", 0, 6, k=AZ[:6]), 2.5, A.is_ge)
+        for w in range(2):
+            tt(cols("tk", 6 * w, 6 * w + 6, k=str(w)), a("nk"), cols("dumL", 6 * w, 6 * w + 6), A.mult)
+        tt(a("Lq"), a("Lf"), a("tk", k="01"), A.max)
+        cp(cols("LE", 0, 12, k="0"), a("Lq"))
+        cp(cols("LE", 12, 18, k="1"), cols("Lq", 0, 6))
+        le0, le1 = cols("LE", 0, 12, k="0"), cols("LE", 6, 18, k="01")
+
+        def put(win, src):
+            run("v", lambda: g.vector.tensor_copy(win[0].indirect(le1[0]), src[0]), [win], [src, le1])
+        if t < 2:
+            act(a("gn"), ind(NX, le0))
+            cp(a("gx"), ind(XN, le0))
+            put(NX, a("gn"))
+            put(XN, a("gx"))
+            if t == 1:
+                n8 = lambda nm, r, lo, hi: (T[nm][r:128:16, lo:hi], NX[1] if nm == "NX" else [nm])
+                dma("g", n8("N32", 0, 0, W), n8("NX", 0, 0, W))
+                dma("g", n8("N32", 0, W, PL), n8("NX", 7, W, PL))
+                dma("g", n8("N32", 0, 0, PL), n8("NX", 1, 0, PL), accum_op=A.add, max_dma_last_dim=4096)
+        else:
+            cp(a("g32"), ind(a("N32"), le0))
+            put(a("N32"), a("g32"))
+            dma("y", ext(T.yn[:]), a("N32", slice(0, 128, 16), slice(0, PL)))
+            dma("s", ext(T.yw[:]), a("WW", k="01"))
+            cp(lo_, a("LP", k="01"))
+            cp(hi_, a("LO", k="01"))
+            tt(cols("yco", 0, 48, k="0"), lo_, hi_, A.min)
+            tt(a("cd"), lo_, hi_, A.max)
+            ts(cols("yco", 48, 96, k="1"), a("cd"), -3072.0, A.add)
+            dma("s", ext(T.yc[:]), a("yco", k="01"))
+    for sem, val in total.items():
+        need("g", sem, val)

@@ -1,29 +1,28 @@
-from concourse.mybir import AluOpType as A, ActivationFunctionType as F, AxisListType
+from concourse.mybir import AluOpType as A, ActivationFunctionType as F
 
-W, K, PL, DUM = 3072, 768, 6144, 6336
+W, K, OFF, TY, DUM, PL = 3072, 768, 64, 4096, 7232, 7424
+KK = 262144.0
 F4, B2, I4, U2 = "float32", "bfloat16", "int32", "uint16"
 SCRATCH = {}
 for names, shape, dtype in (
-        ("XS XF0 XF1 XF2", [W], B2), ("XN NX", [DUM], B2), ("INFO Z", [PL], B2), ("N32", [DUM], F4), ("WW DD", [K], F4),
-        ("nb_", [24, 16], I4), ("nbf", [24, 16], F4), ("ld2 lt2", [24, 2, 16], F4), ("fr", [384], F4), ("LX", [384], U2),
-        ("memc froc", [192], I4), ("curc", [96], I4), ("typc", [48], I4), ("cl yco", [96], F4), ("cd cx cp cq", [48], F4), ("ti", [4, 192], I4),
-        ("T0 T1 TL M0 M1 M01 MT1 MT0 ML1 ML0 NM0 NM1 FH FL", [192], B2), ("ZR", [384], B2),
-        ("pc", [8], I4), ("pf", [8], F4), ("kr kg BL", [128], F4), ("tb", [192], F4), ("mk nbj nb1", [64], F4), ("dm0 dumL", [12], F4),
-        ("pi co", [16], F4), ("hm", [2], F4), ("CN", [24], B2), ("CK", [8], B2), ("CP G8", [16], B2), ("CB1 CB2", [128], B2), ("Mk", [4], F4),
-        ("DL", [24], F4), ("S96 I96 O96 DUMC", [96], B2), ("I6", [6], F4),
-        ("PO", [2, 2, 8, 4], F4), ("PI", [2, 2, 8, 4], I4), ("LP LO LD LK", [48], U2), ("ge nr RA RB", [K], B2),
-        ("t1", [2, 8, 4], F4), ("dd hd", [2, 16, 4], F4), ("TP TO TK", [2, 8, 4, 4], F4),
-        ("fl df d2 ne de", [2, 8, 4], F4), ("wt cs", [64], B2), ("rk wd", [64], F4), ("CC", [1536], B2),
-        ("RU", [192], U2), ("L6", [256], F4), ("Lf tk Lq", [12], F4), ("tot nk", [6], F4), ("eq", [2304], B2), ("jk", [1536], B2),
-        ("gx gn", [192], B2), ("g32", [192], F4), ("LE", [18], U2)):
+        ("XS XF0 XF1 XF2", [W], B2), ("XN NX", [PL], B2), ("INFO", [OFF + W], B2), ("N32", [PL], F4), ("WW DD", [K], F4),
+        ("NB", [2, 2, 96], I4), ("NF", [2, 6, 2, 16], F4), ("FT", [2, 6, 32], F4), ("LX", [384], U2),
+        ("memc froc", [192], I4), ("curc ya", [96], I4), ("typc c1 cd cx cp cq cr m2 ct cf tt_ tu tf ta lr", [48], I4), ("yco", [96], F4),
+        ("HI LO B1 MB FH FL hb", [192], B2), ("GN", [2 * K], B2), ("RA", [K], B2),
+        ("RR PO", [2, 48], I4), ("YY", [48], F4), ("LP LR LK", [48], U2),
+        ("pc", [4], I4), ("pf", [8], F4), ("xr", [144], F4), ("OH co", [32], F4), ("WB WX WF WM", [144], B2),
+        ("kr kg", [128], F4), ("BL BN BK UW U1 I128", [128], B2), ("BF", [128], F4),
+        ("KC MK", [96], F4), ("kb kb0 CA", [6], F4), ("k16 CD1", [192], B2), ("CD2", [96], B2), ("DA DB D0 D1 D2", [192], F4),
+        ("on wt cs", [48], B2), ("SG", [288], F4), ("LC", [6], U2), ("RK", [64], F4), ("W1 W2", [64], I4),
+        ("MV LS QQ g32", [192], F4), ("RU", [192], U2), ("EQ", [2304], B2), ("LQ", [12], F4), ("LE0 LE1", [12], U2),
+        ("gx gn", [192], B2), ("NC NC2", [384], F4)):
     for nm in names.split():
         SCRATCH[nm] = ("sbuf", [128] + shape, dtype)
-PSUMS = ("N0", "N1", "C0", "C1", "XB", "L0", "L1", "XA")
+PSUMS = ("F0", "F1", "PA", "PB", "PC", "PD", "PE", "PH")
 for nm in PSUMS:
-    SCRATCH[nm] = ("psum", [128, 512] if nm in ("L0", "L1", "XA") else [128, 128, 4], F4)
-SEMAPHORES = ["qv", "qp", "qs", "qg", "xl", "xa0", "xa1", "xa2"] + ["e%d" % k for k in range(12)] + ["d%d" % k for k in range(60)]
-AZ = "abcdefghijklmnopqrstuvwxyz"
-SEQ, NV = "st C PO' pd' ls' t1 dO dP hh LP' hd".split(), 2
+    SCRATCH[nm] = ("psum", [128, 512], F4)
+SEMAPHORES = ["qv", "qp", "qs", "qg", "xl", "xa0", "xa1", "xa2"] + ["e%d" % k for k in range(14)] + ["d%d" % k for k in range(30)]
+AZ = "abcdefghijklmnopqrstuvwxyzABCDEF"
 
 
 def rank_program(g, core, T, topo):
@@ -50,14 +49,14 @@ def rank_program(g, core, T, topo):
             kn[s2] = max(kn.get(s2, 0), v2)
         kn[sem] = max(kn.get(sem, 0), val)
 
-    def deps(q, rd, wr, acc=False):
+    def deps(q, rd, wr):
         for key in rd + wr:
             w = last.get(key)
-            if w is not None and not (acc and w[2] == q and key in wr):
+            if w is not None and not (w[2] == q and key not in rd and w[0][0] == "q"):
                 need(q, w[0], w[1])
             if key in PSUMS or key in wr:
                 for s2, (v2, q2) in list(reads.get(key, {}).items()):
-                    if q2 != q or s2[0] in "de":
+                    if q2 != q or s2[0] in "dex":
                         need(q, s2, v2)
 
     def done(q, sem, val, rd, wr):
@@ -71,16 +70,19 @@ def rank_program(g, core, T, topo):
             if key not in wr:
                 reads.setdefault(key, {})[sem] = (val, q)
 
-    def run(q, fn, outs, ins, acc=False):
+    def run(q, fn, outs, ins):
         rd = [x for i in ins for x in i[1]]
         wr = [x for o in outs for x in o[1]]
-        deps(q, rd, wr, acc)
+        deps(q, rd, wr)
         sem = "q" + q
         total[sem] = total.get(sem, 0) + 1
         fn().then_inc(T.sem[sem], 1)
         done(q, sem, total[sem], rd, wr)
 
     def dma(q, out, in_, **kw):
+        for key in out[1]:
+            if key in last:
+                need(q, last[key][0], last[key][1])
         deps(q, in_[1], out[1])
         c = "e" if q == "g" else "d"
         sem = "%s%d" % (c, nd[c])
@@ -89,7 +91,7 @@ def rank_program(g, core, T, topo):
         eng[q].dma_start(out[0], in_[0], **kw).then_inc(T.sem[sem], 16)
         done(q, sem, 16, in_[1], out[1])
 
-    def tt(out, i0, i1, op):
+    def tt(out, i0, i1, op, more=()):
         run("v", lambda: g.vector.tensor_tensor(out[0], i0[0], i1[0], op), [out], [i0, i1])
 
     def ts(out, i0, s1, op0, s2=None, op1=None):
@@ -105,7 +107,10 @@ def rank_program(g, core, T, topo):
     def fill(out, v):
         run("v", lambda: g.vector.memset(out[0], v), [out], [])
 
-    def act(out, i0, scale=None, bias=None, acc=None):
+    def scan(out, d0, d1, op0, op1):
+        run("v", lambda: g.vector.tensor_tensor_scan(out[0], d0[0], d1[0], 0.0, op0, op1), [out], [d0, d1])
+
+    def act(out, i0, scale=None, bias=None, acc=None, fn=None):
         kw, ins, outs = {}, [i0], [out]
         for nm, x in (("scale", scale), ("bias", bias)):
             if isinstance(x, tuple):
@@ -116,125 +121,99 @@ def rank_program(g, core, T, topo):
         if acc is not None:
             outs.append(acc)
             kw["accum_out"] = acc[0]
-        fn = F.Identity if isinstance(bias, tuple) else F.Copy
+        fn = fn or (F.Identity if isinstance(bias, tuple) else F.Copy)
         run("s", lambda: g.scalar.activation(out[0], i0[0], fn, **kw), outs, ins)
 
     def mm(out, lhsT, rhs, start=True, stop=True):
-        run("p", lambda: g.tensor.matmul(out[0], lhsT[0], rhs[0], start, stop), [out], [lhsT, rhs], acc=True)
+        run("p", lambda: g.tensor.matmul(out[0], lhsT[0], rhs[0], start, stop), [out], [lhsT, rhs])
 
-    def iota(out, pattern, base, cm, **kw):
+    def iota(out, pattern, base, cm):
+        kw = {} if out[1][0].startswith("pc") else {"allow_small_or_imprecise_dtypes": True}
         run("g", lambda: g.iota(out[0], pattern, base, cm, **kw), [out], [])
 
-    ext = lambda ap: (ap, [])
-    al, R = slice(None), slice(0, 96)
-    cols = lambda nm, lo, hi, k="": a(nm, al, slice(lo, hi), k=k)
+    def asel(out, in_, pattern, op, fill_, base, cm):
+        run("g", lambda: g.affine_select(out[0], in_[0], pattern, op, fill_, base, cm), [out], [in_])
+
+    ext = lambda ap, k=(): (ap, list(k))
+    al = slice(None)
+    cols = lambda nm, lo, hi, k="", step=1: a(nm, al, slice(lo, hi, step), k=k)
     col = lambda nm, j: a(nm, al, slice(j, j + 1), k=AZ[j])
     half = lambda nm, b: cols(nm, 384 * b, 384 * b + 384, k=str(b))
     l24 = lambda nm, b: cols(nm, 24 * b, 24 * b + 24, k=str(b))
+    rows = lambda nm, r, lo, hi, k: (T[nm][r:128:16, lo:hi], k)
+    at = lambda s: OFF + TY * s
 
-    dma("s", a("nb_"), ext(T.nxt[:]))
+    def tolist(out, wts, buf, lo, hi, k, start=True, stop=True):
+        for r in range(16):
+            mm(out, cols(wts, 15 - r, 143 - r), cols(buf, lo + r, hi, k=k, step=16), start and r == 0, stop and r == 15)
+
+    for s in range(2):
+        for h in range(2):
+            dma("ys"[s], a("NB", al, s, h, al, k=AZ[2 * s + h]), ext(T.nxt[h:8:2, W * s:W * s + W]))
     dma("y", a("memc"), ext(T.mem[:]))
     dma("s", a("curc"), ext(T.cur[:]))
-    dma("y", a("froc"), ext(T.fro[:]))
     dma("s", a("typc"), ext(T.typ[:]))
     dma("y", a("XS"), ext(T.x[:]))
+    dma("s", a("froc"), ext(T.fro[:]))
 
-    fl_ = {"allow_small_or_imprecise_dtypes": True}
     iota(col("pc", 0), [[0, 1]], 0, 1)
-    iota(a("tb"), [[64, 3], [0, 64]], 0, 0, **fl_)
-    iota(a("TL"), [[0, 3], [1, 64]], 0, 0, **fl_)
-    iota(a("kr"), [[1, 128]], 0, 0, **fl_)
-    dma("g", a("WW", k="01"), ext(T.w0[:]))
-    iota(a("kg"), [[1, 8], [0, 16]], 0, 0, **fl_)
-    iota(a("mk"), [[0, 16], [1, 4]], 0, 0, **fl_)
-    iota(a("nbj"), [[384, 2], [0, 8], [1, 4]], 768, 4, **fl_)
-    iota(a("nb1"), [[384, 2], [0, 8], [1, 4]], 769, 4, **fl_)
-    iota(a("dm0"), [[96, 2], [16, 6]], 6144, 0, **fl_)
-    for j, op in ((1, (15, A.bitwise_and)),
-                  (2, (4, A.arith_shift_right)),
-                  (3, (3, A.bitwise_and)), (4, (2, A.arith_shift_right)),
-                  (5, (4, A.arith_shift_right, 1, A.bitwise_and))):
-        ts(col("pc", j), col("pc", 0), *op)
-    cp(cols("pf", 0, 6, k=AZ[:6]), cols("pc", 0, 6, k=AZ[:6]))
+    iota(a("xr"), [[1, 144]], 0, 0)
+    iota(a("hb"), [[1, 3], [0, 64]], 1, 0)
+    iota(a("LO"), [[0, 3], [1, 64]], 0, 0)
+    fill(a("INFO", k=AZ[:8]), 0.0)
+    ts(col("pc", 1), col("pc", 0), 15, A.bitwise_and)
+    ts(col("pc", 2), col("pc", 0), 4, A.arith_shift_right)
+    cp(cols("pf", 0, 3, k="abc"), cols("pc", 0, 3, k="abc"))
     p0, pm, gi = col("pf", 0), col("pf", 1), col("pf", 2)
-    ts(col("pf", 6), pm, 192.0, A.mult)
-    ts(col("hm", 0), col("pf", 5), -1.0, A.mult, 1.0, A.add)
-    ts(a("T0"), a("tb"), col("pf", 6), A.add)
-    ts(a("T1"), a("T0"), 3072.0, A.add)
-    act(cols("L0", 0, 192), a("T0"))
-    act(cols("L0", 192, 384), a("T1"))
-    act(cols("L1", 0, 192), a("TL"))
-    fill(a("ZR"), 0.0)
-    ts(a("pi", k=AZ[:16]), cols("kr", 0, 16), pm, A.is_equal)
-    ts(cols("G8", 0, 8, k="0"), cols("kr", 0, 8), gi, A.is_equal)
-    co, pi = (lambda j: col("co", j)), (lambda j: col("pi", j))
-    g8 = cols("G8", 0, 8, k="0")
-    act(co(7), pi(4), scale=0.25)
-    act(co(1), pi(0), bias=pi(1))
-    act(co(0), co(1), bias=co(7))
-    act(co(10), pi(2), bias=pi(3))
-    act(co(11), co(10), bias=pi(5))
-    act(co(12), co(0), scale=-1.0)
-    act(co(2), co(11), bias=co(12))
-    act(cols("CN", 0, 8, k="0"), g8, scale=co(0))
-    act(cols("CN", 8, 16, k="1"), g8, scale=pi(6))
-    act(cols("CN", 16, 24, k="2"), g8, scale=co(2))
-    act(cols("G8", 8, 16, k="1"), g8)
-    ts(a("Mk"), cols("kr", 0, 4), col("pf", 3), A.is_equal)
-    ts(a("DL"), cols("kr", 0, 24), col("pf", 4), A.is_equal)
+    ts(col("pf", 3), gi, 16.0, A.mult, 15.0, A.add)
+    ts(cols("OH", 0, 16), cols("xr", 0, 16), pm, A.is_equal)
+    ts(a("WB"), a("xr"), col("pf", 3), A.is_equal, KK, A.mult)
+    act(col("pf", 4), pm, scale=3.0)
+    act(a("HI"), a("hb"), bias=col("pf", 4))
+    put_info = lambda q, r, nm: dma(q, rows("INFO", r, OFF, OFF + W, ["INFO" + AZ[r]]), a(nm))
+    put_info("y", 1, "LO")
+    put_info("s", 0, "HI")
+    nco = [0]
+    chains = {"sc0": [(0, 256 / KK), (1, 4 / KK), (2, 65536 / KK), (4, 1 / KK)],
+              "sc1": [(0, 256 / KK), (1, 4 / KK), (2, -131072 / KK), (4, -2 / KK), (3, 65536 / KK), (5, 1 / KK)],
+              "bi0": [(9, 1 / 16), (8, -32768 / KK)], "bi1": [(9, 1 / 16), (8, -49152 / KK)],
+              "wx": [(0, 1.0), (1, 1.0), (4, 1.0), (5, 1.0), (8, -1.0), (9, -136.0)], "wf": [(6, 1 / KK), (7, 1 / KK)], "wm": [(3, 1 / KK)]}
+    co, made = {}, {}
+    for step in range(6):
+        for nm, terms in chains.items():
+            if step < len(terms):
+                key = tuple(terms[:step + 1])
+                if key not in made:
+                    made[key] = col("co", nco[0])
+                    nco[0] += 1
+                    act(made[key], cols("OH", terms[step][0], terms[step][0] + 1), scale=terms[step][1], bias=co.get(nm))
+                co[nm] = made[key]
+    for nm, w in (("WX", "wx"), ("WF", "wf"), ("WM", "wm")):
+        act(a(nm), a("WB"), scale=co[w])
 
-    ti = lambda j: a("ti", al, j, al, k=str(j))
-    ts(ti(0), a("memc"), 1, A.bitwise_and)
-    ts(ti(1), a("memc"), 1, A.arith_shift_right)
-    cp(a("M0"), ti(0))
-    cp(a("M1"), ti(1))
-    cp(a("nbf"), a("nb_"))
-    tt(a("MT1"), a("M1"), cols("L0", 192, 384), A.mult)
-    tt(a("MT0"), a("M0"), cols("L0", 0, 192), A.mult)
-    tt(a("ML1"), a("M1"), cols("L1", 0, 192), A.mult)
-    tt(a("ML0"), a("M0"), cols("L1", 0, 192), A.mult)
-    act(a("ld2", al, al, 0, al, k="0"), a("nbf"), scale=col("hm", 0))
-    act(a("ld2", al, al, 1, al, k="1"), a("nbf"), scale=col("pf", 5))
-    act(a("NM0"), a("M0"), scale=-1.0, bias=1.0)
-    act(a("NM1"), a("M1"), scale=-1.0, bias=1.0)
-    act(cols("L1", 192, 384), a("M1"), scale=0.25)
-    lo_, hi_ = cols("cl", 0, 48, k="0"), cols("cl", 48, 96, k="1")
-    cp(lo_, cols("curc", 0, 48))
-    ts(hi_, cols("curc", 48, 96), 3072.0, A.add)
-    ts(ti(2), a("froc"), 6, A.arith_shift_right)
-    tt(a("cd"), hi_, lo_, A.subtract)
-    ts(ti(3), a("froc"), 63, A.bitwise_and)
+    def nextlist(s):
+        for h in range(2):
+            cp(a("NF", al, s, al, h, al, k=AZ[2 * s + h]), a("NB", al, s, h, al, k=AZ[2 * s + h]))
+        run("v", lambda: g.vector.transpose(T.FT[:, s], T.NF[:, s]), [a("FT", k=str(s))], [a("NF", k=AZ[2 * s:2 * s + 2])])
+        for b in range(6):
+            cp(cols("LX", 192 * s + b, 192 * s + 192, k=AZ[6 * s + b], step=6), a("FT", al, s, b, al, k=str(s)))
+    ts(a("B1"), a("memc"), 2.0, A.is_ge)
+    cp(a("MB"), a("memc"))
+    for r, nm in ((2, "B1"), (3, "MB"), (4, "B1"), (5, "MB")):
+        put_info("y", r, nm)
+    nextlist(0)
+    nextlist(1)
+    c0 = cols("curc", 0, 48)
+    ts(a("c1"), cols("curc", 48, 96), float(TY), A.add)
+    ts(a("m2"), a("typc"), -1.0, A.mult, 2.0, A.add)
+    tt(a("cd"), a("c1"), c0, A.subtract)
     tt(a("cx"), a("cd"), a("typc"), A.mult)
-    ts(a("FH"), ti(2), 64.0, A.mult)
-    tt(a("cp"), lo_, a("cx"), A.add)
-    tt(a("cq"), hi_, a("cx"), A.subtract)
-    cp(a("FL"), ti(3))
-    cp(a("LP", k="01"), a("cp"))
-    cp(a("LO", k="01"), a("cq"))
-    tt(a("M01"), a("M0"), cols("L1", 192, 384), A.mult)
-    for n in range(6):
-        dma("y", (T.INFO[10 + n:128:16, :], ["INFO" + AZ[20 + n]]), a("ZR"))
-    for r, lo, hi in ((0, "T0", "T1"), (1, "TL", "TL"), (7, "T1", "T0"), (4, "M1", "M0"), (2, "MT1", "MT0"), (3, "ML1", "ML0"), (6, "NM1", "NM0"),
-                      (8, "FH", "FH"), (9, "FL", "FL"), (5, "M01", "M01")):
-        for h, nm in enumerate((lo, hi)):
-            dma("sy"[h], (T.INFO[r:128:16, W * h:W * h + W], ["INFO" + AZ[2 * r + h]]), a(nm))
-    info = lambda lo, hi: cols("INFO", lo, hi, k=AZ)
-
-    run("v", lambda: g.vector.transpose(T.lt2[:], T.ld2[:]), [a("lt2")], [a("ld2", k="01")])
-    lx = lambda h: cols("LX", 192 * h, 192 * h + 192, k=str(h))
-    for h in range(2):
-        for ch in range(8 * h, 8 * h + 8):
-            tt(cols("fr", 24 * ch, 24 * ch + 24, k=AZ[ch]), a("lt2", al, al, 0, ch), a("lt2", al, al, 1, ch), A.add)
-        cp(lx(h), cols("fr", 192 * h, 192 * h + 192, k=AZ[8 * h:8 * h + 8]))
-    fill(cols("NX", PL, DUM, k="2"), 0.0)
-    fill(cols("XN", PL, DUM, k="2"), 0.0)
-    for h in range(2):
-        cp(cols("XN", W * h, W * h + W, k=str(h)), ind(a("XS"), lx(h)))
-        act(cols("NX", W * h, W * h + W, k=str(h)), ind(info(W * h, W * h + W), lx(h)))
-        if h == 0:
-            cp(half("RB", 0), ind(info(0, PL), l24("LO", 0)))
-            act(half("RB", 1), ind(info(0, PL), l24("LO", 1)))
-    XN, NX = a("XN", k="012"), a("NX", k="012")
+    tt(a("cq"), a("c1"), a("cx"), A.subtract)
+    tt(a("cp"), c0, a("cx"), A.add)
+    ts(a("cr"), a("cq"), TY - 1, A.bitwise_and)
+    ts(a("LP", k="01"), a("cp"), float(OFF), A.add)
+    ts(a("LR", k="01"), a("cr"), float(OFF), A.add)
+    ts(a("cq"), a("cq"), 4.0, A.mult, 4.0 * OFF, A.add)
 
     def sendx(t):
         deps("g", ["XS"], [])
@@ -248,218 +227,203 @@ def rank_program(g, core, T, topo):
         total[sem] = n
         g.remote_dma(T["XF%d" % t][:], T.XS[:], T.sem[sem], T.sem.xl, pid, rid, topo.mask(core, dst))
         last["XF%d" % t] = (sem, n, "-")
+    iota(a("kr"), [[1, 128]], 0, 0)
+    iota(a("kg"), [[1, 8], [0, 16]], 0, 0)
+    iota(a("k16"), [[0, 12], [1, 16]], 0, 0)
     sendx(0)
-    iota(a("Z"), [[0, PL]], 0, 0, **fl_)
-    iota(a("N32"), [[0, DUM]], 0, 0, **fl_)
-    for k, (r, h, nm) in enumerate(((10, 0, "T0"), (10, 1, "T1"), (11, 0, "TL"), (11, 1, "TL"))):
-        deps("y", [], ["Z"])
-        dma("y", (T.Z[r:128:16, W * h:W * h + W], ["Z" + AZ[k]]), a(nm))
-    zz = (T.Z[:], ["Z", "Za", "Zb", "Zc", "Zd"])
+    dma("g", a("WW", k="01"), ext(T.w0[:]))
+    for nm in ("XN", "NX"):
+        for k, (lo, hi) in zip("xyz", ((0, OFF), (OFF + W, at(1)), (DUM, PL))):
+            iota(cols(nm, lo, hi, k=k), [[0, hi - lo]], 0, 0)
 
-    def tform(bank, c0, n, rowbuf, b, rhs):
-        for i1 in range(4):
-            mm(a(bank, R, slice(c0, c0 + n), i1), a(rowbuf, al, slice(384 * b + i1, 384 * b + 384, 4), k=str(b)), rhs)
-
-    def pads(tp, b, src, nv, between=()):
-        for i0 in range(4):
-            if i0 in (1, 3) and between:
-                between[i0 // 2]()
-            out, m = a(tp, R, b, al, i0, al, k=str(4 * b + i0)), a("Mk", R, slice(i0, i0 + 1))
-            if i0 < nv:
-                ts(out, src, m, A.mult)
-            else:
-                act(out, src, scale=m)
-
-    def tolist(bank, c0, tp, b):
-        mm(cols(bank, c0, c0 + 24), (T[tp][0:96, b], [tp + str(4 * b + i) for i in range(4)]), a("DL", R))
-
-    ot = lambda b: (T.PO[0:96, b, 0], ["PO%d" % b])
-    pt = lambda b: (T.PO[0:96, b, 1], ["PO%d" % b])
+    lx = lambda s, lo, hi: cols("LX", 192 * s + lo, 192 * s + hi, k=AZ[6 * s:6 * s + 6])
+    piece = lambda nm, s, lo, hi, k: cols(nm, at(s) + 16 * lo, at(s) + 16 * hi, k=k)
+    info = lambda lo: cols("INFO", lo, OFF + W, k=AZ[:8])
+    act(piece("XN", 0, 0, 192, "a"), ind(a("XS"), lx(0, 0, 192)))
+    cp(piece("XN", 1, 0, 192, "b"), ind(a("XS"), lx(1, 0, 192)))
+    act(a("RA", k="01"), ind(info(0), a("LR", k="01")))
     for b in range(2):
-        tform("XB", 8 * b, 8, "RB", b, cols("CN", 0, 8, k="0"))
-        cp(ot(b), a("XB", R, slice(8 * b, 8 * b + 8), al))
+        tolist(cols("PH", 24 * b, 24 * b + 24), "WM", "RA", 384 * b, 384 * b + 384, str(b))
+    ts(piece("NX", 0, 0, 192, "a"), ind(info(OFF), lx(0, 0, 192)), co["sc0"], A.mult, co["bi0"], A.add)
+    act(piece("NX", 1, 0, 192, "b"), ind(info(OFF), lx(1, 0, 192)), scale=co["sc1"], bias=co["bi1"])
+    tt(a("ct"), cols("PH", 0, 48), a("m2"), A.mult)
+    XN, NX = a("XN", k="abxyz"), a("NX", k="abxyz")
 
-    def start(b):
-        off, gew, ww = l24("LP", b), half("ge", b), half("WW", b)
-        tt(gew, ind(XN, off), ww, A.is_ge)
-        act(a("N%d" % b, R, slice(0, 8), al), ot(b))
-        c, k2 = 384 * b, (str(b), "xy"[b])
-        act(cols("nr", c, c + 256, k=k2[0]), ind(NX, cols("LP", 24 * b, 24 * b + 16, k=str(b))))
-        act(cols("nr", c + 256, c + 384, k=k2[1]), ind(NX, cols("LP", 24 * b + 16, 24 * b + 24, k=str(b))))
-        for lo, hi, kk in ((0, 64, k2[0]), (64, 96, k2[1])):
-            for i1 in range(4):
-                mm(a("N%d" % b, slice(lo, hi), slice(8, 32), i1), a("nr", al, slice(c + 4 * lo + i1, c + 4 * hi, 4), k=kk), a("CN", k="012"))
+    iota(a("KC"), [[1, 96]], 1025, 0)
+    iota(a("kb0"), [[16, 6]], 0, 0)
+    iota(a("D0"), [[0, 192]], 65536, 0)
+    iota(a("D1"), [[96, 2], [16, 6], [0, 16]], DUM, 0)
+    asel(a("DA"), a("D0"), [[0, 12], [1, 16]], A.is_equal, -1.0, 0, 0)
+    asel(a("D2"), a("D1"), [[0, 12], [1, 16]], A.is_equal, -65536.0, 0, 0)
+    n32 = lambda h: iota(cols("N32", PL // 2 * h, PL // 2 * (h + 1), k="xy"[h]), [[0, PL // 2]], 0, 0)
+    n32(0)
 
-    def find_ops(b, nv):
-        C, N, k = "C%d" % b, "N%d" % b, str(b)
-        t1, hh, hd = a("t1", R, b, k=k), a(C, R, slice(32, 48), al), a("hd", R, b, k=k)
-        dO, dP, dd = (T.dd[0:96, b, 0:8, :], ["ddO" + k]), (T.dd[0:96, b, 8:16, :], ["ddP" + k]), (T.dd[0:96, b], ["ddO" + k, "ddP" + k])
-        po = (T.PO[0:96, b], ["PO" + k])
-        return {"st": lambda: start(b), "C": lambda: tform(C, 0, 16, "ge", b, a("G8", k="01")),
-                "t1": lambda: tt(t1, a(N, R, slice(16, 24), al), ot(b), A.mult),
-                "dO": lambda: tt(dO, a(N, R, slice(8, 16), al), ot(b), A.subtract),
-                "dP": lambda: tt(dP, a(N, R, slice(24, 32), al), t1, A.add),
-                "hh": lambda: ts(hh, a(C, R, slice(0, 16), al), 8.5, A.is_ge),
-                "hd": lambda: tt(hd, hh, dd, A.mult),
-                "PO": lambda: tt(po, a(N, R, slice(0, 16), al), hd, A.add),
-                "pd": lambda: pads("TP", b, pt(b), nv),
-                "ls": lambda: tolist("L%d" % b, 0, "TP", b),
-                "LP": lambda: cp(l24("LP", b), cols("L%d" % b, 0, 24))}
+    def fro_lo():
+        tt(a("FL"), a("froc"), a("FH"), A.subtract)
+        put_info("y", 6, "FH")
+        put_info("y", 7, "FL")
+    late_v = [lambda: cp(a("FH"), a("froc")), fro_lo, lambda: ts(a("BL"), a("kg"), gi, A.is_equal), lambda: ts(a("I128"), a("kr"), p0, A.is_equal),
+              lambda: ts(a("CD1"), a("k16"), pm, A.not_equal, 65536.0, A.mult), lambda: fill(a("on"), 1.0),
+              lambda: fill(cols("RK", 48, 64, k="z"), 0.0), lambda: fill(cols("W1", 48, 64, k="z"), 0), lambda: fill(cols("W2", 48, 64, k="z"), 0)]
+    late_s = [lambda: act(a("BN"), a("BL"), scale=-1.0), lambda: act(a("BF"), a("BL")), lambda: act(a("BK"), a("BL"), scale=16384.0),
+              lambda: act(a("CD2"), cols("CD1", 0, 96), scale=1.625, bias=-40960.0), lambda: act(col("pf", 5), pm, bias=0.5),
+              lambda: act(a("kb"), a("kb0"), bias=col("pf", 5)), lambda: act(a("DB"), a("D2"), bias=pm)]
 
-    def wants(b):
-        k = str(b)
-        PO, PI = (lambda j: (T.PO[0:96, b, j], ["PO" + k])), (lambda j: (T.PI[0:96, b, j], ["PI" + k]))
-        f = lambda nm: a(nm, R, b, k=k)
-        return [lambda: cp((T.PI[0:96, b], ["PI" + k]), (T.PO[0:96, b], ["PO" + k])),
-                lambda: tt(f("fl"), PO(1), PI(1), A.subtract),
-                lambda: tt(f("df"), PI(0), PI(1), A.subtract),
-                lambda: tt(f("d2"), f("df"), f("df"), A.mult),
-                lambda: ts(f("ne"), f("d2"), 9437184.0, A.not_equal, 4.0, A.mult),
-                lambda: tt(a("wt", R, slice(32 * b, 32 * b + 32), k=k), f("fl"), f("ne"), A.mult)]
+    def late_g():
+        asel(a("U1"), a("BN"), [[-1, 128]], A.is_gt, 0.0, 0, 1)
+        asel(a("UW"), a("U1"), [[-1, 128]], A.not_equal, 1024.0, 0, 1)
 
-    def late_constants():
-        for j, i, k in ((3, 8, 9), (4, 7, 1), (5, 10, 11), (6, 1, 11)):
-            act(co(j), pi(i), bias=pi(k))
-        act(co(8), pi(7), scale=6144.0)
-        act(co(9), pi(10), scale=6240.0)
-        act(co(13), co(8), bias=co(9))
-        act(a("CK"), g8, scale=co(3))
-        act(cols("CP", 0, 8, k="0"), g8, scale=co(4))
-        act(cols("CP", 8, 16, k="1"), g8, scale=co(5))
-        ts(a("BL"), a("kg"), gi, A.is_equal)
-        act(a("CB1"), a("BL"), scale=co(4))
-        act(a("CB2"), a("BL"), scale=co(5))
-        ts(a("mk"), a("mk"), 0.5, A.is_ge)
-        ts(a("I96"), cols("kr", 0, 96), p0, A.is_equal)
-        ts(a("S96"), cols("kr", 0, 96), p0, A.is_gt)
-        fill(a("O96"), 1.0)
-        ts(a("I6"), cols("kr", 0, 6), p0, A.is_equal)
-        ts(a("DUMC"), cols("kr", 0, 96), co(6), A.mult, co(13), A.add)
-        ts(a("dumL"), a("dm0"), pm, A.add)
+    rr = lambda j, b: a("RR", al, j, slice(24 * b, 24 * b + 24), k="abcd"[2 * j + b])
+    po = lambda j, b: a("PO", al, j, slice(24 * b, 24 * b + 24), k="abcd"[2 * j + b])
+    both = lambda nm, b: a(nm, al, al, slice(24 * b, 24 * b + 24), k="ac" if b == 0 else "bd")
+
+    def gather(b):
+        Fb, c = "F%d" % b, K * b
+        tt(cols("GN", c, c + 384, k="ab"[b]), ind(XN, l24("LP", b)), half("WW", b), A.is_ge)
+        act(cols("GN", c + 384, c + K, k="cd"[b]), ind(NX, l24("LP", b)))
+        tolist(cols(Fb, 0, 48), "WB", "GN", c, c + K, ("ac", "bd")[b], stop=False)
+        tolist(cols(Fb, 0, 24), "WX", "GN", c + 384, c + K, "cd"[b], start=False)
+
+    def step(b, cast=True, gaps=()):
+        gaps = list(gaps)
+        gap = lambda: gaps.pop(0)() if gaps else None
+        Fb = "F%d" % b
+        tt(l24("YY", b), cols(Fb, 24, 48), po(1, b), A.max)
+        tt(rr(1, b), cols(Fb, 0, 24), po(1, b), A.max)
+        tt(rr(0, b), cols(Fb, 0, 24), l24("YY", b), A.min)
+        gap()
+        ts(both("PO", b), both("RR", b), 32767, A.bitwise_and)
+        gap()
+        if cast:
+            ts(l24("LP", b), po(0, b), 0.25, A.mult)
+        gap()
+
+    def reclist(b):
+        ts(l24("lr", b), rr(0, b), 16383, A.bitwise_and)
+
+    def foreign(b):
+        ts(l24("LR", b), l24("lr", b), 0.25, A.mult)
+        act(half("RA", b), ind(info(0), l24("LR", b)))
+
+    def foreign2(b):
+        tolist(cols("PH", 24 * b, 24 * b + 24), "WF", "RA", 384 * b, 384 * b + 384, str(b))
 
     for t in range(3):
-        for q in range(4):
+        if t == 2:
+            dma("y", ext(T.yw[:], ["yw"]), a("WW", k="01"))
+        gather(0)
+        if t == 0:
+            ts(a("cf"), a("ct"), 1, A.arith_shift_right, 1, A.bitwise_and)
+        gather(1)
+        if t == 0:
+            tt(a("PO", al, 1, al, k="cd"), a("cq"), a("cf"), A.add)
+        for q in range(3):
             for b in range(2):
-                cur_, prv_ = find_ops(b, NV), find_ops(1 - b, NV)
-                for x in SEQ:
-                    if x[-1] != "'":
-                        cur_[x]()
-                    elif q + b > 0:
-                        prv_[x[:-1]]()
-            if t == 0 and q == 0:
-                late_constants()
-        fin = find_ops(1, NV)
-        for x in SEQ:
-            if x in ("hh'", "hd'", "PO'"):
-                fin[x[:-1]]()
-        pads("TO", 0, ot(0), 0)
-        tolist("L0", 64, "TO", 0)
-        w0, w1 = wants(0), wants(1)
-        w0[0]()
-        w1[0]()
-        w0[1]()
-        pads("TP", 1, pt(1), 4, w1[1:3])
-        tolist("L1", 0, "TP", 1)
-        act(half("RA", 0), ind(info(0, PL), l24("LP", 0)))
-        pads("TO", 1, ot(1), 0)
-        tolist("L0", 88, "TO", 1)
-        w0[2]()
-        w1[3]()
-        w0[3]()
-        cp(l24("LO", 0), cols("L0", 64, 88))
-        w0[4]()
-        w1[4]()
-        cp(cols("CC", 0, 96), a("DUMC"))
-        w1[5]()
-        w0[5]()
-        fin["LP"]()
-        act(half("RA", 1), ind(info(0, PL), l24("LP", 1)))
-        run("v", lambda: g.vector.tensor_tensor_scan(T.cs[0:96, :], T.mk[0:96, :], T.wt[0:96, :], 0.0, A.mult, A.add), [a("cs")], [a("mk"), a("wt", k="01")])
-        cp(l24("LO", 1), cols("L0", 88, 112))
-        for b in range(2):
-            act(half("RB", b), ind(zz, l24("LO", b)))
-        mm(a("XA", R, slice(0, 64)), a("I96", R), a("cs", R), True, False)
-        for i1 in range(4):
-            mm(a("XA", R, slice(i1, 64, 4)), a("S96", R), a("cs", R, slice(3, 64, 4)), False, False)
-            mm(a("XA", R, slice(32 + i1, 64, 4)), a("O96", R), a("cs", R, slice(3, 32, 4)), False, i1 == 3)
-        h32 = lambda nm, b, k: (T[nm][0:96, 32 * b:32 * b + 32], [nm + k])
-        for b in range(2):
-            tt(h32("rk", b, str(b)), h32("XA", b, ""), h32("nb1", b, ""), A.subtract)
-        for b in range(2):
-            tt(h32("wd", b, str(b)), h32("wt", b, str(b)), h32("rk", b, str(b)), A.mult)
-        for b in range(2):
-            tt(a("de", R, b, k=str(b)), h32("wd", b, str(b)), h32("nbj", b, ""), A.add)
-        for b in range(2):
-            pads("TP", b, a("de", R, b, k=str(b)), 4)
-            tolist("L1", 24 * b, "TP", b)
-        cp(a("LD"), cols("L1", 0, 48))
-        tt((T.CC[:].indirect(T.LD[:]), ["CC"]), a("RA", k="01"), (T.RB[:], ["RB0", "RB1", "LD"]), A.add)
-        for b in range(2):
-            tform("XB", 8 * b, 8, "RA", b, a("CK"))
-        for b in range(2):
-            pads("TK", b, a("XB", R, slice(8 * b, 8 * b + 8), al), 0)
-            tolist("L0", 24 * b, "TK", b)
-        for i in range(16):
-            mm(a("L1", slice(0, 6), slice(i, 256, 16)), a("CC", al, slice(i, 96, 16)), a("CP", k="01"))
-        mm(cols("XA", 128, 224), a("CB1"), cols("CC", 0, 96))
-        mm(cols("XA", 224, 320), a("CB2"), cols("CC", 0, 96))
-        act(a("L6", slice(0, 6)), a("L1", slice(0, 6), slice(0, 256)))
-        for k in range(2):
-            mm(cols("L1", 256 + 6 * k, 262 + 6 * k), a("L6", slice(0, 6), slice(128 * k, 128 * k + 128)), a("I6", slice(0, 6)))
-        cp(a("LK"), cols("L0", 0, 48))
+                n = 2 * q + b
+                step(b, gaps=late_v[2 * n:2 * n + 2] if t == 0 else ())
+                gather(b)
+                if t == 0 and n >= 2:
+                    for fn in late_s[2 * n - 4:2 * n - 2]:
+                        fn()
+                    if n == 2:
+                        late_g()
+                        sendx(1)
+        if t == 1:
+            n32(1)
+        r0, r1 = a("RR", al, 0, al, k="ab"), a("RR", al, 1, al, k="cd")
+        step(0, t < 2, [lambda: reclist(0), lambda: foreign(0)])
+        foreign2(0)
+        mm(cols("PD", 0, 192), a("I128"), a("CD1"), True, False)
+        mm(cols("PE", 0, 96), a("I128"), a("CD2"), True, False)
+        Fb = "F1"
+        tt(l24("YY", 1), cols(Fb, 24, 48), po(1, 1), A.max)
+        tt(rr(1, 1), cols(Fb, 0, 24), po(1, 1), A.max)
+        tt(rr(0, 1), cols(Fb, 0, 24), l24("YY", 1), A.min)
+        ts(cols("W2", 0, 48, k="a"), r1, 32767, A.bitwise_and, 2, A.arith_shift_right)
+        reclist(1)
+        tt(a("tt_"), r0, r1, A.subtract)
+        foreign(1)
+        ts(a("tf"), r0, 1, A.bitwise_and)
+        ts(a("tu"), a("tt_"), 16380, A.bitwise_and)
+        ts(a("ta"), r0, 16384.0, A.add)
+        tt(a("wt"), a("tu"), a("tf"), A.min)
+        ts(cols("W1", 0, 48, k="a"), a("ta"), 32767, A.bitwise_and, 2, A.arith_shift_right)
+        scan(a("cs"), a("on"), a("wt"), A.mult, A.add)
+        cp(l24("LK", 0), cols("PH", 0, 24))
+        mm(cols("PA", 0, 48), a("BL"), a("cs"))
+        mm(cols("PB", 0, 48), a("UW"), a("wt"), True, False)
+        mm(cols("PB", 0, 48), a("BL"), a("cs"), False, True)
+        foreign2(1)
+        for k in range(6):
+            act(cols("SG", 48 * k, 48 * k + 48, k=AZ[k]), cols("PA", 0, 48), scale=-1.0, bias=cols("kb", k, k + 1), acc=col("CA", k), fn=F.Sign)
+        cp(cols("RK", 0, 48, k="a"), cols("PB", 0, 48))
 
         def pull(b):
-            tt(half("DD", b), ind(a("XF%d" % t), cols("LK", 24 * b, 24 * b + 24)), half("WW", b), A.subtract)
+            tt(half("DD", b), ind(a("XF%d" % t), l24("LK", b)), half("WW", b), A.subtract)
 
         def addw(b):
             ts(half("DD", b), half("DD", b), 8.0, A.min, -8.0, A.max)
-            dma("g", half("WW", b), half("DD", b), accum_op=A.add)
-        if t < 2:
-            sendx(t + 1)
+            dma("g", half("WW", b) if t < 2 else ext(T.yw[:, 384 * b:384 * b + 384], ["yw"] if b == 0 else ["yw1"]), half("DD", b), accum_op=A.add)
         pull(0)
-        addw(0)
-        cp(a("RU"), cols("XA", 128, 320))
-        pull(1)
-        cp(a("Lf"), cols("L1", 256, 268))
-        for k in range(6):
-            for w in range(2):
-                ts(cols("eq", 384 * k + 192 * w, 384 * k + 192 * w + 192, k=AZ[2 * k + w]), a("RU"), (T.Lf[:, 6 * w + k:6 * w + k + 1], ["Lf"]), A.is_equal)
-            if k < 4:
-                act(cols("jk", 384 * k, 384 * k + 384, k=AZ[k]), cols("eq", 384 * k, 384 * k + 384, k=AZ[2 * k:2 * k + 2]), acc=col("tot", k))
-        addw(1)
-        for k in range(4, 6):
-            run("v", lambda k=k: g.vector.tensor_reduce(T.tot[:, k:k + 1], T.eq[:, 384 * k:384 * k + 384], AxisListType.X, A.add),
-                [col("tot", k)], [cols("eq", 0, 1, k=AZ[2 * k:2 * k + 2])])
-        ts(a("nk"), cols("tot", 0, 6, k=AZ[:6]), 2.5, A.is_ge)
+        ts(a("LC"), a("CA", k=AZ[:6]), 48.0, A.add, 0.5, A.mult)
+        ts(both("PO", 1), both("RR", 1), 32767, A.bitwise_and)
+        tt(a("MK"), ind(a("RK", k="az"), a("LC")), a("KC"), A.is_equal)
+        if t < 2:
+            ts(l24("LP", 1), po(0, 1), 0.25, A.mult)
+        else:
+            ts(a("ya"), a("PO", k="abcd"), 2, A.arith_shift_right)
         for w in range(2):
-            tt(cols("tk", 6 * w, 6 * w + 6, k=str(w)), a("nk"), cols("dumL", 6 * w, 6 * w + 6), A.mult)
-        tt(a("Lq"), a("Lf"), a("tk", k="01"), A.max)
-        cp(cols("LE", 0, 12, k="0"), a("Lq"))
-        cp(cols("LE", 12, 18, k="1"), cols("Lq", 0, 6))
-        le0, le1 = cols("LE", 0, 12, k="0"), cols("LE", 6, 18, k="01")
-
-        def put(win, src):
-            run("v", lambda: g.vector.tensor_copy(win[0].indirect(le1[0]), src[0]), [win], [src, le1])
+            tt(cols("MV", 96 * w, 96 * w + 96, k=str(w)), ind(a("W%d" % (w + 1), k="az"), a("LC")), a("MK"), A.mult)
+            mm(cols("PC", 96 * w, 96 * w + 96), a("BF"), cols("MV", 96 * w, 96 * w + 96, k=str(w)))
+        mm(cols("PD", 0, 192), a("BF"), a("MV", k="01"), False, True)
+        cp(l24("LK", 1), cols("PH", 24, 48))
+        addw(0)
+        cp(a("RU"), cols("PC", 0, 192))
+        scan(a("LS"), a("DA"), cols("PD", 0, 192), A.max, A.min)
+        pull(1)
+        addw(1)
+        if t == 0:
+            sendx(2)
+        cp(cols("LE0", 0, 6, k="a"), cols("LS", 96 + 15, 192, step=16))
+        cp(cols("LE0", 6, 12, k="b"), cols("LS", 15, 96, step=16))
+        le0 = a("LE0", k="ab")
         if t < 2:
             act(a("gn"), ind(NX, le0))
-            cp(a("gx"), ind(XN, le0))
+            act(a("gx"), ind(XN, le0))
+        else:
+            act(a("g32"), ind(a("N32", k="xyab"), le0))
+        for e in range(12):
+            ts(cols("EQ", 192 * e, 192 * e + 192, k=AZ[e]), a("RU"), cols("LS", 16 * e + 15, 16 * e + 16), A.is_equal)
+            for w in range(2):
+                mm(cols("PE", 0, 96), a("BK"), cols("EQ", 192 * e + 96 * w, 192 * e + 96 * w + 96, k=AZ[e]), False, e == 11 and w == 1)
+        for w in range(2):
+            scan(cols("QQ", 96 * w, 96 * w + 96, k=str(w)), cols("DB", 96 * w, 96 * w + 96), cols("PE", 0, 96), A.max, A.min)
+        tt(a("LQ"), cols("LS", 15, 192, step=16), cols("QQ", 15, 192, k="01", step=16), A.max)
+        if t == 2:
+            tt(cols("cd", 0, 48), cols("ya", 0, 48), cols("ya", 48, 96), A.min)
+        cp(a("LE1"), a("LQ"))
+        if t == 2:
+            tt(cols("cx", 0, 48), cols("ya", 0, 48), cols("ya", 48, 96), A.max)
+
+        def put(win, src):
+            run("v", lambda: g.vector.tensor_copy(win[0].indirect(T.LE1[:]), src[0]), [win], [src, a("LE1")])
+        if t < 2:
             put(NX, a("gn"))
             put(XN, a("gx"))
             if t == 1:
-                n8 = lambda nm, r, lo, hi: (T[nm][r:128:16, lo:hi], NX[1] if nm == "NX" else [nm])
-                dma("g", n8("N32", 0, 0, W), n8("NX", 0, 0, W))
-                dma("g", n8("N32", 0, W, PL), n8("NX", 7, W, PL))
-                dma("g", n8("N32", 0, 0, PL), n8("NX", 1, 0, PL), accum_op=A.add, max_dma_last_dim=4096)
+                for r in range(2):
+                    for s in range(2):
+                        dma("g", cols("NC", 192 * s, 192 * s + 192, k=str(s)), rows("NX", r, at(s), at(s) + W, NX[1]), **({"accum_op": A.add} if r else {}))
+                act(a("NC2"), a("NC", k="01"), scale=KK / 4, bias=-64.0)
+                for s in range(2):
+                    deps("y", [], ["N32x", "N32y"])
+                    dma("y", rows("N32", 0, at(s), at(s) + W, ["N32" + "ab"[s]]), cols("NC2", 192 * s, 192 * s + 192))
         else:
-            cp(a("g32"), ind(a("N32"), le0))
-            put(a("N32"), a("g32"))
-            dma("y", ext(T.yn[:]), a("N32", slice(0, 128, 16), slice(0, PL)))
-            dma("s", ext(T.yw[:]), a("WW", k="01"))
-            cp(lo_, a("LP", k="01"))
-            cp(hi_, a("LO", k="01"))
-            tt(cols("yco", 0, 48, k="0"), lo_, hi_, A.min)
-            tt(a("cd"), lo_, hi_, A.max)
-            ts(cols("yco", 48, 96, k="1"), a("cd"), -3072.0, A.add)
+            put(a("N32", k="xyab"), a("g32"))
+            for s in range(2):
+                dma("ys"[s], ext(T.yn[:, W * s:W * s + W]), rows("N32", 0, at(s), at(s) + W, ["N32a"]))
+            ts(cols("yco", 0, 48, k="0"), a("cd"), -float(at(0)), A.add)
+            ts(cols("yco", 48, 96, k="1"), a("cx"), -float(at(1)), A.add)
             dma("s", ext(T.yc[:]), a("yco", k="01"))
     for sem, val in total.items():
         need("g", sem, val)

@@ -8,17 +8,17 @@ for names, shape, dtype in (
         ("XS XF0 XF1 XF2", [W], B2), ("XN NX", [PL], B2), ("INFO", [OFF + W], B2), ("N32", [PL], F4), ("WW DD", [K], F4),
         ("NB", [2, 2, 96], I4), ("NF", [2, 6, 2, 16], F4), ("FT", [2, 6, 32], F4), ("LX", [384], U2),
         ("memc froc", [192], I4), ("curc ya", [96], I4), ("typc c1 cd cx cp cq cr m2 ct cf tt_ tu tf ta lr", [48], I4), ("yco", [96], F4),
-        ("HI LO B1 MB FH FL hb", [192], B2), ("GN", [2 * K], B2), ("RA", [K], B2),
+        ("HI LO B1 MB FH FL hb", [192], B2), ("GN", [2 * K], B2), ("RA YG", [K], B2),
         ("RR PO", [2, 48], I4), ("YY", [48], F4), ("LP LR LK", [48], U2),
         ("pc", [4], I4), ("pf", [8], F4), ("xr", [144], F4), ("OH co", [32], F4), ("WB WX WF WM", [144], B2),
-        ("kr kg", [128], F4), ("BL BN BK UW U1 I128", [128], B2), ("BF", [128], F4),
+        ("kr kg", [128], F4), ("BL BN BK UW U1 I128 ZR", [128], B2), ("BF NI", [128], F4),
         ("KC MK", [96], F4), ("kb kb0 CA", [6], F4), ("k16 CD1", [192], B2), ("CD2", [96], B2), ("DA DB D0 D1 D2", [192], F4),
         ("on wt cs", [48], B2), ("SG", [288], F4), ("LC", [6], U2), ("RK", [64], F4), ("W1 W2", [64], I4),
         ("MV LS QQ g32", [192], F4), ("RU", [192], U2), ("EQ", [2304], B2), ("LQ", [12], F4), ("LE0 LE1", [12], U2),
         ("gx gn", [192], B2), ("NC NC2", [384], F4)):
     for nm in names.split():
         SCRATCH[nm] = ("sbuf", [128] + shape, dtype)
-PSUMS = ("F0", "F1", "PA", "PB", "PC", "PD", "PE", "PH")
+PSUMS = ("F0", "F1", "PA", "PH", "PD", "PE", "Y0", "Y1")
 for nm in PSUMS:
     SCRATCH[nm] = ("psum", [128, 512], F4)
 SEMAPHORES = ["qv", "qp", "qs", "qg", "xl", "xa0", "xa1", "xa2"] + ["e%d" % k for k in range(14)] + ["d%d" % k for k in range(30)]
@@ -91,7 +91,7 @@ def rank_program(g, core, T, topo):
         eng[q].dma_start(out[0], in_[0], **kw).then_inc(T.sem[sem], 16)
         done(q, sem, 16, in_[1], out[1])
 
-    def tt(out, i0, i1, op, more=()):
+    def tt(out, i0, i1, op):
         run("v", lambda: g.vector.tensor_tensor(out[0], i0[0], i1[0], op), [out], [i0, i1])
 
     def ts(out, i0, s1, op0, s2=None, op1=None):
@@ -140,8 +140,10 @@ def rank_program(g, core, T, topo):
     col = lambda nm, j: a(nm, al, slice(j, j + 1), k=AZ[j])
     half = lambda nm, b: cols(nm, 384 * b, 384 * b + 384, k=str(b))
     l24 = lambda nm, b: cols(nm, 24 * b, 24 * b + 24, k=str(b))
+    w96 = lambda nm, w, k="": cols(nm, 96 * w, 96 * w + 96, k=k)
     rows = lambda nm, r, lo, hi, k: (T[nm][r:128:16, lo:hi], k)
     at = lambda s: OFF + TY * s
+    skip = lambda: None
 
     def tolist(out, wts, buf, lo, hi, k, start=True, stop=True):
         for r in range(16):
@@ -179,41 +181,35 @@ def rank_program(g, core, T, topo):
               "bi0": [(9, 1 / 16), (8, -32768 / KK)], "bi1": [(9, 1 / 16), (8, -49152 / KK)],
               "wx": [(0, 1.0), (1, 1.0), (4, 1.0), (5, 1.0), (8, -1.0), (9, -136.0)], "wf": [(6, 1 / KK), (7, 1 / KK)], "wm": [(3, 1 / KK)]}
     co, made = {}, {}
-    for step in range(6):
+    for term in range(6):
         for nm, terms in chains.items():
-            if step < len(terms):
-                key = tuple(terms[:step + 1])
+            if term < len(terms):
+                key = tuple(terms[:term + 1])
                 if key not in made:
                     made[key] = col("co", nco[0])
                     nco[0] += 1
-                    act(made[key], cols("OH", terms[step][0], terms[step][0] + 1), scale=terms[step][1], bias=co.get(nm))
+                    act(made[key], cols("OH", terms[term][0], terms[term][0] + 1), scale=terms[term][1], bias=co.get(nm))
                 co[nm] = made[key]
     for nm, w in (("WX", "wx"), ("WF", "wf"), ("WM", "wm")):
         act(a(nm), a("WB"), scale=co[w])
 
-    def nextlist(s):
+    def nextlist(s, gaps):
         for h in range(2):
             cp(a("NF", al, s, al, h, al, k=AZ[2 * s + h]), a("NB", al, s, h, al, k=AZ[2 * s + h]))
+        gaps[0]()
         run("v", lambda: g.vector.transpose(T.FT[:, s], T.NF[:, s]), [a("FT", k=str(s))], [a("NF", k=AZ[2 * s:2 * s + 2])])
+        gaps[1]()
         for b in range(6):
             cp(cols("LX", 192 * s + b, 192 * s + 192, k=AZ[6 * s + b], step=6), a("FT", al, s, b, al, k=str(s)))
+        gaps[2]()
     ts(a("B1"), a("memc"), 2.0, A.is_ge)
     cp(a("MB"), a("memc"))
     for r, nm in ((2, "B1"), (3, "MB"), (4, "B1"), (5, "MB")):
         put_info("y", r, nm)
-    nextlist(0)
-    nextlist(1)
     c0 = cols("curc", 0, 48)
-    ts(a("c1"), cols("curc", 48, 96), float(TY), A.add)
-    ts(a("m2"), a("typc"), -1.0, A.mult, 2.0, A.add)
-    tt(a("cd"), a("c1"), c0, A.subtract)
-    tt(a("cx"), a("cd"), a("typc"), A.mult)
-    tt(a("cq"), a("c1"), a("cx"), A.subtract)
-    tt(a("cp"), c0, a("cx"), A.add)
-    ts(a("cr"), a("cq"), TY - 1, A.bitwise_and)
-    ts(a("LP", k="01"), a("cp"), float(OFF), A.add)
-    ts(a("LR", k="01"), a("cr"), float(OFF), A.add)
-    ts(a("cq"), a("cq"), 4.0, A.mult, 4.0 * OFF, A.add)
+    nextlist(0, [lambda: ts(a("c1"), cols("curc", 48, 96), float(TY), A.add), lambda: tt(a("cd"), a("c1"), c0, A.subtract),
+                 lambda: tt(a("cx"), a("cd"), a("typc"), A.mult)])
+    nextlist(1, [lambda: tt(a("cp"), c0, a("cx"), A.add), lambda: ts(a("LP", k="01"), a("cp"), float(OFF), A.add), skip])
 
     def sendx(t):
         deps("g", ["XS"], [])
@@ -236,17 +232,13 @@ def rank_program(g, core, T, topo):
         for k, (lo, hi) in zip("xyz", ((0, OFF), (OFF + W, at(1)), (DUM, PL))):
             iota(cols(nm, lo, hi, k=k), [[0, hi - lo]], 0, 0)
 
-    lx = lambda s, lo, hi: cols("LX", 192 * s + lo, 192 * s + hi, k=AZ[6 * s:6 * s + 6])
-    piece = lambda nm, s, lo, hi, k: cols(nm, at(s) + 16 * lo, at(s) + 16 * hi, k=k)
+    lx = lambda s: cols("LX", 192 * s, 192 * s + 192, k=AZ[6 * s:6 * s + 6])
+    piece = lambda nm, s: cols(nm, at(s), at(s) + W, k="ab"[s])
     info = lambda lo: cols("INFO", lo, OFF + W, k=AZ[:8])
-    act(piece("XN", 0, 0, 192, "a"), ind(a("XS"), lx(0, 0, 192)))
-    cp(piece("XN", 1, 0, 192, "b"), ind(a("XS"), lx(1, 0, 192)))
-    act(a("RA", k="01"), ind(info(0), a("LR", k="01")))
-    for b in range(2):
-        tolist(cols("PH", 24 * b, 24 * b + 24), "WM", "RA", 384 * b, 384 * b + 384, str(b))
-    ts(piece("NX", 0, 0, 192, "a"), ind(info(OFF), lx(0, 0, 192)), co["sc0"], A.mult, co["bi0"], A.add)
-    act(piece("NX", 1, 0, 192, "b"), ind(info(OFF), lx(1, 0, 192)), scale=co["sc1"], bias=co["bi1"])
-    tt(a("ct"), cols("PH", 0, 48), a("m2"), A.mult)
+    act(piece("XN", 0), ind(a("XS"), lx(0)))
+    cp(piece("XN", 1), ind(a("XS"), lx(1)))
+    ts(piece("NX", 0), ind(info(OFF), lx(0)), co["sc0"], A.mult, co["bi0"], A.add)
+    act(piece("NX", 1), ind(info(OFF), lx(1)), scale=co["sc1"], bias=co["bi1"])
     XN, NX = a("XN", k="abxyz"), a("NX", k="abxyz")
 
     iota(a("KC"), [[1, 96]], 1025, 0)
@@ -262,12 +254,13 @@ def rank_program(g, core, T, topo):
         tt(a("FL"), a("froc"), a("FH"), A.subtract)
         put_info("y", 6, "FH")
         put_info("y", 7, "FL")
-    late_v = [lambda: cp(a("FH"), a("froc")), fro_lo, lambda: ts(a("BL"), a("kg"), gi, A.is_equal), lambda: ts(a("I128"), a("kr"), p0, A.is_equal),
+    late_v = [lambda: ts(a("I128"), a("kr"), p0, A.is_equal), lambda: ts(a("BL"), a("kg"), gi, A.is_equal), lambda: cp(a("FH"), a("froc")), fro_lo,
               lambda: ts(a("CD1"), a("k16"), pm, A.not_equal, 65536.0, A.mult), lambda: fill(a("on"), 1.0),
               lambda: fill(cols("RK", 48, 64, k="z"), 0.0), lambda: fill(cols("W1", 48, 64, k="z"), 0), lambda: fill(cols("W2", 48, 64, k="z"), 0)]
-    late_s = [lambda: act(a("BN"), a("BL"), scale=-1.0), lambda: act(a("BF"), a("BL")), lambda: act(a("BK"), a("BL"), scale=16384.0),
+    late_s = [lambda: act(a("NI"), a("I128"), scale=-1.0), lambda: act(a("ZR"), a("I128"), scale=0.0), lambda: act(a("BN"), a("BL"), scale=-1.0),
+              lambda: act(a("BF"), a("BL")), lambda: act(a("BK"), a("BL"), scale=16384.0),
               lambda: act(a("CD2"), cols("CD1", 0, 96), scale=1.625, bias=-40960.0), lambda: act(col("pf", 5), pm, bias=0.5),
-              lambda: act(a("kb"), a("kb0"), bias=col("pf", 5)), lambda: act(a("DB"), a("D2"), bias=pm)]
+              lambda: act(a("DB"), a("D2"), bias=pm), lambda: act(a("kb"), a("kb0"), bias=col("pf", 5))]
 
     def late_g():
         asel(a("U1"), a("BN"), [[-1, 128]], A.is_gt, 0.0, 0, 1)
@@ -277,133 +270,179 @@ def rank_program(g, core, T, topo):
     po = lambda j, b: a("PO", al, j, slice(24 * b, 24 * b + 24), k="abcd"[2 * j + b])
     both = lambda nm, b: a(nm, al, al, slice(24 * b, 24 * b + 24), k="ac" if b == 0 else "bd")
 
-    def gather(b):
+    def gather(b, first=False):
         Fb, c = "F%d" % b, K * b
         tt(cols("GN", c, c + 384, k="ab"[b]), ind(XN, l24("LP", b)), half("WW", b), A.is_ge)
         act(cols("GN", c + 384, c + K, k="cd"[b]), ind(NX, l24("LP", b)))
-        tolist(cols(Fb, 0, 48), "WB", "GN", c, c + K, ("ac", "bd")[b], stop=False)
-        tolist(cols(Fb, 0, 24), "WX", "GN", c + 384, c + K, "cd"[b], start=False)
+        if first:
+            tolist(cols(Fb, 24, 48), "WB", "GN", c + 384, c + K, "cd"[b])
+            tolist(cols(Fb, 0, 24), "WX", "GN", c + 384, c + K, "cd"[b], stop=False)
+            tolist(cols(Fb, 0, 24), "WB", "GN", c, c + 384, "ab"[b], start=False)
+        else:
+            tolist(cols(Fb, 0, 48), "WB", "GN", c, c + K, ("ac", "bd")[b], stop=False)
+            tolist(cols(Fb, 0, 24), "WX", "GN", c + 384, c + K, "cd"[b], start=False)
 
-    def step(b, cast=True, gaps=()):
-        gaps = list(gaps)
-        gap = lambda: gaps.pop(0)() if gaps else None
+    def choose(b):
         Fb = "F%d" % b
         tt(l24("YY", b), cols(Fb, 24, 48), po(1, b), A.max)
         tt(rr(1, b), cols(Fb, 0, 24), po(1, b), A.max)
         tt(rr(0, b), cols(Fb, 0, 24), l24("YY", b), A.min)
-        gap()
+
+    def step(b, cast=True, gaps=()):
+        gaps = list(gaps) + [skip] * 3
+        choose(b)
+        gaps[0]()
         ts(both("PO", b), both("RR", b), 32767, A.bitwise_and)
-        gap()
+        gaps[1]()
         if cast:
             ts(l24("LP", b), po(0, b), 0.25, A.mult)
-        gap()
+        gaps[2]()
 
-    def reclist(b):
-        ts(l24("lr", b), rr(0, b), 16383, A.bitwise_and)
+    same = lambda b: tt(l24("cr", b), po(1, b), l24("cq", b), A.is_equal)
+    flag = lambda b: tt(l24("cr", b), l24("cr", b), l24("cf", b), A.mult)
+    addf = lambda b: tt(po(1, b), po(1, b), l24("cr", b), A.add)
+    late_v += [lambda: tt(a("ct"), cols("PH", 0, 48), a("m2"), A.mult), skip,
+               lambda: ts(a("cf", k="01"), a("ct"), 1, A.arith_shift_right, 1, A.bitwise_and),
+               skip, lambda: same(0), lambda: flag(0), lambda: addf(0), lambda: same(1), lambda: flag(1)]
 
-    def foreign(b):
-        ts(l24("LR", b), l24("lr", b), 0.25, A.mult)
-        act(half("RA", b), ind(info(0), l24("LR", b)))
+    reclist = lambda b: ts(l24("lr", b), rr(0, b), 16383, A.bitwise_and)
+    reccast = lambda b: ts(l24("LR", b), l24("lr", b), 0.25, A.mult)
+    foreign = lambda b: tolist(cols("PH", 24 * b, 24 * b + 24), "WF", "RA", 384 * b, 384 * b + 384, str(b))
+    forcast = lambda b: cp(l24("LK", b), cols("PH", 24 * b, 24 * b + 24))
 
-    def foreign2(b):
-        tolist(cols("PH", 24 * b, 24 * b + 24), "WF", "RA", 384 * b, 384 * b + 384, str(b))
+    def minus_w(n):
+        b, lo = n % 2, 96 * (n // 2)
+        if lo == 0:
+            mm(cols("Y%d" % b, 0, 384), a("ZR"), cols("XS", 0, 384), True, False)
+        mm(cols("Y%d" % b, lo, lo + 96), a("NI"), cols("WW", 384 * b + lo, 384 * b + lo + 96, k=str(b)), False, False)
+
+    def next_out(part):
+        if part == 0:
+            for r in range(2):
+                for s in range(2):
+                    dma("g", cols("NC", 192 * s, 192 * s + 192, k=str(s)), rows("NX", r, at(s), at(s) + W, NX[1]), **({"accum_op": A.add} if r else {}))
+        else:
+            act(a("NC2"), a("NC", k="01"), scale=KK / 4, bias=-64.0)
+            for s in range(2):
+                deps("y", [], ["N32x", "N32y"])
+                dma("y", rows("N32", 0, at(s), at(s) + W, ["N32" + "ab"[s]]), cols("NC2", 192 * s, 192 * s + 192))
 
     for t in range(3):
+        gather(0, t > 0)
+        if t == 0:
+            tt(a("c1"), a("c1"), a("cx"), A.subtract)
+        else:
+            tt(half("WW", 1), cols("Y1", 0, 384), half("WW", 1), A.add)
+        gather(1)
         if t == 2:
             dma("y", ext(T.yw[:], ["yw"]), a("WW", k="01"))
-        gather(0)
         if t == 0:
-            ts(a("cf"), a("ct"), 1, A.arith_shift_right, 1, A.bitwise_and)
-        gather(1)
-        if t == 0:
-            tt(a("PO", al, 1, al, k="cd"), a("cq"), a("cf"), A.add)
-        for q in range(3):
+            ts(a("cr", k="01"), a("c1"), TY - 1, A.bitwise_and)
+            ts(a("PO", al, 1, al, k="cd"), a("c1"), 4.0, A.mult, 4.0 * OFF, A.add)
+            ts(a("LR", k="01"), a("cr", k="01"), float(OFF), A.add)
+            ts(a("cq", k="01"), a("c1"), 4.0, A.mult, 4.0 * OFF, A.add)
+            ts(a("m2"), a("typc"), -1.0, A.mult, 2.0, A.add)
             for b in range(2):
-                n = 2 * q + b
-                step(b, gaps=late_v[2 * n:2 * n + 2] if t == 0 else ())
-                gather(b)
-                if t == 0 and n >= 2:
-                    for fn in late_s[2 * n - 4:2 * n - 2]:
-                        fn()
-                    if n == 2:
-                        late_g()
-                        sendx(1)
+                act(half("RA", b), ind(info(0), l24("LR", b)))
+        for n in range(6):
+            step(n % 2, gaps=late_v[3 * n:3 * n + 3] if t == 0 else ())
+            gather(n % 2)
+            if t == 0:
+                if n == 0:
+                    tolist(cols("PH", 0, 48), "WM", "RA", 0, K, "01")
+                for fn in late_s[2 * n - 2:2 * n] if n else ():
+                    fn()
+                if n == 2:
+                    late_g()
+                    sendx(1)
+            for k in (((), (0,), (1,), (2, 3), (4, 5), (6, 7)) if t == 0 else ((0,), (1,), (2,), (3, 4), (5, 6), (7,)))[n]:
+                minus_w(k)
+            if t == 2 and n == 5:
+                next_out(1)
         if t == 1:
             n32(1)
         r0, r1 = a("RR", al, 0, al, k="ab"), a("RR", al, 1, al, k="cd")
-        step(0, t < 2, [lambda: reclist(0), lambda: foreign(0)])
-        foreign2(0)
+        step(0, t < 2, [lambda: reclist(0), lambda: reccast(0), (lambda: addf(1)) if t == 0 else skip])
+        act(half("RA", 0), ind(info(0), l24("LR", 0)))
         mm(cols("PD", 0, 192), a("I128"), a("CD1"), True, False)
+        foreign(0)
         mm(cols("PE", 0, 96), a("I128"), a("CD2"), True, False)
-        Fb = "F1"
-        tt(l24("YY", 1), cols(Fb, 24, 48), po(1, 1), A.max)
-        tt(rr(1, 1), cols(Fb, 0, 24), po(1, 1), A.max)
-        tt(rr(0, 1), cols(Fb, 0, 24), l24("YY", 1), A.min)
-        ts(cols("W2", 0, 48, k="a"), r1, 32767, A.bitwise_and, 2, A.arith_shift_right)
-        reclist(1)
-        tt(a("tt_"), r0, r1, A.subtract)
-        foreign(1)
-        ts(a("tf"), r0, 1, A.bitwise_and)
-        ts(a("tu"), a("tt_"), 16380, A.bitwise_and)
-        ts(a("ta"), r0, 16384.0, A.add)
-        tt(a("wt"), a("tu"), a("tf"), A.min)
-        ts(cols("W1", 0, 48, k="a"), a("ta"), 32767, A.bitwise_and, 2, A.arith_shift_right)
-        scan(a("cs"), a("on"), a("wt"), A.mult, A.add)
-        cp(l24("LK", 0), cols("PH", 0, 24))
-        mm(cols("PA", 0, 48), a("BL"), a("cs"))
-        mm(cols("PB", 0, 48), a("UW"), a("wt"), True, False)
-        mm(cols("PB", 0, 48), a("BL"), a("cs"), False, True)
-        foreign2(1)
-        for k in range(6):
-            act(cols("SG", 48 * k, 48 * k + 48, k=AZ[k]), cols("PA", 0, 48), scale=-1.0, bias=cols("kb", k, k + 1), acc=col("CA", k), fn=F.Sign)
-        cp(cols("RK", 0, 48, k="a"), cols("PB", 0, 48))
 
         def pull(b):
-            tt(half("DD", b), ind(a("XF%d" % t), l24("LK", b)), half("WW", b), A.subtract)
+            act(half("YG", b), ind(a("XF%d" % t), l24("LK", b)))
+            mm(cols("Y%d" % b, 0, 384), a("I128"), half("YG", b), False, True)
 
         def addw(b):
-            ts(half("DD", b), half("DD", b), 8.0, A.min, -8.0, A.max)
+            ts(half("DD", b), cols("Y%d" % b, 0, 384), 8.0, A.min, -8.0, A.max)
             dma("g", half("WW", b) if t < 2 else ext(T.yw[:, 384 * b:384 * b + 384], ["yw"] if b == 0 else ["yw1"]), half("DD", b), accum_op=A.add)
+        choose(1)
+        ts(cols("W2", 0, 48, k="a"), r1, 32767, A.bitwise_and, 2, A.arith_shift_right)
+        tt(a("tt_"), r0, r1, A.subtract)
+        ts(a("tf"), r0, 1, A.bitwise_and)
+        ts(a("tu"), a("tt_"), 16380, A.bitwise_and)
+        reclist(1)
+        tt(a("wt"), a("tu"), a("tf"), A.min)
+        reccast(1)
+        scan(a("cs"), a("on"), a("wt"), A.mult, A.add)
+        forcast(0)
+        mm(cols("PA", 0, 48), a("BL"), a("cs"))
+        mm(cols("PH", 64, 112), a("UW"), a("wt"), True, False)
+        mm(cols("PH", 64, 112), a("BL"), a("cs"), False, True)
+        for k in range(6):
+            act(cols("SG", 48 * k, 48 * k + 48, k=AZ[k]), cols("PA", 0, 48), scale=-1.0, bias=cols("kb", k, k + 1), acc=col("CA", k), fn=F.Sign)
+        cp(half("RA", 1), ind(info(0), l24("LR", 1)))
+        cp(cols("RK", 0, 48, k="a"), cols("PH", 64, 112))
+        ts(a("ta"), r0, 16384.0, A.add)
+        foreign(1)
         pull(0)
         ts(a("LC"), a("CA", k=AZ[:6]), 48.0, A.add, 0.5, A.mult)
-        ts(both("PO", 1), both("RR", 1), 32767, A.bitwise_and)
+        ts(cols("W1", 0, 48, k="a"), a("ta"), 32767, A.bitwise_and, 2, A.arith_shift_right)
         tt(a("MK"), ind(a("RK", k="az"), a("LC")), a("KC"), A.is_equal)
+        ts(both("PO", 1), both("RR", 1), 32767, A.bitwise_and)
+        for w in range(2):
+            tt(w96("MV", w, str(w)), ind(a("W%d" % (w + 1), k="az"), a("LC")), a("MK"), A.mult)
+            mm(w96("PA", w), a("BF"), w96("MV", w, str(w)))
+            mm(w96("PD", w), a("BF"), w96("MV", w, str(w)), False, w == 1)
+        forcast(1)
+        addw(0)
+        cp(a("RU"), cols("PA", 0, 192))
+        scan(a("LS"), a("DA"), cols("PD", 0, 192), A.max, A.min)
+        pull(1)
         if t < 2:
             ts(l24("LP", 1), po(0, 1), 0.25, A.mult)
         else:
             ts(a("ya"), a("PO", k="abcd"), 2, A.arith_shift_right)
-        for w in range(2):
-            tt(cols("MV", 96 * w, 96 * w + 96, k=str(w)), ind(a("W%d" % (w + 1), k="az"), a("LC")), a("MK"), A.mult)
-            mm(cols("PC", 96 * w, 96 * w + 96), a("BF"), cols("MV", 96 * w, 96 * w + 96, k=str(w)))
-        mm(cols("PD", 0, 192), a("BF"), a("MV", k="01"), False, True)
-        cp(l24("LK", 1), cols("PH", 24, 48))
-        addw(0)
-        cp(a("RU"), cols("PC", 0, 192))
-        scan(a("LS"), a("DA"), cols("PD", 0, 192), A.max, A.min)
-        pull(1)
-        addw(1)
-        if t == 0:
-            sendx(2)
-        cp(cols("LE0", 0, 6, k="a"), cols("LS", 96 + 15, 192, step=16))
-        cp(cols("LE0", 6, 12, k="b"), cols("LS", 15, 96, step=16))
-        le0 = a("LE0", k="ab")
-        if t < 2:
-            act(a("gn"), ind(NX, le0))
-            act(a("gx"), ind(XN, le0))
-        else:
-            act(a("g32"), ind(a("N32", k="xyab"), le0))
         for e in range(12):
             ts(cols("EQ", 192 * e, 192 * e + 192, k=AZ[e]), a("RU"), cols("LS", 16 * e + 15, 16 * e + 16), A.is_equal)
             for w in range(2):
                 mm(cols("PE", 0, 96), a("BK"), cols("EQ", 192 * e + 96 * w, 192 * e + 96 * w + 96, k=AZ[e]), False, e == 11 and w == 1)
+            if e == 0:
+                cp(cols("LE0", 0, 6, k="a"), cols("LS", 96 + 15, 192, step=16))
+                cp(cols("LE0", 6, 12, k="b"), cols("LS", 15, 96, step=16))
+                le0 = a("LE0", k="ab")
+                if t < 2:
+                    act(a("gn"), ind(NX, le0))
+                    act(a("gx"), ind(XN, le0))
+                else:
+                    act(a("g32"), ind(a("N32", k="xyab"), le0))
+            if e == 3 and t == 2:
+                addw(1)
+        if t < 2:
+            ts(cols("Y1", 0, 384), cols("Y1", 0, 384), 8.0, A.min, -8.0, A.max)
+        if t == 0:
+            sendx(2)
+        if t == 2:
+            tt(a("cd"), cols("ya", 0, 48), cols("ya", 48, 96), A.min)
+            tt(a("cx"), cols("ya", 0, 48), cols("ya", 48, 96), A.max)
         for w in range(2):
-            scan(cols("QQ", 96 * w, 96 * w + 96, k=str(w)), cols("DB", 96 * w, 96 * w + 96), cols("PE", 0, 96), A.max, A.min)
+            scan(w96("QQ", w, str(w)), w96("DB", w), cols("PE", 0, 96), A.max, A.min)
         tt(a("LQ"), cols("LS", 15, 192, step=16), cols("QQ", 15, 192, k="01", step=16), A.max)
         if t == 2:
-            tt(cols("cd", 0, 48), cols("ya", 0, 48), cols("ya", 48, 96), A.min)
+            ts(cols("yco", 0, 48, k="0"), a("cd"), -float(at(0)), A.add)
         cp(a("LE1"), a("LQ"))
         if t == 2:
-            tt(cols("cx", 0, 48), cols("ya", 0, 48), cols("ya", 48, 96), A.max)
+            ts(cols("yco", 48, 96, k="1"), a("cx"), -float(at(1)), A.add)
+            dma("s", ext(T.yc[:]), a("yco", k="01"))
 
         def put(win, src):
             run("v", lambda: g.vector.tensor_copy(win[0].indirect(T.LE1[:]), src[0]), [win], [src, a("LE1")])
@@ -411,19 +450,10 @@ def rank_program(g, core, T, topo):
             put(NX, a("gn"))
             put(XN, a("gx"))
             if t == 1:
-                for r in range(2):
-                    for s in range(2):
-                        dma("g", cols("NC", 192 * s, 192 * s + 192, k=str(s)), rows("NX", r, at(s), at(s) + W, NX[1]), **({"accum_op": A.add} if r else {}))
-                act(a("NC2"), a("NC", k="01"), scale=KK / 4, bias=-64.0)
-                for s in range(2):
-                    deps("y", [], ["N32x", "N32y"])
-                    dma("y", rows("N32", 0, at(s), at(s) + W, ["N32" + "ab"[s]]), cols("NC2", 192 * s, 192 * s + 192))
+                next_out(0)
         else:
             put(a("N32", k="xyab"), a("g32"))
             for s in range(2):
                 dma("ys"[s], ext(T.yn[:, W * s:W * s + W]), rows("N32", 0, at(s), at(s) + W, ["N32a"]))
-            ts(cols("yco", 0, 48, k="0"), a("cd"), -float(at(0)), A.add)
-            ts(cols("yco", 48, 96, k="1"), a("cx"), -float(at(1)), A.add)
-            dma("s", ext(T.yc[:]), a("yco", k="01"))
     for sem, val in total.items():
         need("g", sem, val)

@@ -2,23 +2,31 @@ from concourse.mybir import AluOpType as A, ActivationFunctionType as F
 
 W, K, OFF, TY, DUM, PL = 3072, 768, 64, 4096, 7232, 7424
 KK = 262144.0
+RND = 12582912.0
+CUT = (0, 24, 48)
+ALL = "012"[:len(CUT) - 1]
+HEAD, TAIL = ALL[:-1], ALL[-1]
+CYCLE = "r0 o0 p0 r1 m0 o1 p1 c0 m1 g0 c1 h0 G1"
+FINAL = "r0 o0 p0 d0 r1 R0 o1 p1 d1 C0 m0"
+SPLIT = 10
+SHIFT = 384
 F4, B2, I4, U2 = "float32", "bfloat16", "int32", "uint16"
 SCRATCH = {}
 for names, shape, dtype in (
-        ("XS XF0 XF1 XF2", [W], B2), ("XN NX", [PL], B2), ("INFO", [OFF + W], B2), ("N32", [PL], F4), ("WW DD", [K], F4),
-        ("NB", [2, 2, 96], I4), ("NF", [2, 6, 2, 16], F4), ("FT", [2, 6, 32], F4), ("LX", [384], U2),
-        ("memc froc", [192], I4), ("curc ya", [96], I4), ("typc c1 cd cx cp cq cr m2 ct cf tt_ tu tf ta lr", [48], I4), ("yco", [96], F4),
-        ("HI LO B1 MB FH FL hb", [192], B2), ("GN", [2 * K], B2), ("RA YG", [K], B2),
-        ("RR PO", [2, 48], I4), ("YY", [48], F4), ("LP LR LK", [48], U2),
-        ("pc", [4], I4), ("pf", [8], F4), ("xr", [144], F4), ("OH co", [32], F4), ("WB WX WF WM", [144], B2),
-        ("kr kg", [128], F4), ("BL BN BK UW U1 I128 ZR", [128], B2), ("BF NI", [128], F4),
-        ("KC MK", [96], F4), ("kb kb0 CA", [6], F4), ("k16 CD1", [192], B2), ("CD2", [96], B2), ("DA DB D0 D1 D2", [192], F4),
+        ("XS XF0 XF1 XF2", [W], B2), ("XN", [PL], B2), ("NX", [PL], F4), ("INFO", [OFF + W], B2), ("WW", [K], F4),
+        ("NB", [2, 2, 96], I4), ("NF", [2, 6, 2, 16], F4), ("FT", [2, 6, 32], F4), ("LX", [2, 192], U2),
+        ("memc froc m0", [192], I4), ("curc ya", [96], I4), ("typc c1 cd cx cp cq cr m2 ct cf df tu tf ta lr", [48], I4), ("yco", [96], F4),
+        ("HI LO B1 B0 FH FL hb", [192], B2), ("GN0 GN1 GN2", [512, 2], B2), ("RA YG W0", [K], B2),
+        ("RR PO", [2, 48], I4), ("YY", [48], F4), ("ZO XX0 XX1 XX2", [64], F4), ("CK Ca Cb", [64], B2), ("LP LR LK", [48], U2),
+        ("pc", [4], I4), ("pf co", [16], F4), ("WB Wa Wb", [144], B2),
+        ("BL BN BK UW U1 I128 ON O1 NJ M16 Ba", [128], B2), ("BF NI", [128], F4),
+        ("KC MK", [96], F4), ("kb kb0 CA", [6], F4), ("CD0 CD1", [192], B2), ("CD2", [96], B2), ("DA DB D0 D1 D2", [192], F4),
         ("on wt cs", [48], B2), ("SG", [288], F4), ("LC", [6], U2), ("RK", [64], F4), ("W1 W2", [64], I4),
-        ("MV LS QQ g32", [192], F4), ("RU", [192], U2), ("EQ", [2304], B2), ("LQ", [12], F4), ("LE0 LE1", [12], U2),
-        ("gx gn", [192], B2), ("NC NC2", [384], F4)):
+        ("MV LS QQ gn", [192], F4), ("RU", [192], U2), ("EQ", [2304], B2), ("LQ", [12], F4), ("LE0 LE1", [12], U2),
+        ("gx", [192], B2), ("NC NC2 NC3", [384], F4)):
     for nm in names.split():
         SCRATCH[nm] = ("sbuf", [128] + shape, dtype)
-PSUMS = ("F0", "F1", "PA", "PH", "PD", "PE", "Y0", "Y1")
+PSUMS = ("F0", "F1", "F2", "PA", "PD", "PE", "Y0", "Y1")
 for nm in PSUMS:
     SCRATCH[nm] = ("psum", [128, 512], F4)
 SEMAPHORES = ["qv", "qp", "qs", "qg", "xl", "xa0", "xa1", "xa2"] + ["e%d" % k for k in range(14)] + ["d%d" % k for k in range(30)]
@@ -56,7 +64,7 @@ def rank_program(g, core, T, topo):
                 need(q, w[0], w[1])
             if key in PSUMS or key in wr:
                 for s2, (v2, q2) in list(reads.get(key, {}).items()):
-                    if q2 != q or s2[0] in "dex":
+                    if q2 != q or s2[0] in "dex" or key in wr:
                         need(q, s2, v2)
 
     def done(q, sem, val, rd, wr):
@@ -127,89 +135,108 @@ def rank_program(g, core, T, topo):
     def mm(out, lhsT, rhs, start=True, stop=True):
         run("p", lambda: g.tensor.matmul(out[0], lhsT[0], rhs[0], start, stop), [out], [lhsT, rhs])
 
-    def iota(out, pattern, base, cm):
-        kw = {} if out[1][0].startswith("pc") else {"allow_small_or_imprecise_dtypes": True}
+    def iota(out, pattern, base, cm=0, whole=False):
+        kw = {} if whole else {"allow_small_or_imprecise_dtypes": True}
         run("g", lambda: g.iota(out[0], pattern, base, cm, **kw), [out], [])
 
     def asel(out, in_, pattern, op, fill_, base, cm):
         run("g", lambda: g.affine_select(out[0], in_[0], pattern, op, fill_, base, cm), [out], [in_])
 
+    def put(q, win, off, src):
+        dst = win[0].indirect(off[0])
+        if q == "v":
+            run("v", lambda: g.vector.tensor_copy(dst, src[0]), [win], [src, off])
+        else:
+            run("s", lambda: g.scalar.activation(dst, src[0], F.Silu), [win], [src, off])
+
     ext = lambda ap, k=(): (ap, list(k))
     al = slice(None)
     cols = lambda nm, lo, hi, k="", step=1: a(nm, al, slice(lo, hi, step), k=k)
     col = lambda nm, j: a(nm, al, slice(j, j + 1), k=AZ[j])
-    half = lambda nm, b: cols(nm, 384 * b, 384 * b + 384, k=str(b))
-    l24 = lambda nm, b: cols(nm, 24 * b, 24 * b + 24, k=str(b))
+    lo_, hi_ = lambda bs: CUT[int(bs[0])], lambda bs: CUT[int(bs[-1]) + 1]
+    wide = lambda bs: hi_(bs) - lo_(bs)
+    lst = lambda nm, bs: cols(nm, lo_(bs), hi_(bs), k=bs)
+    unit = lambda nm, bs: cols(nm, 16 * lo_(bs), 16 * hi_(bs), k=bs)
     w96 = lambda nm, w, k="": cols(nm, 96 * w, 96 * w + 96, k=k)
     rows = lambda nm, r, lo, hi, k: (T[nm][r:128:16, lo:hi], k)
     at = lambda s: OFF + TY * s
     skip = lambda: None
+    pads = list(zip("xyz", ((0, OFF), (OFF + W, at(1)), (DUM, PL))))
 
-    def tolist(out, wts, buf, lo, hi, k, start=True, stop=True):
-        for r in range(16):
-            mm(out, cols(wts, 15 - r, 143 - r), cols(buf, lo + r, hi, k=k, step=16), start and r == 0, stop and r == 15)
+    def tolist(out, rhs, start=True, rs=range(16)):
+        for r in rs:
+            mm(out, cols("WB", 15 - r, 143 - r), rhs(r), start and r == 0, r == 15)
 
-    for s in range(2):
-        for h in range(2):
-            dma("ys"[s], a("NB", al, s, h, al, k=AZ[2 * s + h]), ext(T.nxt[h:8:2, W * s:W * s + W]))
     dma("y", a("memc"), ext(T.mem[:]))
+    for h in range(2):
+        for s in range(2):
+            dma("sy"[s], a("NB", al, s, h, al, k=AZ[2 * s + h]), ext(T.nxt[h:8:2, W * s:W * s + W]))
     dma("s", a("curc"), ext(T.cur[:]))
     dma("s", a("typc"), ext(T.typ[:]))
-    dma("y", a("XS"), ext(T.x[:]))
-    dma("s", a("froc"), ext(T.fro[:]))
 
-    iota(col("pc", 0), [[0, 1]], 0, 1)
-    iota(a("xr"), [[1, 144]], 0, 0)
-    iota(a("hb"), [[1, 3], [0, 64]], 1, 0)
-    iota(a("LO"), [[0, 3], [1, 64]], 0, 0)
-    fill(a("INFO", k=AZ[:8]), 0.0)
+    iota(col("pc", 0), [[0, 1]], 0, 1, True)
+    iota(a("hb"), [[256, 3], [0, 64]], 0)
+    iota(a("LO"), [[0, 3], [4, 64]], 4 * OFF)
+    fill(cols("INFO", 0, 1024, k="p"), 0.0)
     ts(col("pc", 1), col("pc", 0), 15, A.bitwise_and)
-    ts(col("pc", 2), col("pc", 0), 4, A.arith_shift_right)
-    cp(cols("pf", 0, 3, k="abc"), cols("pc", 0, 3, k="abc"))
-    p0, pm, gi = col("pf", 0), col("pf", 1), col("pf", 2)
-    ts(col("pf", 3), gi, 16.0, A.mult, 15.0, A.add)
-    ts(cols("OH", 0, 16), cols("xr", 0, 16), pm, A.is_equal)
-    ts(a("WB"), a("xr"), col("pf", 3), A.is_equal, KK, A.mult)
-    act(col("pf", 4), pm, scale=3.0)
+    fill(cols("INFO", 1024, 2048, k=AZ[:8]), 0.0)
+    pm = col("pf", 1)
+    cp(pm, col("pc", 1))
+    fill(cols("INFO", 2048, OFF + W, k=AZ[:8]), 0.0)
+    for k, (lo, hi) in pads:
+        act(cols("NX", lo, hi, k=k), cols("INFO", 0, hi - lo, k="p"))
+    act(col("pf", 4), pm, scale=768.0)
+    act(col("pf", 6), pm, bias=-2.5, fn=F.Abs)
+    act(col("pf", 5), pm, bias=0.5)
     act(a("HI"), a("hb"), bias=col("pf", 4))
     put_info = lambda q, r, nm: dma(q, rows("INFO", r, OFF, OFF + W, ["INFO" + AZ[r]]), a(nm))
-    put_info("y", 1, "LO")
-    put_info("s", 0, "HI")
-    nco = [0]
-    chains = {"sc0": [(0, 256 / KK), (1, 4 / KK), (2, 65536 / KK), (4, 1 / KK)],
-              "sc1": [(0, 256 / KK), (1, 4 / KK), (2, -131072 / KK), (4, -2 / KK), (3, 65536 / KK), (5, 1 / KK)],
-              "bi0": [(9, 1 / 16), (8, -32768 / KK)], "bi1": [(9, 1 / 16), (8, -49152 / KK)],
-              "wx": [(0, 1.0), (1, 1.0), (4, 1.0), (5, 1.0), (8, -1.0), (9, -136.0)], "wf": [(6, 1 / KK), (7, 1 / KK)], "wm": [(3, 1 / KK)]}
-    co, made = {}, {}
-    for term in range(6):
-        for nm, terms in chains.items():
-            if term < len(terms):
-                key = tuple(terms[:term + 1])
-                if key not in made:
-                    made[key] = col("co", nco[0])
-                    nco[0] += 1
-                    act(made[key], cols("OH", terms[term][0], terms[term][0] + 1), scale=terms[term][1], bias=co.get(nm))
-                co[nm] = made[key]
-    for nm, w in (("WX", "wx"), ("WF", "wf"), ("WM", "wm")):
-        act(a(nm), a("WB"), scale=co[w])
+    sc0, sc1, bi0, gsc, wf, wm = [col("co", j) for j in range(6)]
+    ts(a("m0"), a("memc"), 1, A.bitwise_and)
+    ts(a("B1"), a("memc"), 2.0, A.is_ge, 65536.0, A.mult)
+    ts(sc0, pm, 3.0, A.is_le)
+    ts(sc1, pm, 2.0, A.is_ge)
+    ts(a("B0"), a("m0"), 65536.0, A.mult)
+    deps("y", [], ["INFOp"])
+    for q, r, nm in (("y", 3, "LO"), ("s", 2, "HI"), ("y", 0, "B1"), ("s", 1, "B1"), ("y", 4, "B0"), ("s", 5, "B0")):
+        put_info(q, r, nm)
+    dma("y", a("XS"), ext(T.x[:]))
+    dma("y", a("W0", k=[b + h for b in ALL for h in "ab"]), ext(T.w0[:]))
+    dma("y", a("froc"), ext(T.fro[:]))
+    act(a("D0"), a("hb"), scale=0.0, bias=65536.0, fn=F.Silu)
 
-    def nextlist(s, gaps):
-        for h in range(2):
-            cp(a("NF", al, s, al, h, al, k=AZ[2 * s + h]), a("NB", al, s, h, al, k=AZ[2 * s + h]))
-        gaps[0]()
-        run("v", lambda: g.vector.transpose(T.FT[:, s], T.NF[:, s]), [a("FT", k=str(s))], [a("NF", k=AZ[2 * s:2 * s + 2])])
-        gaps[1]()
-        for b in range(6):
-            cp(cols("LX", 192 * s + b, 192 * s + 192, k=AZ[6 * s + b], step=6), a("FT", al, s, b, al, k=str(s)))
-        gaps[2]()
-    ts(a("B1"), a("memc"), 2.0, A.is_ge)
-    cp(a("MB"), a("memc"))
-    for r, nm in ((2, "B1"), (3, "MB"), (4, "B1"), (5, "MB")):
-        put_info("y", r, nm)
-    c0 = cols("curc", 0, 48)
-    nextlist(0, [lambda: ts(a("c1"), cols("curc", 48, 96), float(TY), A.add), lambda: tt(a("cd"), a("c1"), c0, A.subtract),
-                 lambda: tt(a("cx"), a("cd"), a("typc"), A.mult)])
-    nextlist(1, [lambda: tt(a("cp"), c0, a("cx"), A.add), lambda: ts(a("LP", k="01"), a("cp"), float(OFF), A.add), skip])
+    cur0, cur1 = cols("curc", 0, 48), cols("curc", 48, 96)
+    for h in range(2):
+        cp(a("NF", al, al, al, h, al, k=str(h)), a("NB", al, al, h, al, k=AZ[h] + AZ[2 + h]))
+    tt(a("cd"), cur1, cur0, A.subtract)
+    ts(a("c1"), a("typc"), float(TY), A.mult, float(OFF), A.add)
+    ts(bi0, pm, 2.0, A.is_equal, 4.0 * TY, A.mult)
+    run("v", lambda: g.vector.transpose(T.FT[:], T.NF[:]), [a("FT")], [a("NF", k="01")])
+    tt(a("cx"), a("cd"), a("typc"), A.mult)
+    tt(a("c1"), a("c1"), cur0, A.add)
+    ts(col("co", 7), pm, 4.0, A.is_equal, 1 / KK / 65536, A.mult)
+    for b in range(6):
+        cp(a("LX", al, al, slice(b, 192, 6), k=AZ[b]), a("FT", al, al, b, al))
+        if b == 1:
+            tt(a("cr"), cur1, a("cx"), A.subtract)
+    ts(col("co", 8), pm, 1.0, A.is_equal, 2 / KK / 65536, A.mult)
+    ts(a("LR", k=ALL), a("cr"), float(OFF), A.add)
+    tt(a("cp"), a("c1"), a("cx"), A.add)
+    ts(col("co", 6), col("pf", 6), 2.0, A.is_lt, 1 / KK, A.mult)
+    tt(wm, col("co", 7), col("co", 8), A.add)
+
+    group = lambda out, in_, tmp, n: (asel(tmp, in_, [[-16, n], [0, 16]], A.is_ge, 0.0, 0, 1), asel(out, tmp, [[16, n], [0, 16]], A.is_ge, 0.0, 15, -1))
+    part = lambda nm, lo, hi, k="": a(nm, slice(lo, hi), al, k=k)
+    iota(a("Wa"), [[0, 144]], int(KK))
+    asel(a("Wb"), a("Wa"), [[0, 9], [1, 16]], A.is_equal, 0.0, -15, 0)
+    group(a("WB"), a("Wb"), a("Wa"), 9)
+    iota(a("O1"), [[0, 128]], 1)
+    iota(a("Ca"), [[0, 32], [17024, 2]], -17280)
+    asel(a("ON"), a("O1"), [[0, 128]], A.is_ge, 2.0, -64, 1)
+    asel(a("Cb"), a("Ca"), [[0, 64]], A.is_ge, 0.0, 63, -1)
+    iota(a("ZO"), [[0, 32], [1, 2]], 0)
+    asel(a("CK"), a("Cb"), [[0, 64]], A.not_equal, 1.0, -64, 1)
+    for k, (lo, hi) in pads:
+        iota(cols("XN", lo, hi, k=k), [[0, hi - lo]], 0)
 
     def sendx(t):
         deps("g", ["XS"], [])
@@ -223,237 +250,223 @@ def rank_program(g, core, T, topo):
         total[sem] = n
         g.remote_dma(T["XF%d" % t][:], T.XS[:], T.sem[sem], T.sem.xl, pid, rid, topo.mask(core, dst))
         last["XF%d" % t] = (sem, n, "-")
-    iota(a("kr"), [[1, 128]], 0, 0)
-    iota(a("kg"), [[1, 8], [0, 16]], 0, 0)
-    iota(a("k16"), [[0, 12], [1, 16]], 0, 0)
     sendx(0)
-    dma("g", a("WW", k="01"), ext(T.w0[:]))
-    for nm in ("XN", "NX"):
-        for k, (lo, hi) in zip("xyz", ((0, OFF), (OFF + W, at(1)), (DUM, PL))):
-            iota(cols(nm, lo, hi, k=k), [[0, hi - lo]], 0, 0)
-
-    lx = lambda s: cols("LX", 192 * s, 192 * s + 192, k=AZ[6 * s:6 * s + 6])
-    piece = lambda nm, s: cols(nm, at(s), at(s) + W, k="ab"[s])
-    info = lambda lo: cols("INFO", lo, OFF + W, k=AZ[:8])
-    act(piece("XN", 0), ind(a("XS"), lx(0)))
-    cp(piece("XN", 1), ind(a("XS"), lx(1)))
-    ts(piece("NX", 0), ind(info(OFF), lx(0)), co["sc0"], A.mult, co["bi0"], A.add)
-    act(piece("NX", 1), ind(info(OFF), lx(1)), scale=co["sc1"], bias=co["bi1"])
-    XN, NX = a("XN", k="abxyz"), a("NX", k="abxyz")
-
-    iota(a("KC"), [[1, 96]], 1025, 0)
-    iota(a("kb0"), [[16, 6]], 0, 0)
-    iota(a("D0"), [[0, 192]], 65536, 0)
-    iota(a("D1"), [[96, 2], [16, 6], [0, 16]], DUM, 0)
+    asel(a("I128"), a("O1"), [[-1, 128]], A.is_equal, 0.0, 0, 1)
+    group(a("BL"), a("O1"), a("Ba"), 8)
+    iota(a("KC"), [[1, 96]], 1025)
+    iota(a("kb0"), [[16, 6]], 0)
+    iota(a("D1"), [[96, 2], [16, 6], [0, 16]], DUM)
     asel(a("DA"), a("D0"), [[0, 12], [1, 16]], A.is_equal, -1.0, 0, 0)
     asel(a("D2"), a("D1"), [[0, 12], [1, 16]], A.is_equal, -65536.0, 0, 0)
-    n32 = lambda h: iota(cols("N32", PL // 2 * h, PL // 2 * (h + 1), k="xy"[h]), [[0, PL // 2]], 0, 0)
-    n32(0)
+    iota(a("CD0"), [[0, 192]], 65536)
+    asel(a("M16"), a("O1"), [[0, 8], [1, 16]], A.is_equal, 0.0, 0, -1)
+    asel(a("CD1"), a("CD0"), [[0, 12], [1, 16]], A.not_equal, 0.0, 0, -1)
+    asel(a("CD2"), cols("CD0", 0, 96), [[0, 6], [1, 16]], A.not_equal, -40960.0, 0, -1)
+    iota(a("on"), [[0, 48]], 1)
+    iota(cols("RK", 48, 64, k="z"), [[0, 16]], 0)
+    for nm in ("W1", "W2"):
+        iota(cols(nm, 48, 64, k="z"), [[0, 16]], 0, 0, True)
 
-    def fro_lo():
-        tt(a("FL"), a("froc"), a("FH"), A.subtract)
-        put_info("y", 6, "FH")
-        put_info("y", 7, "FL")
-    late_v = [lambda: ts(a("I128"), a("kr"), p0, A.is_equal), lambda: ts(a("BL"), a("kg"), gi, A.is_equal), lambda: cp(a("FH"), a("froc")), fro_lo,
-              lambda: ts(a("CD1"), a("k16"), pm, A.not_equal, 65536.0, A.mult), lambda: fill(a("on"), 1.0),
-              lambda: fill(cols("RK", 48, 64, k="z"), 0.0), lambda: fill(cols("W1", 48, 64, k="z"), 0), lambda: fill(cols("W2", 48, 64, k="z"), 0)]
-    late_s = [lambda: act(a("NI"), a("I128"), scale=-1.0), lambda: act(a("ZR"), a("I128"), scale=0.0), lambda: act(a("BN"), a("BL"), scale=-1.0),
+    lx = lambda s, lo=0, hi=W: a("LX", al, s, slice(lo // 16, hi // 16), k=AZ[:6])
+    piece = lambda nm, s, lo=0, hi=W, k="": cols(nm, at(s) + lo, at(s) + hi, k=k or "ab"[s])
+    info = lambda lo: cols("INFO", lo, OFF + W, k=AZ[:8] + "p")
+    act(piece("NX", 0), ind(info(OFF), lx(0)), scale=sc0, bias=bi0)
+    ts(piece("NX", 1), ind(info(OFF), lx(1)), sc1, A.mult)
+    act(a("RA", k=ALL), ind(info(0), a("LR", k=ALL)), scale=wm)
+    tolist(cols("PA", 0, 48), lambda r: cols("RA", r, K, k=ALL, step=16))
+    act(piece("XN", 0, SHIFT), ind(a("XS"), lx(0, SHIFT)))
+    cp(a("LP", k=ALL), a("cp"))
+    ts(a("m2"), a("typc"), -1.0, A.mult, 2.0, A.add)
+    ts(a("cd"), a("typc"), -4.0 * TY, A.mult, 4.0 * at(1), A.add)
+    ts(a("cx"), a("cr"), 4.0, A.mult)
+    ts(gsc, col("co", 6), 1 / KK / 65536, A.max)
+    cp(piece("XN", 1), ind(a("XS"), lx(1)))
+    tt(a("ct"), cols("PA", 0, 48), a("m2"), A.mult)
+    tt(a("cq"), a("cx"), a("cd"), A.add)
+    cp(piece("XN", 0, 0, SHIFT, "c"), ind(a("XS"), lx(0, 0, SHIFT)))
+    ts(a("cf"), a("ct"), 1, A.arith_shift_right, 1, A.bitwise_and)
+    ts(wf, pm, 6.0, A.is_ge, 1 / KK, A.mult)
+    XN, NX = a("XN", k="abcxyz"), a("NX", k="abxyz")
+    late_s = [lambda: act(a("NJ"), a("I128"), scale=-1.0), lambda: act(a("BN"), a("BL"), scale=-1.0),
               lambda: act(a("BF"), a("BL")), lambda: act(a("BK"), a("BL"), scale=16384.0),
-              lambda: act(a("CD2"), cols("CD1", 0, 96), scale=1.625, bias=-40960.0), lambda: act(col("pf", 5), pm, bias=0.5),
-              lambda: act(a("DB"), a("D2"), bias=pm), lambda: act(a("kb"), a("kb0"), bias=col("pf", 5))]
+              lambda: act(a("DB"), a("D2"), bias=pm), lambda: act(a("kb"), a("kb0"), bias=col("pf", 5)),
+              lambda: act(a("NI"), a("I128"), scale=-1.0)]
 
-    def late_g():
-        asel(a("U1"), a("BN"), [[-1, 128]], A.is_gt, 0.0, 0, 1)
-        asel(a("UW"), a("U1"), [[-1, 128]], A.not_equal, 1024.0, 0, 1)
+    st = lambda nm, j, bs: a(nm, al, j, slice(lo_(bs), hi_(bs)), k=[str(j) + b for b in bs])
+    both = lambda nm, b: a(nm, al, al, slice(lo_(b), hi_(b)), k=["0" + b, "1" + b])
+    xx = lambda b: cols("XX" + b, 1, 2 * wide(b), step=2)
+    wkeys = lambda bs: [b + h for b in bs for h in "ab"]
+    wcols = lambda lo, hi, bs, t: cols("WW" if t else "W0", 16 * lo, 16 * hi, k=wkeys(bs))
 
-    rr = lambda j, b: a("RR", al, j, slice(24 * b, 24 * b + 24), k="abcd"[2 * j + b])
-    po = lambda j, b: a("PO", al, j, slice(24 * b, 24 * b + 24), k="abcd"[2 * j + b])
-    both = lambda nm, b: a(nm, al, al, slice(24 * b, 24 * b + 24), k="ac" if b == 0 else "bd")
+    def features(b, t, lo, hi):
+        c = lo_(b)
+        tt(a("GN" + b, al, slice(16 * lo, 16 * hi), 0, k="a"), ind(XN, cols("LP", c + lo, c + hi, k=b)),
+           wcols(c + lo, c + hi, b, t), A.is_ge)
 
-    def gather(b, first=False):
-        Fb, c = "F%d" % b, K * b
-        tt(cols("GN", c, c + 384, k="ab"[b]), ind(XN, l24("LP", b)), half("WW", b), A.is_ge)
-        act(cols("GN", c + 384, c + K, k="cd"[b]), ind(NX, l24("LP", b)))
-        if first:
-            tolist(cols(Fb, 24, 48), "WB", "GN", c + 384, c + K, "cd"[b])
-            tolist(cols(Fb, 0, 24), "WX", "GN", c + 384, c + K, "cd"[b], stop=False)
-            tolist(cols(Fb, 0, 24), "WB", "GN", c, c + 384, "ab"[b], start=False)
-        else:
-            tolist(cols(Fb, 0, 48), "WB", "GN", c, c + K, ("ac", "bd")[b], stop=False)
-            tolist(cols(Fb, 0, 24), "WX", "GN", c + 384, c + K, "cd"[b], start=False)
+    def codes(b):
+        act(a("GN" + b, al, slice(0, 16 * wide(b)), 1, k="b"), ind(NX, lst("LP", b)), scale=gsc)
 
-    def choose(b):
-        Fb = "F%d" % b
-        tt(l24("YY", b), cols(Fb, 24, 48), po(1, b), A.max)
-        tt(rr(1, b), cols(Fb, 0, 24), po(1, b), A.max)
-        tt(rr(0, b), cols(Fb, 0, 24), l24("YY", b), A.min)
+    def sums(b):
+        Fb = cols("F" + b, 0, 2 * wide(b))
+        mm(Fb, a("ON"), cols("CK", 0, 2 * wide(b)), True, False)
+        tolist(Fb, lambda r: a("GN" + b, al, slice(r, 16 * wide(b), 16), al, k="ab"), start=False)
 
-    def step(b, cast=True, gaps=()):
-        gaps = list(gaps) + [skip] * 3
-        choose(b)
-        gaps[0]()
-        ts(both("PO", b), both("RR", b), 32767, A.bitwise_and)
-        gaps[1]()
-        if cast:
-            ts(l24("LP", b), po(0, b), 0.25, A.mult)
-        gaps[2]()
+    def read(b):
+        n = 2 * wide(b)
+        scan(cols("XX" + b, 0, n), cols("ZO", 0, n), cols("F" + b, 0, n), A.mult, A.add)
+        tt(lst("YY", b), cols("F" + b, 1, n, step=2), st("PO", 1, b), A.max)
 
-    same = lambda b: tt(l24("cr", b), po(1, b), l24("cq", b), A.is_equal)
-    flag = lambda b: tt(l24("cr", b), l24("cr", b), l24("cf", b), A.mult)
-    addf = lambda b: tt(po(1, b), po(1, b), l24("cr", b), A.add)
-    late_v += [lambda: tt(a("ct"), cols("PH", 0, 48), a("m2"), A.mult), skip,
-               lambda: ts(a("cf", k="01"), a("ct"), 1, A.arith_shift_right, 1, A.bitwise_and),
-               skip, lambda: same(0), lambda: flag(0), lambda: addf(0), lambda: same(1), lambda: flag(1)]
+    other = lambda b: tt(st("RR", 1, b), xx(b), st("PO", 1, b), A.max)
+    pick = lambda b: tt(st("RR", 0, b), xx(b), lst("YY", b), A.min)
+    differ = lambda b: tt(lst("df", b), xx(b), st("PO", 1, b), A.subtract)
+    mask = lambda b: ts(both("PO", b), both("RR", b), 32765, A.bitwise_and)
+    cast = lambda b: ts(lst("LP", b), st("PO", 0, b), 0.25, A.mult)
 
-    reclist = lambda b: ts(l24("lr", b), rr(0, b), 16383, A.bitwise_and)
-    reccast = lambda b: ts(l24("LR", b), l24("lr", b), 0.25, A.mult)
-    foreign = lambda b: tolist(cols("PH", 24 * b, 24 * b + 24), "WF", "RA", 384 * b, 384 * b + 384, str(b))
-    forcast = lambda b: cp(l24("LK", b), cols("PH", 24 * b, 24 * b + 24))
-
-    def minus_w(n):
-        b, lo = n % 2, 96 * (n // 2)
-        if lo == 0:
-            mm(cols("Y%d" % b, 0, 384), a("ZR"), cols("XS", 0, 384), True, False)
-        mm(cols("Y%d" % b, lo, lo + 96), a("NI"), cols("WW", 384 * b + lo, 384 * b + lo + 96, k=str(b)), False, False)
+    bank = lambda bs: cols("Y0" if bs == HEAD else "Y1", 0, 16 * wide(bs))
+    reclist = lambda bs: ts(lst("lr", bs), st("RR", 0, bs), 16380, A.bitwise_and)
+    reccast = lambda bs: ts(lst("LR", bs), lst("lr", bs), 0.25, A.mult)
+    fro_of = lambda bs: act(unit("RA", bs), ind(info(0), lst("LR", bs)), scale=wf)
+    fcols = lambda bs: cols("F" + bs[0], 64, 64 + wide(bs))
+    foreign = lambda bs, rs: tolist(fcols(bs), lambda r: cols("RA", 16 * lo_(bs) + r, 16 * hi_(bs), k=bs, step=16), rs=rs)
+    forcast = lambda bs: cp(lst("LK", bs), fcols(bs))
+    minus_w = lambda bs, t: mm(bank(bs), a("NI" if t else "NJ"), wcols(lo_(bs), hi_(bs), bs, t), True, False)
 
     def next_out(part):
-        if part == 0:
-            for r in range(2):
-                for s in range(2):
-                    dma("g", cols("NC", 192 * s, 192 * s + 192, k=str(s)), rows("NX", r, at(s), at(s) + W, NX[1]), **({"accum_op": A.add} if r else {}))
-        else:
-            act(a("NC2"), a("NC", k="01"), scale=KK / 4, bias=-64.0)
-            for s in range(2):
-                deps("y", [], ["N32x", "N32y"])
-                dma("y", rows("N32", 0, at(s), at(s) + W, ["N32" + "ab"[s]]), cols("NC2", 192 * s, 192 * s + 192))
+        for s in range(2):
+            nc = lambda nm: cols(nm, 192 * s, 192 * s + 192, k=str(s))
+            if part == 0:
+                dma("y", nc("NC"), rows("NX", 2, at(s), at(s) + W, NX[1]))
+            elif part == 1:
+                dma("g", nc("NC"), rows("NX", 3, at(s), at(s) + W, NX[1]), accum_op=A.add)
+            elif part == 2:
+                act(nc("NC2"), nc("NC"), scale=0.25, bias=RND - OFF - TY * (1 - s))
+            elif part == 3:
+                act(nc("NC3"), nc("NC2"), bias=-RND)
+            else:
+                dma("y", rows("NX", 0, at(s), at(s) + W, ["NX" + "ab"[s]]), nc("NC3"))
 
     for t in range(3):
-        gather(0, t > 0)
+        later = cast if t < 2 else lambda b: None
+        ops = {"r": read, "o": other, "p": pick, "m": mask, "c": lambda b: (cast(b), codes(b)), "g": lambda b: features(b, t, 0, SPLIT),
+               "h": lambda b: (features(b, t, SPLIT, wide(b)), sums(b)), "G": lambda b: (features(b, t, 0, wide(b)), sums(b)),
+               "d": differ, "l": later, "R": reclist, "C": lambda bs: (reccast(bs), fro_of(bs))}
+        for b in ALL:
+            codes(b)
+            ops["G"](b)
         if t == 0:
-            tt(a("c1"), a("c1"), a("cx"), A.subtract)
-        else:
-            tt(half("WW", 1), cols("Y1", 0, 384), half("WW", 1), A.add)
-        gather(1)
-        if t == 2:
-            dma("y", ext(T.yw[:], ["yw"]), a("WW", k="01"))
-        if t == 0:
-            ts(a("cr", k="01"), a("c1"), TY - 1, A.bitwise_and)
-            ts(a("PO", al, 1, al, k="cd"), a("c1"), 4.0, A.mult, 4.0 * OFF, A.add)
-            ts(a("LR", k="01"), a("cr", k="01"), float(OFF), A.add)
-            ts(a("cq", k="01"), a("c1"), 4.0, A.mult, 4.0 * OFF, A.add)
-            ts(a("m2"), a("typc"), -1.0, A.mult, 2.0, A.add)
-            for b in range(2):
-                act(half("RA", b), ind(info(0), l24("LR", b)))
-        for n in range(6):
-            step(n % 2, gaps=late_v[3 * n:3 * n + 3] if t == 0 else ())
-            gather(n % 2)
-            if t == 0:
-                if n == 0:
-                    tolist(cols("PH", 0, 48), "WM", "RA", 0, K, "01")
-                for fn in late_s[2 * n - 2:2 * n] if n else ():
+            tt(st("PO", 1, ALL), a("cq"), a("cf"), A.add)
+            cp(a("FH"), a("froc"))
+            for fn in late_s[:4]:
+                fn()
+            asel(a("U1"), a("BN"), [[-1, 128]], A.is_gt, 0.0, 0, 1)
+            asel(a("UW"), a("U1"), [[-1, 128]], A.not_equal, 1024.0, 0, 1)
+            sendx(1)
+        for q in range(3):
+            if q < 2:
+                minus_w((HEAD, TAIL)[q], t)
+            for tok in CYCLE.split():
+                ops[tok[0]](tok[1:])
+                if t == 0 and q == 0 and tok == "r0":
+                    tt(a("FL"), a("froc"), a("FH"), A.subtract)
+                    put_info("y", 6, "FH")
+                    put_info("y", 7, "FL")
+            if t == 0 and q == 0:
+                for fn in late_s[4:]:
                     fn()
-                if n == 2:
-                    late_g()
-                    sendx(1)
-            for k in (((), (0,), (1,), (2, 3), (4, 5), (6, 7)) if t == 0 else ((0,), (1,), (2,), (3, 4), (5, 6), (7,)))[n]:
-                minus_w(k)
-            if t == 2 and n == 5:
-                next_out(1)
-        if t == 1:
-            n32(1)
-        r0, r1 = a("RR", al, 0, al, k="ab"), a("RR", al, 1, al, k="cd")
-        step(0, t < 2, [lambda: reclist(0), lambda: reccast(0), (lambda: addf(1)) if t == 0 else skip])
-        act(half("RA", 0), ind(info(0), l24("LR", 0)))
-        mm(cols("PD", 0, 192), a("I128"), a("CD1"), True, False)
-        foreign(0)
-        mm(cols("PE", 0, 96), a("I128"), a("CD2"), True, False)
+            if t == 2:
+                for part_ in ((), (2,), (3, 4))[q]:
+                    next_out(part_)
+        r0, r1 = st("RR", 0, ALL), st("RR", 1, ALL)
+        for tok in FINAL.split():
+            ops[tok[0]](tok[1:])
+        mm(cols("PD", 0, 192), part("M16", 0, 16), part("CD1", 0, 16), True, False)
+        pull = lambda bs: act(unit("YG", bs), ind(a("XF%d" % t), lst("LK", bs)))
+        meet = lambda bs: mm(bank(bs), a("I128"), unit("YG", bs), False, True)
 
-        def pull(b):
-            act(half("YG", b), ind(a("XF%d" % t), l24("LK", b)))
-            mm(cols("Y%d" % b, 0, 384), a("I128"), half("YG", b), False, True)
+        cut = lambda bs: ts(bank(bs), bank(bs), 8.0, A.min, -8.0, A.max)
 
-        def addw(b):
-            ts(half("DD", b), cols("Y%d" % b, 0, 384), 8.0, A.min, -8.0, A.max)
-            dma("g", half("WW", b) if t < 2 else ext(T.yw[:, 384 * b:384 * b + 384], ["yw"] if b == 0 else ["yw1"]), half("DD", b), accum_op=A.add)
-        choose(1)
-        ts(cols("W2", 0, 48, k="a"), r1, 32767, A.bitwise_and, 2, A.arith_shift_right)
-        tt(a("tt_"), r0, r1, A.subtract)
+        def addw(bs, h):
+            n = 8 * wide(bs)
+            c = 16 * lo_(bs) + n * h
+            k = wkeys(bs)[h::2]
+            tt(cols("WW", c, c + n, k=k), cols(bank(bs)[1][0], n * h, n * h + n), cols("WW" if t else "W0", c, c + n, k=k), A.add)
+            if t == 2 and h == 1:
+                dma("y", ext(T.yw[:, 16 * lo_(bs):16 * hi_(bs)]), wcols(lo_(bs), hi_(bs), bs, t))
+        ts(a("tu"), lst("df", ALL), 16380, A.bitwise_and)
         ts(a("tf"), r0, 1, A.bitwise_and)
-        ts(a("tu"), a("tt_"), 16380, A.bitwise_and)
-        reclist(1)
+        reclist(TAIL)
+        mask(TAIL)
+        later(HEAD[-1])
         tt(a("wt"), a("tu"), a("tf"), A.min)
-        reccast(1)
+        reccast(TAIL)
+        ts(a("ta"), r0, 16384.0, A.add)
+        later(TAIL)
         scan(a("cs"), a("on"), a("wt"), A.mult, A.add)
-        forcast(0)
+        ts(unit("RA", TAIL), ind(info(0), lst("LR", TAIL)), wf, A.mult)
+        mm(cols("PE", 128, 176), a("UW"), a("wt"), True, False)
+        foreign(HEAD, range(6))
         mm(cols("PA", 0, 48), a("BL"), a("cs"))
-        mm(cols("PH", 64, 112), a("UW"), a("wt"), True, False)
-        mm(cols("PH", 64, 112), a("BL"), a("cs"), False, True)
+        mm(cols("PE", 128, 176), a("BL"), a("cs"), False, True)
+        foreign(HEAD, range(6, 16))
         for k in range(6):
             act(cols("SG", 48 * k, 48 * k + 48, k=AZ[k]), cols("PA", 0, 48), scale=-1.0, bias=cols("kb", k, k + 1), acc=col("CA", k), fn=F.Sign)
-        cp(half("RA", 1), ind(info(0), l24("LR", 1)))
-        cp(cols("RK", 0, 48, k="a"), cols("PH", 64, 112))
-        ts(a("ta"), r0, 16384.0, A.add)
-        foreign(1)
-        pull(0)
-        ts(a("LC"), a("CA", k=AZ[:6]), 48.0, A.add, 0.5, A.mult)
+        foreign(TAIL, range(16))
+        ts(cols("W2", 0, 48, k="a"), r1, 32767, A.bitwise_and, 2, A.arith_shift_right)
         ts(cols("W1", 0, 48, k="a"), a("ta"), 32767, A.bitwise_and, 2, A.arith_shift_right)
+        cp(cols("RK", 0, 48, k="a"), cols("PE", 128, 176))
+        mm(cols("PE", 0, 96), part("M16", 0, 16), part("CD2", 0, 16), True, False)
+        forcast(HEAD)
+        pull(HEAD)
+        meet(HEAD)
+        ts(a("LC"), a("CA", k=AZ[:6]), 48.0, A.add, 0.5, A.mult)
+        if t == 2:
+            ts(a("ya"), a("PO", k=[j + b for j in "01" for b in ALL]), 2, A.arith_shift_right)
+        forcast(TAIL)
+        pull(TAIL)
         tt(a("MK"), ind(a("RK", k="az"), a("LC")), a("KC"), A.is_equal)
-        ts(both("PO", 1), both("RR", 1), 32767, A.bitwise_and)
-        for w in range(2):
-            tt(w96("MV", w, str(w)), ind(a("W%d" % (w + 1), k="az"), a("LC")), a("MK"), A.mult)
-            mm(w96("PA", w), a("BF"), w96("MV", w, str(w)))
-            mm(w96("PD", w), a("BF"), w96("MV", w, str(w)), False, w == 1)
-        forcast(1)
-        addw(0)
-        cp(a("RU"), cols("PA", 0, 192))
-        scan(a("LS"), a("DA"), cols("PD", 0, 192), A.max, A.min)
-        pull(1)
-        if t < 2:
-            ts(l24("LP", 1), po(0, 1), 0.25, A.mult)
-        else:
-            ts(a("ya"), a("PO", k="abcd"), 2, A.arith_shift_right)
-        for e in range(12):
-            ts(cols("EQ", 192 * e, 192 * e + 192, k=AZ[e]), a("RU"), cols("LS", 16 * e + 15, 16 * e + 16), A.is_equal)
-            for w in range(2):
-                mm(cols("PE", 0, 96), a("BK"), cols("EQ", 192 * e + 96 * w, 192 * e + 96 * w + 96, k=AZ[e]), False, e == 11 and w == 1)
-            if e == 0:
-                cp(cols("LE0", 0, 6, k="a"), cols("LS", 96 + 15, 192, step=16))
-                cp(cols("LE0", 6, 12, k="b"), cols("LS", 15, 96, step=16))
-                le0 = a("LE0", k="ab")
-                if t < 2:
-                    act(a("gn"), ind(NX, le0))
-                    act(a("gx"), ind(XN, le0))
-                else:
-                    act(a("g32"), ind(a("N32", k="xyab"), le0))
-            if e == 3 and t == 2:
-                addw(1)
-        if t < 2:
-            ts(cols("Y1", 0, 384), cols("Y1", 0, 384), 8.0, A.min, -8.0, A.max)
-        if t == 0:
-            sendx(2)
         if t == 2:
             tt(a("cd"), cols("ya", 0, 48), cols("ya", 48, 96), A.min)
             tt(a("cx"), cols("ya", 0, 48), cols("ya", 48, 96), A.max)
         for w in range(2):
-            scan(w96("QQ", w, str(w)), w96("DB", w), cols("PE", 0, 96), A.max, A.min)
-        tt(a("LQ"), cols("LS", 15, 192, step=16), cols("QQ", 15, 192, k="01", step=16), A.max)
+            tt(w96("MV", w, str(w)), ind(a("W%d" % (w + 1), k="az"), a("LC")), a("MK"), A.mult)
+        for nm, w in (("PD", 0), ("PA", 0), ("PD", 1), ("PA", 1)):
+            mm(w96(nm, w), a("BF"), w96("MV", w, str(w)), nm == "PA", nm == "PA" or w == 1)
+        meet(TAIL)
+        cut(HEAD)
         if t == 2:
             ts(cols("yco", 0, 48, k="0"), a("cd"), -float(at(0)), A.add)
-        cp(a("LE1"), a("LQ"))
-        if t == 2:
             ts(cols("yco", 48, 96, k="1"), a("cx"), -float(at(1)), A.add)
-            dma("s", ext(T.yc[:]), a("yco", k="01"))
-
-        def put(win, src):
-            run("v", lambda: g.vector.tensor_copy(win[0].indirect(T.LE1[:]), src[0]), [win], [src, a("LE1")])
+            dma("y", ext(T.yc[:]), a("yco", k="01"))
+        addw(HEAD, 0)
+        scan(a("LS"), a("DA"), cols("PD", 0, 192), A.max, A.min)
+        cp(a("RU"), cols("PA", 0, 192))
+        addw(HEAD, 1)
+        cp(a("LE0"), cols("LS", 15, 192, step=16))
+        for nm, win in (("gx", XN), ("gn", NX))[t // 2:]:
+            for w in range(2):
+                act(w96(nm, 1 - w, str(w)), ind(win, cols("LE0", 6 * w, 6 * w + 6)))
+        if t == 0:
+            sendx(2)
+        for e in range(12):
+            ts(cols("EQ", 192 * e, 192 * e + 192, k=AZ[e]), a("RU"), cols("LS", 16 * e + 15, 16 * e + 16), A.is_equal)
+            for w in range(2):
+                mm(cols("PE", 0, 96), a("BK"), cols("EQ", 192 * e + 96 * w, 192 * e + 96 * w + 96, k=AZ[e]), False, e == 11 and w == 1)
+        cut(TAIL)
+        for w in range(2):
+            scan(w96("QQ", w, str(w)), w96("DB", w), cols("PE", 0, 96), A.max, A.min)
+        addw(TAIL, 0)
+        tt(a("LQ"), cols("LS", 15, 192, step=16), cols("QQ", 15, 192, k="01", step=16), A.max)
+        addw(TAIL, 1)
+        cp(a("LE1"), a("LQ"))
         if t < 2:
-            put(NX, a("gn"))
-            put(XN, a("gx"))
+            put("s", NX, a("LE1"), a("gn", k="01"))
+            put("v", XN, a("LE1"), a("gx", k="01"))
             if t == 1:
                 next_out(0)
+                next_out(1)
         else:
-            put(a("N32", k="xyab"), a("g32"))
+            put("v", NX, a("LE1"), a("gn", k="01"))
             for s in range(2):
-                dma("ys"[s], ext(T.yn[:, W * s:W * s + W]), rows("N32", 0, at(s), at(s) + W, ["N32a"]))
+                dma("ys"[s], ext(T.yn[:, W * s:W * s + W]), rows("NX", 0, at(s), at(s) + W, NX[1]))
     for sem, val in total.items():
         need("g", sem, val)

@@ -6,30 +6,33 @@ RND = 12582912.0
 CUT = (0, 24, 48)
 ALL = "012"[:len(CUT) - 1]
 HEAD, TAIL = ALL[:-1], ALL[-1]
-CYCLE = "r0 o0 p0 r1 m0 o1 p1 c0 m1 g0 c1 h0 G1"
-FINAL = "r0 o0 p0 d0 r1 R0 o1 p1 d1 C0 m0"
-SPLIT = 10
-SHIFT = 384
+CYCLE = "r0 o0 p0 r1 m0 o1 p1 c0 m1 g0:10 c1 g0 g1"
+FINAL = "r0 p0 d0 o0 r1 R0 d1 p1 C0 o1"
+SHIFT = 320
+START = "L0 x1408 L1 M0 x192 M1 L2 F0 F1 x384"
+ROUND0 = ("r0 x192 o0 p0 r1 x128 m0 o1 p1 x160 c0 x m1 L4 c1 g0 g1",
+          "L3 L5 r0 o0 p0 r1 m0 o1 p1 c0 m1 g0:10 c1 g0 g1 L6",
+          "L8 r0 L7 o0 p0 r1 m0 o1 p1 c0 s0 m1 g0:10 c1 f0 s1 g0 a0 f1 g1 a1")
 F4, B2, I4, U2 = "float32", "bfloat16", "int32", "uint16"
 SCRATCH = {}
 for names, shape, dtype in (
-        ("XS XF0 XF1 XF2", [W], B2), ("XN", [PL], B2), ("NX", [PL], F4), ("INFO", [OFF + W], B2), ("WW", [K], F4),
-        ("NB", [2, 2, 96], I4), ("NF", [2, 6, 2, 16], F4), ("FT", [2, 6, 32], F4), ("LX", [2, 192], U2),
+        ("XS XF0 XF1 XF2", [W], B2), ("XN", [PL], B2), ("NX", [PL], F4), ("INFO", [OFF + W], B2), ("WW DD", [K], F4),
+        ("NB", [2, 192], I4), ("NF", [12, 2, 16], F4), ("FT", [12, 32], F4), ("LX", [384], U2),
         ("memc froc m0", [192], I4), ("curc ya", [96], I4), ("typc c1 cd cx cp cq cr m2 ct cf df tu tf ta lr", [48], I4), ("yco", [96], F4),
         ("HI LO B1 B0 FH FL hb", [192], B2), ("GN0 GN1 GN2", [512, 2], B2), ("RA YG W0", [K], B2),
-        ("RR PO", [2, 48], I4), ("YY", [48], F4), ("ZO XX0 XX1 XX2", [64], F4), ("CK Ca Cb", [64], B2), ("LP LR LK", [48], U2),
-        ("pc", [4], I4), ("pf co", [16], F4), ("WB Wa Wb", [144], B2),
-        ("BL BN BK UW U1 I128 ON O1 NJ M16 Ba", [128], B2), ("BF NI", [128], F4),
-        ("KC MK", [96], F4), ("kb kb0 CA", [6], F4), ("CD0 CD1", [192], B2), ("CD2", [96], B2), ("DA DB D0 D1 D2", [192], F4),
-        ("on wt cs", [48], B2), ("SG", [288], F4), ("LC", [6], U2), ("RK", [64], F4), ("W1 W2", [64], I4),
-        ("MV LS QQ gn", [192], F4), ("RU", [192], U2), ("EQ", [2304], B2), ("LQ", [12], F4), ("LE0 LE1", [12], U2),
+        ("RR", [3, 48], I4), ("PO", [2, 48], I4), ("YY", [48], F4), ("ZO XX0 XX1 XX2", [64], F4), ("CK Ca Cb", [64], B2), ("LP LR LK", [48], U2),
+        ("pc", [4], I4), ("pf", [8], F4), ("co", [24], F4), ("WB WC Wa Wb", [144], B2), ("cn", [48], B2),
+        ("BL BN BK UW U1 U2 I128 ON O1 NJ M16 Ba", [128], B2), ("BF NI", [128], F4),
+        ("KC MK", [96], F4), ("kb kb0 CA", [6], F4), ("CD0 CD1 CD2 CD3", [192], B2), ("DA D1 D2", [192], F4),
+        ("on wt cs", [48], B2), ("SG", [288], F4), ("LC", [6], U2), ("RK", [64], F4), ("WP", [2, 64], I4),
+        ("MV gn", [192], F4), ("QQ DB", [384], F4), ("RU", [192], U2), ("EQ", [2304], B2), ("LE0 LE1", [12], U2),
         ("gx", [192], B2), ("NC NC2 NC3", [384], F4)):
     for nm in names.split():
         SCRATCH[nm] = ("sbuf", [128] + shape, dtype)
 PSUMS = ("F0", "F1", "F2", "PA", "PD", "PE", "Y0", "Y1")
 for nm in PSUMS:
     SCRATCH[nm] = ("psum", [128, 512], F4)
-SEMAPHORES = ["qv", "qp", "qs", "qg", "xl", "xa0", "xa1", "xa2"] + ["e%d" % k for k in range(14)] + ["d%d" % k for k in range(30)]
+SEMAPHORES = ["qv", "qp", "qs", "qg", "xl", "xa0", "xa1", "xa2", "rows"] + ["e%d" % k for k in range(14)] + ["d%d" % k for k in range(30)]
 AZ = "abcdefghijklmnopqrstuvwxyzABCDEF"
 
 
@@ -163,14 +166,13 @@ def rank_program(g, core, T, topo):
     skip = lambda: None
     pads = list(zip("xyz", ((0, OFF), (OFF + W, at(1)), (DUM, PL))))
 
-    def tolist(out, rhs, start=True, rs=range(16)):
-        for r in rs:
-            mm(out, cols("WB", 15 - r, 143 - r), rhs(r), start and r == 0, r == 15)
+    def tolist(out, rhs, start=True, wts="WB"):
+        for r in range(16):
+            mm(out, cols(wts, 15 - r, 143 - r), rhs(r), start and r == 0, r == 15)
 
     dma("y", a("memc"), ext(T.mem[:]))
     for h in range(2):
-        for s in range(2):
-            dma("sy"[s], a("NB", al, s, h, al, k=AZ[2 * s + h]), ext(T.nxt[h:8:2, W * s:W * s + W]))
+        dma("sy"[h], a("NB", al, h, al, k=str(h)), ext(T.nxt[h:8:2, :]))
     dma("s", a("curc"), ext(T.cur[:]))
     dma("s", a("typc"), ext(T.typ[:]))
 
@@ -179,50 +181,56 @@ def rank_program(g, core, T, topo):
     iota(a("LO"), [[0, 3], [4, 64]], 4 * OFF)
     fill(cols("INFO", 0, 1024, k="p"), 0.0)
     ts(col("pc", 1), col("pc", 0), 15, A.bitwise_and)
-    fill(cols("INFO", 1024, 2048, k=AZ[:8]), 0.0)
+    fill(cols("INFO", 1024, 2048, k="q"), 0.0)
     pm = col("pf", 1)
+    ts(col("pf", 4), col("pc", 1), 768.0, A.mult)
     cp(pm, col("pc", 1))
     fill(cols("INFO", 2048, OFF + W, k=AZ[:8]), 0.0)
-    for k, (lo, hi) in pads:
-        act(cols("NX", lo, hi, k=k), cols("INFO", 0, hi - lo, k="p"))
-    act(col("pf", 4), pm, scale=768.0)
-    act(col("pf", 6), pm, bias=-2.5, fn=F.Abs)
-    act(col("pf", 5), pm, bias=0.5)
-    act(a("HI"), a("hb"), bias=col("pf", 4))
-    put_info = lambda q, r, nm: dma(q, rows("INFO", r, OFF, OFF + W, ["INFO" + AZ[r]]), a(nm))
+    ts(a("HI"), a("hb"), col("pf", 4), A.add)
     sc0, sc1, bi0, gsc, wf, wm = [col("co", j) for j in range(6)]
+    cc = lambda j: col("co", j)
+    u = 1 / KK / 65536
+    for j, fn, scale, bias in ((6, F.Sign, -1.0, 3.5), (7, F.Sign, 1.0, -1.5), (8, F.Abs, 1.0, -2.0), (9, F.Abs, 1.0, -2.5),
+                               (10, F.Sign, 1.0, -5.5), (11, F.Abs, 1.0, -4.0), (12, F.Abs, 1.0, -1.0)):
+        act(cc(j), pm, scale=scale, bias=bias, fn=fn)
+    for out, j, fn, scale, bias in ((sc0, 6, F.Relu, 1.0, 0.0), (sc1, 7, F.Relu, 1.0, 0.0), (bi0, 8, F.Relu, -4.0 * TY, 4.0 * TY),
+                                    (cc(13), 9, F.Sign, -1.0, 1.0), (cc(14), 9, F.Sign, -1.0, 2.0), (wf, 10, F.Relu, 1 / KK, 0.0),
+                                    (cc(15), 11, F.Relu, -u, u), (cc(16), 12, F.Relu, -2 * u, 2 * u)):
+        act(out, cc(j), scale=scale, bias=bias, fn=fn)
+    pad = lambda k, lo, hi: [act(cols("NX", c, min(c + 192, hi), k=k), cols("hb", 0, min(192, hi - c)), scale=0.0) for c in range(lo, hi, 192)]
+    for k, (lo, hi) in pads[::2]:
+        pad(k, lo, hi)
+    put_info = lambda q, r, nm: dma(q, rows("INFO", r, OFF, OFF + W, ["INFO" + AZ[r]]), a(nm))
     ts(a("m0"), a("memc"), 1, A.bitwise_and)
     ts(a("B1"), a("memc"), 2.0, A.is_ge, 65536.0, A.mult)
-    ts(sc0, pm, 3.0, A.is_le)
-    ts(sc1, pm, 2.0, A.is_ge)
     ts(a("B0"), a("m0"), 65536.0, A.mult)
-    deps("y", [], ["INFOp"])
-    for q, r, nm in (("y", 3, "LO"), ("s", 2, "HI"), ("y", 0, "B1"), ("s", 1, "B1"), ("y", 4, "B0"), ("s", 5, "B0")):
+    for q, r, nm in (("y", 3, "LO"), ("y", 2, "HI"), ("s", 0, "B1"), ("y", 1, "B1"), ("s", 4, "B0"), ("y", 5, "B0")):
         put_info(q, r, nm)
+    g.scalar.sem_inc(T.sem.rows, 1)
+    g.sync.wait_ge(T.sem.rows, 1)
     dma("y", a("XS"), ext(T.x[:]))
     dma("y", a("W0", k=[b + h for b in ALL for h in "ab"]), ext(T.w0[:]))
+    dma("y", cols("XN", OFF + W, at(1), k="y"), ext(T.x[:, 0:TY - W]))
     dma("y", a("froc"), ext(T.fro[:]))
-    act(a("D0"), a("hb"), scale=0.0, bias=65536.0, fn=F.Silu)
+    act(cc(17), cc(13), fn=F.Relu)
+    act(gsc, cc(14), scale=(1 / KK - u) / 2, bias=(1 / KK + u) / 2)
+    pad("y", OFF + W, at(1))
 
     cur0, cur1 = cols("curc", 0, 48), cols("curc", 48, 96)
     for h in range(2):
-        cp(a("NF", al, al, al, h, al, k=str(h)), a("NB", al, al, h, al, k=AZ[h] + AZ[2 + h]))
+        cp(a("NF", al, al, h, al, k=str(h)), a("NB", al, h, al, k=str(h)))
     tt(a("cd"), cur1, cur0, A.subtract)
     ts(a("c1"), a("typc"), float(TY), A.mult, float(OFF), A.add)
-    ts(bi0, pm, 2.0, A.is_equal, 4.0 * TY, A.mult)
     run("v", lambda: g.vector.transpose(T.FT[:], T.NF[:]), [a("FT")], [a("NF", k="01")])
     tt(a("cx"), a("cd"), a("typc"), A.mult)
     tt(a("c1"), a("c1"), cur0, A.add)
-    ts(col("co", 7), pm, 4.0, A.is_equal, 1 / KK / 65536, A.mult)
-    for b in range(6):
-        cp(a("LX", al, al, slice(b, 192, 6), k=AZ[b]), a("FT", al, al, b, al))
+    ts(a("cn"), a("typc"), 4.0 * TY, A.mult, -4.0 * at(1), A.add)
+    for b in range(12):
+        cp(cols("LX", b, 384, k=AZ[b], step=12), a("FT", al, b, al))
         if b == 1:
-            tt(a("cr"), cur1, a("cx"), A.subtract)
-    ts(col("co", 8), pm, 1.0, A.is_equal, 2 / KK / 65536, A.mult)
-    ts(a("LR", k=ALL), a("cr"), float(OFF), A.add)
-    tt(a("cp"), a("c1"), a("cx"), A.add)
-    ts(col("co", 6), col("pf", 6), 2.0, A.is_lt, 1 / KK, A.mult)
-    tt(wm, col("co", 7), col("co", 8), A.add)
+            tt(a("cp"), a("c1"), a("cx"), A.add)
+    cp(a("LP", k=ALL), a("cp"))
+    tt(a("cr"), cur1, a("cx"), A.subtract)
 
     group = lambda out, in_, tmp, n: (asel(tmp, in_, [[-16, n], [0, 16]], A.is_ge, 0.0, 0, 1), asel(out, tmp, [[16, n], [0, 16]], A.is_ge, 0.0, 15, -1))
     part = lambda nm, lo, hi, k="": a(nm, slice(lo, hi), al, k=k)
@@ -235,7 +243,8 @@ def rank_program(g, core, T, topo):
     asel(a("Cb"), a("Ca"), [[0, 64]], A.is_ge, 0.0, 63, -1)
     iota(a("ZO"), [[0, 32], [1, 2]], 0)
     asel(a("CK"), a("Cb"), [[0, 64]], A.not_equal, 1.0, -64, 1)
-    for k, (lo, hi) in pads:
+    asel(a("I128"), a("O1"), [[-1, 128]], A.is_equal, 0.0, 0, 1)
+    for k, (lo, hi) in pads[::2]:
         iota(cols("XN", lo, hi, k=k), [[0, hi - lo]], 0)
 
     def sendx(t):
@@ -250,50 +259,46 @@ def rank_program(g, core, T, topo):
         total[sem] = n
         g.remote_dma(T["XF%d" % t][:], T.XS[:], T.sem[sem], T.sem.xl, pid, rid, topo.mask(core, dst))
         last["XF%d" % t] = (sem, n, "-")
+    asel(a("Ba"), a("O1"), [[-16, 8], [0, 16]], A.is_ge, 0.0, 0, 1)
+    iota(a("BN"), [[0, 128]], -1)
+    asel(a("BL"), a("Ba"), [[16, 8], [0, 16]], A.is_ge, 0.0, 15, -1)
     sendx(0)
-    asel(a("I128"), a("O1"), [[-1, 128]], A.is_equal, 0.0, 0, 1)
-    group(a("BL"), a("O1"), a("Ba"), 8)
-    iota(a("KC"), [[1, 96]], 1025)
-    iota(a("kb0"), [[16, 6]], 0)
     iota(a("D1"), [[96, 2], [16, 6], [0, 16]], DUM)
-    asel(a("DA"), a("D0"), [[0, 12], [1, 16]], A.is_equal, -1.0, 0, 0)
+    iota(a("kb0"), [[16, 6]], 0)
+    asel(a("U1"), a("BN"), [[-1, 128]], A.is_gt, 0.0, 0, 1)
     asel(a("D2"), a("D1"), [[0, 12], [1, 16]], A.is_equal, -65536.0, 0, 0)
-    iota(a("CD0"), [[0, 192]], 65536)
+    asel(a("U2"), a("U1"), [[16, 8], [0, 16]], A.is_ge, 0.0, 15, -1)
+    iota(a("CD3"), [[0, 192]], -65536)
+    asel(a("UW"), a("U2"), [[-1, 128]], A.not_equal, 1024.0, 0, 1)
     asel(a("M16"), a("O1"), [[0, 8], [1, 16]], A.is_equal, 0.0, 0, -1)
-    asel(a("CD1"), a("CD0"), [[0, 12], [1, 16]], A.not_equal, 0.0, 0, -1)
-    asel(a("CD2"), cols("CD0", 0, 96), [[0, 6], [1, 16]], A.not_equal, -40960.0, 0, -1)
+    asel(a("CD1"), a("CD3"), [[0, 12], [1, 16]], A.not_equal, 0.0, 0, -1)
+    iota(a("CD0"), [[0, 192]], 65536)
+    iota(a("KC"), [[1, 96]], 1025)
+    asel(a("CD2"), a("CD0"), [[0, 6], [1, 16], [1000, 2]], A.not_equal, -40960.0, 0, -1)
+    asel(a("DA"), a("CD0"), [[0, 12], [1, 16]], A.not_equal, -1.0, 0, 0)
     iota(a("on"), [[0, 48]], 1)
     iota(cols("RK", 48, 64, k="z"), [[0, 16]], 0)
-    for nm in ("W1", "W2"):
-        iota(cols(nm, 48, 64, k="z"), [[0, 16]], 0, 0, True)
+    iota(a("WP", al, al, slice(48, 64), k="z"), [[0, 32]], 0, 0, True)
 
-    lx = lambda s, lo=0, hi=W: a("LX", al, s, slice(lo // 16, hi // 16), k=AZ[:6])
+    lx = lambda s, lo=0, hi=W: cols("LX", 192 * s + lo // 16, 192 * s + hi // 16, k=AZ[:12])
     piece = lambda nm, s, lo=0, hi=W, k="": cols(nm, at(s) + lo, at(s) + hi, k=k or "ab"[s])
-    info = lambda lo: cols("INFO", lo, OFF + W, k=AZ[:8] + "p")
+    info = lambda lo: cols("INFO", lo, OFF + W, k=AZ[:8] + "pq")
+    act(a("WC"), a("WB"), scale=cc(17))
     act(piece("NX", 0), ind(info(OFF), lx(0)), scale=sc0, bias=bi0)
     ts(piece("NX", 1), ind(info(OFF), lx(1)), sc1, A.mult)
-    act(a("RA", k=ALL), ind(info(0), a("LR", k=ALL)), scale=wm)
-    tolist(cols("PA", 0, 48), lambda r: cols("RA", r, K, k=ALL, step=16))
-    act(piece("XN", 0, SHIFT), ind(a("XS"), lx(0, SHIFT)))
-    cp(a("LP", k=ALL), a("cp"))
-    ts(a("m2"), a("typc"), -1.0, A.mult, 2.0, A.add)
-    ts(a("cd"), a("typc"), -4.0 * TY, A.mult, 4.0 * at(1), A.add)
-    ts(a("cx"), a("cr"), 4.0, A.mult)
-    ts(gsc, col("co", 6), 1 / KK / 65536, A.max)
-    cp(piece("XN", 1), ind(a("XS"), lx(1)))
-    tt(a("ct"), cols("PA", 0, 48), a("m2"), A.mult)
-    tt(a("cq"), a("cx"), a("cd"), A.add)
-    cp(piece("XN", 0, 0, SHIFT, "c"), ind(a("XS"), lx(0, 0, SHIFT)))
-    ts(a("cf"), a("ct"), 1, A.arith_shift_right, 1, A.bitwise_and)
-    ts(wf, pm, 6.0, A.is_ge, 1 / KK, A.mult)
     XN, NX = a("XN", k="abcxyz"), a("NX", k="abxyz")
-    late_s = [lambda: act(a("NJ"), a("I128"), scale=-1.0), lambda: act(a("BN"), a("BL"), scale=-1.0),
-              lambda: act(a("BF"), a("BL")), lambda: act(a("BK"), a("BL"), scale=16384.0),
-              lambda: act(a("DB"), a("D2"), bias=pm), lambda: act(a("kb"), a("kb0"), bias=col("pf", 5)),
-              lambda: act(a("NI"), a("I128"), scale=-1.0)]
+    built = [SHIFT]
+
+    def build(n):
+        lo = built[0]
+        built[0] = hi = lo + int(n) if n else W
+        cp(piece("XN", 1, lo, hi), ind(a("XS"), lx(1, lo, hi)))
+    late_s = [lambda: (act(wm, cc(15), bias=cc(16)), act(a("NI"), a("I128"), scale=-1.0), act(a("NJ"), a("I128"), scale=-1.0)),
+              lambda: act(a("BK"), a("BL"), scale=16384.0, fn=F.Silu), lambda: act(col("pf", 5), pm, bias=0.5), lambda: act(a("BF"), a("BL")),
+              lambda: act(cols("DB", 0, 384, k="e", step=2), a("D2"), bias=pm), lambda: act(a("kb"), a("kb0"), bias=col("pf", 5))]
 
     st = lambda nm, j, bs: a(nm, al, j, slice(lo_(bs), hi_(bs)), k=[str(j) + b for b in bs])
-    both = lambda nm, b: a(nm, al, al, slice(lo_(b), hi_(b)), k=["0" + b, "1" + b])
+    both = lambda nm, b: a(nm, al, slice(0, 2), slice(lo_(b), hi_(b)), k=["0" + b, "1" + b])
     xx = lambda b: cols("XX" + b, 1, 2 * wide(b), step=2)
     wkeys = lambda bs: [b + h for b in bs for h in "ab"]
     wcols = lambda lo, hi, bs, t: cols("WW" if t else "W0", 16 * lo, 16 * hi, k=wkeys(bs))
@@ -322,12 +327,38 @@ def rank_program(g, core, T, topo):
     mask = lambda b: ts(both("PO", b), both("RR", b), 32765, A.bitwise_and)
     cast = lambda b: ts(lst("LP", b), st("PO", 0, b), 0.25, A.mult)
 
+    def mlist(b):
+        out = cols(("PA", "PD", "PE")[int(b)], 0, wide(b))
+        mm(out, a("I128"), cols("cn", lo_(b), hi_(b)), True, False)
+        tolist(out, lambda r: a("GN" + b, al, slice(r, 16 * wide(b), 16), 1, k="b"), start=False, wts="WC")
+    mcast = lambda b: ts(lst("LK", b), cols(("PA", "PD", "PE")[int(b)], 0, wide(b)), 0.25, A.mult)
+
+    def first(b):
+        tt(a("GN" + b, al, slice(0, 16 * wide(b)), 0, k="a"), ind(a("XS"), lst("LK", b)), wcols(lo_(b), hi_(b), b, 0), A.is_ge)
+        sums(b)
+
+    same = lambda b: tt(lst("cx", b), st("PO", 1, b), cols("cq", lo_(b), hi_(b)), A.is_equal)
+    flag = lambda b: tt(lst("cx", b), lst("cx", b), cols("cf", lo_(b), hi_(b)), A.mult)
+    addf = lambda b: tt(st("PO", 1, b), st("PO", 1, b), lst("cx", b), A.add)
+
+    def fro_lo():
+        tt(a("FL"), a("froc"), a("FH"), A.subtract)
+        put_info("y", 6, "FH")
+        put_info("y", 7, "FL")
+        deps("g", ["INFOg", "INFOh"], [])
+        sendx(1)
+    late_v = [lambda: ts(a("cd"), a("cr"), 4.0, A.mult), lambda: tt(a("cq"), a("cd"), a("cn"), A.subtract),
+              lambda: cp(st("PO", 1, ALL), a("cq")), lambda: ts(a("m2"), a("typc"), -1.0, A.mult, 2.0, A.add),
+              lambda: ts(a("LR", k=ALL), a("cr"), float(OFF), A.add), lambda: cp(a("FH"), a("froc")),
+              lambda: tt(a("ct"), cols("PA", 0, 48), a("m2"), A.mult),
+              lambda: ts(a("cf"), a("ct"), 1, A.arith_shift_right, 1, A.bitwise_and), fro_lo]
+
     bank = lambda bs: cols("Y0" if bs == HEAD else "Y1", 0, 16 * wide(bs))
     reclist = lambda bs: ts(lst("lr", bs), st("RR", 0, bs), 16380, A.bitwise_and)
     reccast = lambda bs: ts(lst("LR", bs), lst("lr", bs), 0.25, A.mult)
     fro_of = lambda bs: act(unit("RA", bs), ind(info(0), lst("LR", bs)), scale=wf)
     fcols = lambda bs: cols("F" + bs[0], 64, 64 + wide(bs))
-    foreign = lambda bs, rs: tolist(fcols(bs), lambda r: cols("RA", 16 * lo_(bs) + r, 16 * hi_(bs), k=bs, step=16), rs=rs)
+    foreign = lambda bs: tolist(fcols(bs), lambda r: cols("RA", 16 * lo_(bs) + r, 16 * hi_(bs), k=bs, step=16))
     forcast = lambda bs: cp(lst("LK", bs), fcols(bs))
     minus_w = lambda bs, t: mm(bank(bs), a("NI" if t else "NJ"), wcols(lo_(bs), hi_(bs), bs, t), True, False)
 
@@ -347,31 +378,43 @@ def rank_program(g, core, T, topo):
 
     for t in range(3):
         later = cast if t < 2 else lambda b: None
-        ops = {"r": read, "o": other, "p": pick, "m": mask, "c": lambda b: (cast(b), codes(b)), "g": lambda b: features(b, t, 0, SPLIT),
-               "h": lambda b: (features(b, t, SPLIT, wide(b)), sums(b)), "G": lambda b: (features(b, t, 0, wide(b)), sums(b)),
-               "d": differ, "l": later, "R": reclist, "C": lambda bs: (reccast(bs), fro_of(bs))}
+        got = {b: 0 for b in ALL}
+
+        def gather(b):
+            b, hi = (b[0], int(b[2:])) if len(b) > 1 else (b, wide(b))
+            features(b, t, got[b], hi)
+            got[b] = hi % wide(b)
+            if not got[b]:
+                sums(b)
+        ops = {"r": read, "o": other, "p": pick, "m": mask, "c": lambda b: (cast(b), codes(b)), "g": gather,
+               "d": differ, "l": later, "R": reclist, "C": lambda bs: (reccast(bs), fro_of(bs)), "x": build, "L": lambda n: late_v[int(n)](),
+               "F": first, "M": mcast, "s": same, "f": flag, "a": addf}
         for b in ALL:
             codes(b)
-            ops["G"](b)
+            if t:
+                gather(b)
+            else:
+                mlist(b)
         if t == 0:
-            tt(st("PO", 1, ALL), a("cq"), a("cf"), A.add)
-            cp(a("FH"), a("froc"))
-            for fn in late_s[:4]:
-                fn()
-            asel(a("U1"), a("BN"), [[-1, 128]], A.is_gt, 0.0, 0, 1)
-            asel(a("UW"), a("U1"), [[-1, 128]], A.not_equal, 1024.0, 0, 1)
-            sendx(1)
-        for q in range(3):
-            if q < 2:
-                minus_w((HEAD, TAIL)[q], t)
-            for tok in CYCLE.split():
+            act(piece("XN", 0), ind(a("XS"), lx(0)))
+            act(piece("XN", 1, 0, SHIFT, "c"), ind(a("XS"), lx(1, 0, SHIFT)))
+            for tok in START.split():
                 ops[tok[0]](tok[1:])
-                if t == 0 and q == 0 and tok == "r0":
-                    tt(a("FL"), a("froc"), a("FH"), A.subtract)
-                    put_info("y", 6, "FH")
-                    put_info("y", 7, "FL")
+        if t == 2:
+            dma("y", ext(T.yw[:, 0:16 * hi_(HEAD)], ["yw" + HEAD]), wcols(0, hi_(HEAD), HEAD, t))
+        for q in range(3):
+            if q < 2 and t:
+                minus_w((HEAD, TAIL)[q], t)
+            if q and not t:
+                minus_w((HEAD, TAIL)[q - 1], t)
+            for tok in (CYCLE if t else ROUND0[q]).split():
+                ops[tok[0]](tok[1:])
             if t == 0 and q == 0:
-                for fn in late_s[4:]:
+                late_s[0]()
+                act(a("RA", k=ALL), ind(info(0), a("LR", k=ALL)), scale=wm)
+                tolist(cols("PA", 0, 48), lambda r: cols("RA", r, K, k=ALL, step=16))
+            if t == 0 and q:
+                for fn in (late_s[1:2], late_s[2:])[q - 1]:
                     fn()
             if t == 2:
                 for part_ in ((), (2,), (3, 4))[q]:
@@ -383,7 +426,8 @@ def rank_program(g, core, T, topo):
         pull = lambda bs: act(unit("YG", bs), ind(a("XF%d" % t), lst("LK", bs)))
         meet = lambda bs: mm(bank(bs), a("I128"), unit("YG", bs), False, True)
 
-        cut = lambda bs: ts(bank(bs), bank(bs), 8.0, A.min, -8.0, A.max)
+        cut = lambda out, bs: ts(out, bank(bs), 8.0, A.min, -8.0, A.max)
+        yw = lambda bs: ext(T.yw[:, 16 * lo_(bs):16 * hi_(bs)], ["yw" + bs])
 
         def addw(bs, h):
             n = 8 * wide(bs)
@@ -391,81 +435,81 @@ def rank_program(g, core, T, topo):
             k = wkeys(bs)[h::2]
             tt(cols("WW", c, c + n, k=k), cols(bank(bs)[1][0], n * h, n * h + n), cols("WW" if t else "W0", c, c + n, k=k), A.add)
             if t == 2 and h == 1:
-                dma("y", ext(T.yw[:, 16 * lo_(bs):16 * hi_(bs)]), wcols(lo_(bs), hi_(bs), bs, t))
+                dma("y", yw(bs), wcols(lo_(bs), hi_(bs), bs, t))
         ts(a("tu"), lst("df", ALL), 16380, A.bitwise_and)
         ts(a("tf"), r0, 1, A.bitwise_and)
         reclist(TAIL)
-        mask(TAIL)
-        later(HEAD[-1])
         tt(a("wt"), a("tu"), a("tf"), A.min)
+        ts(a("RR", al, 2, al, k="t"), r0, 16384.0, A.add)
         reccast(TAIL)
-        ts(a("ta"), r0, 16384.0, A.add)
-        later(TAIL)
         scan(a("cs"), a("on"), a("wt"), A.mult, A.add)
+        ts(a("WP", al, al, slice(0, 48), k="a"), (T.RR[:, 1:3], r1[1] + ["RRt"]), 32767, A.bitwise_and, 2, A.arith_shift_right)
         ts(unit("RA", TAIL), ind(info(0), lst("LR", TAIL)), wf, A.mult)
-        mm(cols("PE", 128, 176), a("UW"), a("wt"), True, False)
-        foreign(HEAD, range(6))
+        mm(cols("PE", 256, 304), a("UW"), a("wt"), True, False)
         mm(cols("PA", 0, 48), a("BL"), a("cs"))
-        mm(cols("PE", 128, 176), a("BL"), a("cs"), False, True)
-        foreign(HEAD, range(6, 16))
+        mm(cols("PE", 256, 304), a("BL"), a("cs"), False, True)
+        foreign(HEAD)
         for k in range(6):
             act(cols("SG", 48 * k, 48 * k + 48, k=AZ[k]), cols("PA", 0, 48), scale=-1.0, bias=cols("kb", k, k + 1), acc=col("CA", k), fn=F.Sign)
-        foreign(TAIL, range(16))
-        ts(cols("W2", 0, 48, k="a"), r1, 32767, A.bitwise_and, 2, A.arith_shift_right)
-        ts(cols("W1", 0, 48, k="a"), a("ta"), 32767, A.bitwise_and, 2, A.arith_shift_right)
-        cp(cols("RK", 0, 48, k="a"), cols("PE", 128, 176))
-        mm(cols("PE", 0, 96), part("M16", 0, 16), part("CD2", 0, 16), True, False)
+        foreign(TAIL)
+        cp(cols("RK", 0, 48, k="a"), cols("PE", 256, 304))
+        mm(cols("PE", 0, 192), part("M16", 0, 16), part("CD2", 0, 16), True, False)
         forcast(HEAD)
         pull(HEAD)
         meet(HEAD)
         ts(a("LC"), a("CA", k=AZ[:6]), 48.0, A.add, 0.5, A.mult)
-        if t == 2:
-            ts(a("ya"), a("PO", k=[j + b for j in "01" for b in ALL]), 2, A.arith_shift_right)
+        state = lambda nm: a(nm, al, slice(0, 2), al, k=[j + b for j in "01" for b in ALL])
+        ts(state("PO"), state("RR"), 32765 if t < 2 else 32764, A.bitwise_and)
+        tt(a("MK"), ind(a("RK", k="az"), a("LC")), a("KC"), A.is_equal)
         forcast(TAIL)
         pull(TAIL)
-        tt(a("MK"), ind(a("RK", k="az"), a("LC")), a("KC"), A.is_equal)
-        if t == 2:
-            tt(a("cd"), cols("ya", 0, 48), cols("ya", 48, 96), A.min)
-            tt(a("cx"), cols("ya", 0, 48), cols("ya", 48, 96), A.max)
+        if t < 2:
+            cast(ALL)
+        else:
+            tt(a("cd"), st("PO", 0, ALL), st("PO", 1, ALL), A.min)
         for w in range(2):
-            tt(w96("MV", w, str(w)), ind(a("W%d" % (w + 1), k="az"), a("LC")), a("MK"), A.mult)
-        for nm, w in (("PD", 0), ("PA", 0), ("PD", 1), ("PA", 1)):
-            mm(w96(nm, w), a("BF"), w96("MV", w, str(w)), nm == "PA", nm == "PA" or w == 1)
+            tt(w96("MV", w, str(w)), ind(a("WP", al, 1 - w, al, k="az"), a("LC")), a("MK"), A.mult)
+        for nm, w in (("PD", 0), ("PD", 1), ("PA", 0), ("F2", 1)):
+            mm(w96(nm, w), a("BF"), w96("MV", w, str(w)), nm != "PD", nm != "PD" or w == 1)
         meet(TAIL)
-        cut(HEAD)
+        cut(unit("DD", HEAD) if t == 2 else bank(HEAD), HEAD)
         if t == 2:
-            ts(cols("yco", 0, 48, k="0"), a("cd"), -float(at(0)), A.add)
-            ts(cols("yco", 48, 96, k="1"), a("cx"), -float(at(1)), A.add)
+            dma("g", yw(HEAD), unit("DD", HEAD), accum_op=A.add)
+            tt(a("cx"), st("PO", 0, ALL), st("PO", 1, ALL), A.max)
+        scan(cols("DB", 1, 384, k="o", step=2), a("DA"), cols("PD", 0, 192), A.min, A.max)
+        cp(w96("RU", 0, "0"), w96("PA", 0))
+        cp(w96("RU", 1, "1"), w96("F2", 1))
+        cp(a("LE0"), cols("DB", 31, 384, k="o", step=32))
+        if t < 2:
+            addw(HEAD, 0)
+        else:
+            ts(cols("yco", 0, 48, k="0"), a("cd"), 0.25, A.mult, -float(at(0)), A.add)
+            ts(cols("yco", 48, 96, k="1"), a("cx"), 0.25, A.mult, -float(at(1)), A.add)
             dma("y", ext(T.yc[:]), a("yco", k="01"))
-        addw(HEAD, 0)
-        scan(a("LS"), a("DA"), cols("PD", 0, 192), A.max, A.min)
-        cp(a("RU"), cols("PA", 0, 192))
-        addw(HEAD, 1)
-        cp(a("LE0"), cols("LS", 15, 192, step=16))
         for nm, win in (("gx", XN), ("gn", NX))[t // 2:]:
             for w in range(2):
                 act(w96(nm, 1 - w, str(w)), ind(win, cols("LE0", 6 * w, 6 * w + 6)))
         if t == 0:
             sendx(2)
         for e in range(12):
-            ts(cols("EQ", 192 * e, 192 * e + 192, k=AZ[e]), a("RU"), cols("LS", 16 * e + 15, 16 * e + 16), A.is_equal)
+            ts(cols("EQ", 192 * e, 192 * e + 192, k=AZ[e]), a("RU", k="01"), cols("DB", 32 * e + 31, 32 * e + 32, k="o"), A.is_equal)
             for w in range(2):
-                mm(cols("PE", 0, 96), a("BK"), cols("EQ", 192 * e + 96 * w, 192 * e + 96 * w + 96, k=AZ[e]), False, e == 11 and w == 1)
-        cut(TAIL)
+                mm(cols("PE", 0, 192, step=2), a("BK"), cols("EQ", 192 * e + 96 * w, 192 * e + 96 * w + 96, k=AZ[e]), False, e == 11 and w == 1)
+        cut(bank(TAIL), TAIL)
+        if t < 2:
+            addw(HEAD, 1)
         for w in range(2):
-            scan(w96("QQ", w, str(w)), w96("DB", w), cols("PE", 0, 96), A.max, A.min)
+            scan(cols("QQ", 192 * w, 192 * w + 192, k=str(w)), cols("DB", 192 * w, 192 * w + 192, k="eo"), cols("PE", 0, 192), A.max, A.min)
         addw(TAIL, 0)
-        tt(a("LQ"), cols("LS", 15, 192, step=16), cols("QQ", 15, 192, k="01", step=16), A.max)
+        cp(a("LE1"), cols("QQ", 31, 384, k="01", step=32))
         addw(TAIL, 1)
-        cp(a("LE1"), a("LQ"))
         if t < 2:
             put("s", NX, a("LE1"), a("gn", k="01"))
-            put("v", XN, a("LE1"), a("gx", k="01"))
-            if t == 1:
-                next_out(0)
-                next_out(1)
-        else:
-            put("v", NX, a("LE1"), a("gn", k="01"))
+        put("v", XN if t < 2 else NX, a("LE1"), a("gx" if t < 2 else "gn", k="01"))
+        if t == 1:
+            next_out(0)
+            next_out(1)
+        if t == 2:
             for s in range(2):
                 dma("ys"[s], ext(T.yn[:, W * s:W * s + W]), rows("NX", 0, at(s), at(s) + W, NX[1]))
     for sem, val in total.items():

from concourse.mybir import AluOpType as A, ActivationFunctionType as F

W, K, OFF, TY, DUM, PL = 3072, 768, 64, 4096, 7232, 7424
KK = 262144.0
RND = 12582912.0
CUT = (0, 24, 48)
ALL = "012"[:len(CUT) - 1]
HEAD, TAIL = ALL[:-1], ALL[-1]
CYCLE = "r0 o0 p0 r1 m0 o1 p1 c0 m1 g0:10 c1 g0 g1"
FINAL = "r0 p0 d0 o0 r1 R0 d1 p1 C0 o1"
SHIFT = 320
START = "L0 x1408 L1 M0 x192 M1 L2 F0 F1 x384"
ROUND0 = ("r0 x192 o0 p0 r1 x128 m0 o1 p1 x160 c0 x m1 L4 c1 g0 g1",
          "L3 L5 r0 o0 p0 r1 m0 o1 p1 c0 m1 g0:10 c1 g0 g1 L6",
          "L8 r0 L7 o0 p0 r1 m0 o1 p1 c0 s0 m1 g0:10 c1 f0 s1 g0 a0 f1 g1 a1")
F4, B2, I4, U2 = "float32", "bfloat16", "int32", "uint16"
SCRATCH = {}
for names, shape, dtype in (
        ("XS XF0 XF1 XF2", [W], B2), ("XN", [PL], B2), ("NX", [PL], F4), ("INFO", [OFF + W], B2), ("WW DD", [K], F4),
        ("NB", [2, 192], I4), ("NF", [12, 2, 16], F4), ("FT", [12, 32], F4), ("LX", [384], U2),
        ("memc froc m0", [192], I4), ("curc ya", [96], I4), ("typc c1 cd cx cp cq cr m2 ct cf df tu tf ta lr", [48], I4), ("yco", [96], F4),
        ("HI LO B1 B0 FH FL hb", [192], B2), ("GN0 GN1 GN2", [512, 2], B2), ("RA YG W0", [K], B2),
        ("RR", [3, 48], I4), ("PO", [2, 48], I4), ("YY", [48], F4), ("ZO XX0 XX1 XX2", [64], F4), ("CK Ca Cb", [64], B2), ("LP LR LK", [48], U2),
        ("pc", [4], I4), ("pf", [8], F4), ("co", [24], F4), ("WB WC Wa Wb", [144], B2), ("cn", [48], B2),
        ("BL BN BK UW U1 U2 I128 ON O1 NJ M16 Ba", [128], B2), ("BF NI", [128], F4),
        ("KC MK", [96], F4), ("kb kb0 CA", [6], F4), ("CD0 CD1 CD2 CD3", [192], B2), ("DA D1 D2", [192], F4),
        ("on wt cs", [48], B2), ("SG", [288], F4), ("LC", [6], U2), ("RK", [64], F4), ("WP", [2, 64], I4),
        ("MV gn", [192], F4), ("QQ DB", [384], F4), ("RU", [192], U2), ("EQ", [2304], B2), ("LE0 LE1", [12], U2),
        ("gx", [192], B2), ("NC NC2 NC3", [384], F4)):
    for nm in names.split():
        SCRATCH[nm] = ("sbuf", [128] + shape, dtype)
PSUMS = ("F0", "F1", "F2", "PA", "PD", "PE", "Y0", "Y1")
for nm in PSUMS:
    SCRATCH[nm] = ("psum", [128, 512], F4)
SEMAPHORES = ["qv", "qp", "qs", "qg", "xl", "xa0", "xa1", "xa2", "rows"] + ["e%d" % k for k in range(14)] + ["d%d" % k for k in range(30)]
AZ = "abcdefghijklmnopqrstuvwxyzABCDEF"


def rank_program(g, core, T, topo):
    rank = T.rank_of(core)
    if rank is None:
        return
    eng = {"v": g.vector, "p": g.tensor, "s": g.scalar, "g": g, "y": g.sync}
    total, snap, last, reads, nd = {}, {}, {}, {}, {"d": 0, "e": 0}
    know = {q: {} for q in eng}

    def a(name, *idx, k=""):
        t = T[name]
        return (t[idx] if idx else t[:], [name + c for c in k] if k else [name])

    def ind(win, off):
        return (win[0].indirect(off[0]), win[1] + off[1])

    def need(q, sem, val):
        kn = know[q]
        if kn.get(sem, 0) >= val:
            return
        eng[q].wait_ge(T.sem[sem], val)
        for s2, v2 in snap.get((sem, val), {}).items():
            kn[s2] = max(kn.get(s2, 0), v2)
        kn[sem] = max(kn.get(sem, 0), val)

    def deps(q, rd, wr):
        for key in rd + wr:
            w = last.get(key)
            if w is not None and not (w[2] == q and key not in rd and w[0][0] == "q"):
                need(q, w[0], w[1])
            if key in PSUMS or key in wr:
                for s2, (v2, q2) in list(reads.get(key, {}).items()):
                    if q2 != q or s2[0] in "dex" or key in wr:
                        need(q, s2, v2)

    def done(q, sem, val, rd, wr):
        m = dict(know[q])
        m[sem] = val
        snap[(sem, val)] = m
        for key in wr:
            last[key] = (sem, val, q)
            reads[key] = {}
        for key in rd:
            if key not in wr:
                reads.setdefault(key, {})[sem] = (val, q)

    def run(q, fn, outs, ins):
        rd = [x for i in ins for x in i[1]]
        wr = [x for o in outs for x in o[1]]
        deps(q, rd, wr)
        sem = "q" + q
        total[sem] = total.get(sem, 0) + 1
        fn().then_inc(T.sem[sem], 1)
        done(q, sem, total[sem], rd, wr)

    def dma(q, out, in_, **kw):
        for key in out[1]:
            if key in last:
                need(q, last[key][0], last[key][1])
        deps(q, in_[1], out[1])
        c = "e" if q == "g" else "d"
        sem = "%s%d" % (c, nd[c])
        nd[c] += 1
        total[sem] = 16
        eng[q].dma_start(out[0], in_[0], **kw).then_inc(T.sem[sem], 16)
        done(q, sem, 16, in_[1], out[1])

    def tt(out, i0, i1, op):
        run("v", lambda: g.vector.tensor_tensor(out[0], i0[0], i1[0], op), [out], [i0, i1])

    def ts(out, i0, s1, op0, s2=None, op1=None):
        ins = [i0] + [s for s in (s1, s2) if isinstance(s, tuple)]
        x1 = s1[0] if isinstance(s1, tuple) else s1
        x2 = s2[0] if isinstance(s2, tuple) else s2
        more = [x2, op0] if op1 is None else [x2, op0, op1]
        run("v", lambda: g.vector.tensor_scalar(out[0], i0[0], x1, *more), [out], ins)

    def cp(out, i0):
        run("v", lambda: g.vector.tensor_copy(out[0], i0[0]), [out], [i0])

    def fill(out, v):
        run("v", lambda: g.vector.memset(out[0], v), [out], [])

    def scan(out, d0, d1, op0, op1):
        run("v", lambda: g.vector.tensor_tensor_scan(out[0], d0[0], d1[0], 0.0, op0, op1), [out], [d0, d1])

    def act(out, i0, scale=None, bias=None, acc=None, fn=None):
        kw, ins, outs = {}, [i0], [out]
        for nm, x in (("scale", scale), ("bias", bias)):
            if isinstance(x, tuple):
                ins.append(x)
                kw[nm] = x[0]
            elif x is not None:
                kw[nm] = x
        if acc is not None:
            outs.append(acc)
            kw["accum_out"] = acc[0]
        fn = fn or (F.Identity if isinstance(bias, tuple) else F.Copy)
        run("s", lambda: g.scalar.activation(out[0], i0[0], fn, **kw), outs, ins)

    def mm(out, lhsT, rhs, start=True, stop=True):
        run("p", lambda: g.tensor.matmul(out[0], lhsT[0], rhs[0], start, stop), [out], [lhsT, rhs])

    def iota(out, pattern, base, cm=0, whole=False):
        kw = {} if whole else {"allow_small_or_imprecise_dtypes": True}
        run("g", lambda: g.iota(out[0], pattern, base, cm, **kw), [out], [])

    def asel(out, in_, pattern, op, fill_, base, cm):
        run("g", lambda: g.affine_select(out[0], in_[0], pattern, op, fill_, base, cm), [out], [in_])

    def put(q, win, off, src):
        dst = win[0].indirect(off[0])
        if q == "v":
            run("v", lambda: g.vector.tensor_copy(dst, src[0]), [win], [src, off])
        else:
            run("s", lambda: g.scalar.activation(dst, src[0], F.Silu), [win], [src, off])

    ext = lambda ap, k=(): (ap, list(k))
    al = slice(None)
    cols = lambda nm, lo, hi, k="", step=1: a(nm, al, slice(lo, hi, step), k=k)
    col = lambda nm, j: a(nm, al, slice(j, j + 1), k=AZ[j])
    lo_, hi_ = lambda bs: CUT[int(bs[0])], lambda bs: CUT[int(bs[-1]) + 1]
    wide = lambda bs: hi_(bs) - lo_(bs)
    lst = lambda nm, bs: cols(nm, lo_(bs), hi_(bs), k=bs)
    unit = lambda nm, bs: cols(nm, 16 * lo_(bs), 16 * hi_(bs), k=bs)
    w96 = lambda nm, w, k="": cols(nm, 96 * w, 96 * w + 96, k=k)
    rows = lambda nm, r, lo, hi, k: (T[nm][r:128:16, lo:hi], k)
    at = lambda s: OFF + TY * s
    skip = lambda: None
    pads = list(zip("xyz", ((0, OFF), (OFF + W, at(1)), (DUM, PL))))

    def tolist(out, rhs, start=True, wts="WB"):
        for r in range(16):
            mm(out, cols(wts, 15 - r, 143 - r), rhs(r), start and r == 0, r == 15)

    dma("y", a("memc"), ext(T.mem[:]))
    for h in range(2):
        dma("sy"[h], a("NB", al, h, al, k=str(h)), ext(T.nxt[h:8:2, :]))
    dma("s", a("curc"), ext(T.cur[:]))
    dma("s", a("typc"), ext(T.typ[:]))

    iota(col("pc", 0), [[0, 1]], 0, 1, True)
    iota(a("hb"), [[256, 3], [0, 64]], 0)
    iota(a("LO"), [[0, 3], [4, 64]], 4 * OFF)
    fill(cols("INFO", 0, 1024, k="p"), 0.0)
    ts(col("pc", 1), col("pc", 0), 15, A.bitwise_and)
    fill(cols("INFO", 1024, 2048, k="q"), 0.0)
    pm = col("pf", 1)
    ts(col("pf", 4), col("pc", 1), 768.0, A.mult)
    cp(pm, col("pc", 1))
    fill(cols("INFO", 2048, OFF + W, k=AZ[:8]), 0.0)
    ts(a("HI"), a("hb"), col("pf", 4), A.add)
    sc0, sc1, bi0, gsc, wf, wm = [col("co", j) for j in range(6)]
    cc = lambda j: col("co", j)
    u = 1 / KK / 65536
    for j, fn, scale, bias in ((6, F.Sign, -1.0, 3.5), (7, F.Sign, 1.0, -1.5), (8, F.Abs, 1.0, -2.0), (9, F.Abs, 1.0, -2.5),
                               (10, F.Sign, 1.0, -5.5), (11, F.Abs, 1.0, -4.0), (12, F.Abs, 1.0, -1.0)):
        act(cc(j), pm, scale=scale, bias=bias, fn=fn)
    for out, j, fn, scale, bias in ((sc0, 6, F.Relu, 1.0, 0.0), (sc1, 7, F.Relu, 1.0, 0.0), (bi0, 8, F.Relu, -4.0 * TY, 4.0 * TY),
                                    (cc(13), 9, F.Sign, -1.0, 1.0), (cc(14), 9, F.Sign, -1.0, 2.0), (wf, 10, F.Relu, 1 / KK, 0.0),
                                    (cc(15), 11, F.Relu, -u, u), (cc(16), 12, F.Relu, -2 * u, 2 * u)):
        act(out, cc(j), scale=scale, bias=bias, fn=fn)
    pad = lambda k, lo, hi: [act(cols("NX", c, min(c + 192, hi), k=k), cols("hb", 0, min(192, hi - c)), scale=0.0) for c in range(lo, hi, 192)]
    for k, (lo, hi) in pads[::2]:
        pad(k, lo, hi)
    put_info = lambda q, r, nm: dma(q, rows("INFO", r, OFF, OFF + W, ["INFO" + AZ[r]]), a(nm))
    ts(a("m0"), a("memc"), 1, A.bitwise_and)
    ts(a("B1"), a("memc"), 2.0, A.is_ge, 65536.0, A.mult)
    ts(a("B0"), a("m0"), 65536.0, A.mult)
    for q, r, nm in (("y", 3, "LO"), ("y", 2, "HI"), ("s", 0, "B1"), ("y", 1, "B1"), ("s", 4, "B0"), ("y", 5, "B0")):
        put_info(q, r, nm)
    g.scalar.sem_inc(T.sem.rows, 1)
    g.sync.wait_ge(T.sem.rows, 1)
    dma("y", a("XS"), ext(T.x[:]))
    dma("y", a("W0", k=[b + h for b in ALL for h in "ab"]), ext(T.w0[:]))
    dma("y", cols("XN", OFF + W, at(1), k="y"), ext(T.x[:, 0:TY - W]))
    dma("y", a("froc"), ext(T.fro[:]))
    act(cc(17), cc(13), fn=F.Relu)
    act(gsc, cc(14), scale=(1 / KK - u) / 2, bias=(1 / KK + u) / 2)
    pad("y", OFF + W, at(1))

    cur0, cur1 = cols("curc", 0, 48), cols("curc", 48, 96)
    for h in range(2):
        cp(a("NF", al, al, h, al, k=str(h)), a("NB", al, h, al, k=str(h)))
    tt(a("cd"), cur1, cur0, A.subtract)
    ts(a("c1"), a("typc"), float(TY), A.mult, float(OFF), A.add)
    run("v", lambda: g.vector.transpose(T.FT[:], T.NF[:]), [a("FT")], [a("NF", k="01")])
    tt(a("cx"), a("cd"), a("typc"), A.mult)
    tt(a("c1"), a("c1"), cur0, A.add)
    ts(a("cn"), a("typc"), 4.0 * TY, A.mult, -4.0 * at(1), A.add)
    for b in range(12):
        cp(cols("LX", b, 384, k=AZ[b], step=12), a("FT", al, b, al))
        if b == 1:
            tt(a("cp"), a("c1"), a("cx"), A.add)
    cp(a("LP", k=ALL), a("cp"))
    tt(a("cr"), cur1, a("cx"), A.subtract)

    group = lambda out, in_, tmp, n: (asel(tmp, in_, [[-16, n], [0, 16]], A.is_ge, 0.0, 0, 1), asel(out, tmp, [[16, n], [0, 16]], A.is_ge, 0.0, 15, -1))
    part = lambda nm, lo, hi, k="": a(nm, slice(lo, hi), al, k=k)
    iota(a("Wa"), [[0, 144]], int(KK))
    asel(a("Wb"), a("Wa"), [[0, 9], [1, 16]], A.is_equal, 0.0, -15, 0)
    group(a("WB"), a("Wb"), a("Wa"), 9)
    iota(a("O1"), [[0, 128]], 1)
    iota(a("Ca"), [[0, 32], [17024, 2]], -17280)
    asel(a("ON"), a("O1"), [[0, 128]], A.is_ge, 2.0, -64, 1)
    asel(a("Cb"), a("Ca"), [[0, 64]], A.is_ge, 0.0, 63, -1)
    iota(a("ZO"), [[0, 32], [1, 2]], 0)
    asel(a("CK"), a("Cb"), [[0, 64]], A.not_equal, 1.0, -64, 1)
    asel(a("I128"), a("O1"), [[-1, 128]], A.is_equal, 0.0, 0, 1)
    for k, (lo, hi) in pads[::2]:
        iota(cols("XN", lo, hi, k=k), [[0, hi - lo]], 0)

    def sendx(t):
        deps("g", ["XS"], [])
        if t:
            need("g", "xl", total["xl"])
        dst = T.cores[(rank - 1 - t) % 8]
        rid, pid = topo.addr(dst, core)
        n = len(topo.engines(core, dst))
        sem = "xa%d" % t
        total["xl"] = total.get("xl", 0) + n
        total[sem] = n
        g.remote_dma(T["XF%d" % t][:], T.XS[:], T.sem[sem], T.sem.xl, pid, rid, topo.mask(core, dst))
        last["XF%d" % t] = (sem, n, "-")
    asel(a("Ba"), a("O1"), [[-16, 8], [0, 16]], A.is_ge, 0.0, 0, 1)
    iota(a("BN"), [[0, 128]], -1)
    asel(a("BL"), a("Ba"), [[16, 8], [0, 16]], A.is_ge, 0.0, 15, -1)
    sendx(0)
    iota(a("D1"), [[96, 2], [16, 6], [0, 16]], DUM)
    iota(a("kb0"), [[16, 6]], 0)
    asel(a("U1"), a("BN"), [[-1, 128]], A.is_gt, 0.0, 0, 1)
    asel(a("D2"), a("D1"), [[0, 12], [1, 16]], A.is_equal, -65536.0, 0, 0)
    asel(a("U2"), a("U1"), [[16, 8], [0, 16]], A.is_ge, 0.0, 15, -1)
    iota(a("CD3"), [[0, 192]], -65536)
    asel(a("UW"), a("U2"), [[-1, 128]], A.not_equal, 1024.0, 0, 1)
    asel(a("M16"), a("O1"), [[0, 8], [1, 16]], A.is_equal, 0.0, 0, -1)
    asel(a("CD1"), a("CD3"), [[0, 12], [1, 16]], A.not_equal, 0.0, 0, -1)
    iota(a("CD0"), [[0, 192]], 65536)
    iota(a("KC"), [[1, 96]], 1025)
    asel(a("CD2"), a("CD0"), [[0, 6], [1, 16], [1000, 2]], A.not_equal, -40960.0, 0, -1)
    asel(a("DA"), a("CD0"), [[0, 12], [1, 16]], A.not_equal, -1.0, 0, 0)
    iota(a("on"), [[0, 48]], 1)
    iota(cols("RK", 48, 64, k="z"), [[0, 16]], 0)
    iota(a("WP", al, al, slice(48, 64), k="z"), [[0, 32]], 0, 0, True)

    lx = lambda s, lo=0, hi=W: cols("LX", 192 * s + lo // 16, 192 * s + hi // 16, k=AZ[:12])
    piece = lambda nm, s, lo=0, hi=W, k="": cols(nm, at(s) + lo, at(s) + hi, k=k or "ab"[s])
    info = lambda lo: cols("INFO", lo, OFF + W, k=AZ[:8] + "pq")
    act(a("WC"), a("WB"), scale=cc(17))
    act(piece("NX", 0), ind(info(OFF), lx(0)), scale=sc0, bias=bi0)
    ts(piece("NX", 1), ind(info(OFF), lx(1)), sc1, A.mult)
    XN, NX = a("XN", k="abcxyz"), a("NX", k="abxyz")
    built = [SHIFT]

    def build(n):
        lo = built[0]
        built[0] = hi = lo + int(n) if n else W
        cp(piece("XN", 1, lo, hi), ind(a("XS"), lx(1, lo, hi)))
    late_s = [lambda: (act(wm, cc(15), bias=cc(16)), act(a("NI"), a("I128"), scale=-1.0), act(a("NJ"), a("I128"), scale=-1.0)),
              lambda: act(a("BK"), a("BL"), scale=16384.0, fn=F.Silu), lambda: act(col("pf", 5), pm, bias=0.5), lambda: act(a("BF"), a("BL")),
              lambda: act(cols("DB", 0, 384, k="e", step=2), a("D2"), bias=pm), lambda: act(a("kb"), a("kb0"), bias=col("pf", 5))]

    st = lambda nm, j, bs: a(nm, al, j, slice(lo_(bs), hi_(bs)), k=[str(j) + b for b in bs])
    both = lambda nm, b: a(nm, al, slice(0, 2), slice(lo_(b), hi_(b)), k=["0" + b, "1" + b])
    xx = lambda b: cols("XX" + b, 1, 2 * wide(b), step=2)
    wkeys = lambda bs: [b + h for b in bs for h in "ab"]
    wcols = lambda lo, hi, bs, t: cols("WW" if t else "W0", 16 * lo, 16 * hi, k=wkeys(bs))

    def features(b, t, lo, hi):
        c = lo_(b)
        tt(a("GN" + b, al, slice(16 * lo, 16 * hi), 0, k="a"), ind(XN, cols("LP", c + lo, c + hi, k=b)),
           wcols(c + lo, c + hi, b, t), A.is_ge)

    def codes(b):
        act(a("GN" + b, al, slice(0, 16 * wide(b)), 1, k="b"), ind(NX, lst("LP", b)), scale=gsc)

    def sums(b):
        Fb = cols("F" + b, 0, 2 * wide(b))
        mm(Fb, a("ON"), cols("CK", 0, 2 * wide(b)), True, False)
        tolist(Fb, lambda r: a("GN" + b, al, slice(r, 16 * wide(b), 16), al, k="ab"), start=False)

    def read(b):
        n = 2 * wide(b)
        scan(cols("XX" + b, 0, n), cols("ZO", 0, n), cols("F" + b, 0, n), A.mult, A.add)
        tt(lst("YY", b), cols("F" + b, 1, n, step=2), st("PO", 1, b), A.max)

    other = lambda b: tt(st("RR", 1, b), xx(b), st("PO", 1, b), A.max)
    pick = lambda b: tt(st("RR", 0, b), xx(b), lst("YY", b), A.min)
    differ = lambda b: tt(lst("df", b), xx(b), st("PO", 1, b), A.subtract)
    mask = lambda b: ts(both("PO", b), both("RR", b), 32765, A.bitwise_and)
    cast = lambda b: ts(lst("LP", b), st("PO", 0, b), 0.25, A.mult)

    def mlist(b):
        out = cols(("PA", "PD", "PE")[int(b)], 0, wide(b))
        mm(out, a("I128"), cols("cn", lo_(b), hi_(b)), True, False)
        tolist(out, lambda r: a("GN" + b, al, slice(r, 16 * wide(b), 16), 1, k="b"), start=False, wts="WC")
    mcast = lambda b: ts(lst("LK", b), cols(("PA", "PD", "PE")[int(b)], 0, wide(b)), 0.25, A.mult)

    def first(b):
        tt(a("GN" + b, al, slice(0, 16 * wide(b)), 0, k="a"), ind(a("XS"), lst("LK", b)), wcols(lo_(b), hi_(b), b, 0), A.is_ge)
        sums(b)

    same = lambda b: tt(lst("cx", b), st("PO", 1, b), cols("cq", lo_(b), hi_(b)), A.is_equal)
    flag = lambda b: tt(lst("cx", b), lst("cx", b), cols("cf", lo_(b), hi_(b)), A.mult)
    addf = lambda b: tt(st("PO", 1, b), st("PO", 1, b), lst("cx", b), A.add)

    def fro_lo():
        tt(a("FL"), a("froc"), a("FH"), A.subtract)
        put_info("y", 6, "FH")
        put_info("y", 7, "FL")
        deps("g", ["INFOg", "INFOh"], [])
        sendx(1)
    late_v = [lambda: ts(a("cd"), a("cr"), 4.0, A.mult), lambda: tt(a("cq"), a("cd"), a("cn"), A.subtract),
              lambda: cp(st("PO", 1, ALL), a("cq")), lambda: ts(a("m2"), a("typc"), -1.0, A.mult, 2.0, A.add),
              lambda: ts(a("LR", k=ALL), a("cr"), float(OFF), A.add), lambda: cp(a("FH"), a("froc")),
              lambda: tt(a("ct"), cols("PA", 0, 48), a("m2"), A.mult),
              lambda: ts(a("cf"), a("ct"), 1, A.arith_shift_right, 1, A.bitwise_and), fro_lo]

    bank = lambda bs: cols("Y0" if bs == HEAD else "Y1", 0, 16 * wide(bs))
    reclist = lambda bs: ts(lst("lr", bs), st("RR", 0, bs), 16380, A.bitwise_and)
    reccast = lambda bs: ts(lst("LR", bs), lst("lr", bs), 0.25, A.mult)
    fro_of = lambda bs: act(unit("RA", bs), ind(info(0), lst("LR", bs)), scale=wf)
    fcols = lambda bs: cols("F" + bs[0], 64, 64 + wide(bs))
    foreign = lambda bs: tolist(fcols(bs), lambda r: cols("RA", 16 * lo_(bs) + r, 16 * hi_(bs), k=bs, step=16))
    forcast = lambda bs: cp(lst("LK", bs), fcols(bs))
    minus_w = lambda bs, t: mm(bank(bs), a("NI" if t else "NJ"), wcols(lo_(bs), hi_(bs), bs, t), True, False)

    def next_out(part):
        for s in range(2):
            nc = lambda nm: cols(nm, 192 * s, 192 * s + 192, k=str(s))
            if part == 0:
                dma("y", nc("NC"), rows("NX", 2, at(s), at(s) + W, NX[1]))
            elif part == 1:
                dma("g", nc("NC"), rows("NX", 3, at(s), at(s) + W, NX[1]), accum_op=A.add)
            elif part == 2:
                act(nc("NC2"), nc("NC"), scale=0.25, bias=RND - OFF - TY * (1 - s))
            elif part == 3:
                act(nc("NC3"), nc("NC2"), bias=-RND)
            else:
                dma("y", rows("NX", 0, at(s), at(s) + W, ["NX" + "ab"[s]]), nc("NC3"))

    for t in range(3):
        later = cast if t < 2 else lambda b: None
        got = {b: 0 for b in ALL}

        def gather(b):
            b, hi = (b[0], int(b[2:])) if len(b) > 1 else (b, wide(b))
            features(b, t, got[b], hi)
            got[b] = hi % wide(b)
            if not got[b]:
                sums(b)
        ops = {"r": read, "o": other, "p": pick, "m": mask, "c": lambda b: (cast(b), codes(b)), "g": gather,
               "d": differ, "l": later, "R": reclist, "C": lambda bs: (reccast(bs), fro_of(bs)), "x": build, "L": lambda n: late_v[int(n)](),
               "F": first, "M": mcast, "s": same, "f": flag, "a": addf}
        for b in ALL:
            codes(b)
            if t:
                gather(b)
            else:
                mlist(b)
        if t == 0:
            act(piece("XN", 0), ind(a("XS"), lx(0)))
            act(piece("XN", 1, 0, SHIFT, "c"), ind(a("XS"), lx(1, 0, SHIFT)))
            for tok in START.split():
                ops[tok[0]](tok[1:])
        if t == 2:
            dma("y", ext(T.yw[:, 0:16 * hi_(HEAD)], ["yw" + HEAD]), wcols(0, hi_(HEAD), HEAD, t))
        for q in range(3):
            if q < 2 and t:
                minus_w((HEAD, TAIL)[q], t)
            if q and not t:
                minus_w((HEAD, TAIL)[q - 1], t)
            for tok in (CYCLE if t else ROUND0[q]).split():
                ops[tok[0]](tok[1:])
            if t == 0 and q == 0:
                late_s[0]()
                act(a("RA", k=ALL), ind(info(0), a("LR", k=ALL)), scale=wm)
                tolist(cols("PA", 0, 48), lambda r: cols("RA", r, K, k=ALL, step=16))
            if t == 0 and q:
                for fn in (late_s[1:2], late_s[2:])[q - 1]:
                    fn()
            if t == 2:
                for part_ in ((), (2,), (3, 4))[q]:
                    next_out(part_)
        r0, r1 = st("RR", 0, ALL), st("RR", 1, ALL)
        for tok in FINAL.split():
            ops[tok[0]](tok[1:])
        mm(cols("PD", 0, 192), part("M16", 0, 16), part("CD1", 0, 16), True, False)
        pull = lambda bs: act(unit("YG", bs), ind(a("XF%d" % t), lst("LK", bs)))
        meet = lambda bs: mm(bank(bs), a("I128"), unit("YG", bs), False, True)

        cut = lambda out, bs: ts(out, bank(bs), 8.0, A.min, -8.0, A.max)
        yw = lambda bs: ext(T.yw[:, 16 * lo_(bs):16 * hi_(bs)], ["yw" + bs])

        def addw(bs, h):
            n = 8 * wide(bs)
            c = 16 * lo_(bs) + n * h
            k = wkeys(bs)[h::2]
            tt(cols("WW", c, c + n, k=k), cols(bank(bs)[1][0], n * h, n * h + n), cols("WW" if t else "W0", c, c + n, k=k), A.add)
            if t == 2 and h == 1:
                dma("y", yw(bs), wcols(lo_(bs), hi_(bs), bs, t))
        ts(a("tu"), lst("df", ALL), 16380, A.bitwise_and)
        ts(a("tf"), r0, 1, A.bitwise_and)
        reclist(TAIL)
        tt(a("wt"), a("tu"), a("tf"), A.min)
        ts(a("RR", al, 2, al, k="t"), r0, 16384.0, A.add)
        reccast(TAIL)
        scan(a("cs"), a("on"), a("wt"), A.mult, A.add)
        ts(a("WP", al, al, slice(0, 48), k="a"), (T.RR[:, 1:3], r1[1] + ["RRt"]), 32767, A.bitwise_and, 2, A.arith_shift_right)
        ts(unit("RA", TAIL), ind(info(0), lst("LR", TAIL)), wf, A.mult)
        mm(cols("PE", 256, 304), a("UW"), a("wt"), True, False)
        mm(cols("PA", 0, 48), a("BL"), a("cs"))
        mm(cols("PE", 256, 304), a("BL"), a("cs"), False, True)
        foreign(HEAD)
        for k in range(6):
            act(cols("SG", 48 * k, 48 * k + 48, k=AZ[k]), cols("PA", 0, 48), scale=-1.0, bias=cols("kb", k, k + 1), acc=col("CA", k), fn=F.Sign)
        foreign(TAIL)
        cp(cols("RK", 0, 48, k="a"), cols("PE", 256, 304))
        mm(cols("PE", 0, 192), part("M16", 0, 16), part("CD2", 0, 16), True, False)
        forcast(HEAD)
        pull(HEAD)
        meet(HEAD)
        ts(a("LC"), a("CA", k=AZ[:6]), 48.0, A.add, 0.5, A.mult)
        state = lambda nm: a(nm, al, slice(0, 2), al, k=[j + b for j in "01" for b in ALL])
        ts(state("PO"), state("RR"), 32765 if t < 2 else 32764, A.bitwise_and)
        tt(a("MK"), ind(a("RK", k="az"), a("LC")), a("KC"), A.is_equal)
        forcast(TAIL)
        pull(TAIL)
        if t < 2:
            cast(ALL)
        else:
            tt(a("cd"), st("PO", 0, ALL), st("PO", 1, ALL), A.min)
        for w in range(2):
            tt(w96("MV", w, str(w)), ind(a("WP", al, 1 - w, al, k="az"), a("LC")), a("MK"), A.mult)
        for nm, w in (("PD", 0), ("PD", 1), ("PA", 0), ("F2", 1)):
            mm(w96(nm, w), a("BF"), w96("MV", w, str(w)), nm != "PD", nm != "PD" or w == 1)
        meet(TAIL)
        cut(unit("DD", HEAD) if t == 2 else bank(HEAD), HEAD)
        if t == 2:
            dma("g", yw(HEAD), unit("DD", HEAD), accum_op=A.add)
            tt(a("cx"), st("PO", 0, ALL), st("PO", 1, ALL), A.max)
        scan(cols("DB", 1, 384, k="o", step=2), a("DA"), cols("PD", 0, 192), A.min, A.max)
        cp(w96("RU", 0, "0"), w96("PA", 0))
        cp(w96("RU", 1, "1"), w96("F2", 1))
        cp(a("LE0"), cols("DB", 31, 384, k="o", step=32))
        if t < 2:
            addw(HEAD, 0)
        else:
            ts(cols("yco", 0, 48, k="0"), a("cd"), 0.25, A.mult, -float(at(0)), A.add)
            ts(cols("yco", 48, 96, k="1"), a("cx"), 0.25, A.mult, -float(at(1)), A.add)
            dma("y", ext(T.yc[:]), a("yco", k="01"))
        for nm, win in (("gx", XN), ("gn", NX))[t // 2:]:
            for w in range(2):
                act(w96(nm, 1 - w, str(w)), ind(win, cols("LE0", 6 * w, 6 * w + 6)))
        if t == 0:
            sendx(2)
        for e in range(12):
            ts(cols("EQ", 192 * e, 192 * e + 192, k=AZ[e]), a("RU", k="01"), cols("DB", 32 * e + 31, 32 * e + 32, k="o"), A.is_equal)
            for w in range(2):
                mm(cols("PE", 0, 192, step=2), a("BK"), cols("EQ", 192 * e + 96 * w, 192 * e + 96 * w + 96, k=AZ[e]), False, e == 11 and w == 1)
        cut(bank(TAIL), TAIL)
        if t < 2:
            addw(HEAD, 1)
        for w in range(2):
            scan(cols("QQ", 192 * w, 192 * w + 192, k=str(w)), cols("DB", 192 * w, 192 * w + 192, k="eo"), cols("PE", 0, 192), A.max, A.min)
        addw(TAIL, 0)
        cp(a("LE1"), cols("QQ", 31, 384, k="01", step=32))
        addw(TAIL, 1)
        if t < 2:
            put("s", NX, a("LE1"), a("gn", k="01"))
        put("v", XN if t < 2 else NX, a("LE1"), a("gx" if t < 2 else "gn", k="01"))
        if t == 1:
            next_out(0)
            next_out(1)
        if t == 2:
            for s in range(2):
                dma("ys"[s], ext(T.yn[:, W * s:W * s + W]), rows("NX", 0, at(s), at(s) + W, NX[1]))
    for sem, val in total.items():
        need("g", sem, val)
